import numpy as np
import ml_dtypes


def mxq(x, axis, fmt="e4m3"):
    dtype, down = {"e4m3": (ml_dtypes.float8_e4m3fn, 7), "e5m2": (ml_dtypes.float8_e5m2, 14)}[fmt]
    v = np.moveaxis(np.asarray(x, np.float32).astype(ml_dtypes.bfloat16).astype(np.float64), axis, -1)
    blocks = v.reshape(v.shape[:-1] + (-1, 32))
    amax = np.abs(blocks).max(-1, keepdims=True)
    byte = np.maximum(np.where(amax > 0, np.frexp(amax)[1] - 1 + 127, 0) - down, 1)
    scale = np.exp2(byte - 127.0)
    codes = (blocks / scale).astype(np.float32).astype(dtype).astype(np.float64)
    return np.moveaxis((codes * scale).reshape(v.shape), -1, axis)


WIDE = False


def mx_kscale(k):
    if not WIDE:
        return np.ones(k)
    levels = np.array([10, -10, 5, -5, 0])
    if k % 512:
        return np.exp2(np.random.permutation(np.resize(levels, k // 32))).repeat(32)
    a = np.empty((k // 512, 16))
    for p in range(k // 512):
        a[p, :8] = np.random.permutation(np.resize(levels, 8))
        for g in range(8):
            far = levels[np.abs(levels - a[p, g]) >= 10]
            a[p, g + 8] = far[np.random.randint(len(far))]
    return np.exp2(a.ravel()).repeat(32)


def f64(x):
    return np.asarray(x).astype(np.float64)


def striped(idx):
    return np.tile(idx.reshape(-1, 16).T, (8, 1)).astype(np.uint16)


def unstriped(offs):
    return offs[:16].T.reshape(-1).astype(np.int64)


E2M1 = np.array([0.0, 0.5, 1.0, 1.5, 2.0, 3.0, 4.0, 6.0, -0.0, -0.5, -1.0, -1.5, -2.0, -3.0, -4.0, -6.0])


def pack_weight(w, fmt):
    k, n = w.shape
    w = f64(np.asarray(w, np.float32).astype(ml_dtypes.bfloat16)).reshape(k // 32, 32, n)
    amax = np.abs(w).max(1)
    if fmt == "e4m3":
        byte = np.frexp(amax)[1] - 1 + 127 - 7
    else:
        mant, ex = np.frexp(amax / 6.0)
        byte = np.where(mant > 0.5, ex, ex - 1) + 127
    byte = np.clip(np.where(amax > 0, byte, 1), 1, 254)
    scaled = (w * np.exp2(127.0 - byte)[:, None, :]).reshape(k, n).astype(np.float32)
    by_word = np.ascontiguousarray(scaled.reshape(k // 512, 128, 4, n).transpose(0, 1, 3, 2))
    if fmt == "e4m3":
        words = by_word.astype(ml_dtypes.float8_e4m3fn).view(np.uint8)
    else:
        c = by_word.astype(ml_dtypes.float4_e2m1fn).view(np.uint8) & 0xF
        words = (c[..., 0::2] | (c[..., 1::2] << 4)).reshape(k // 512, 128, 2 * n)
    return np.ascontiguousarray(words), np.ascontiguousarray(byte.astype(np.uint8).reshape(k // 512, 16, n))


def unpack_weight(words, scales, fmt):
    g, _, n = scales.shape
    words = np.ascontiguousarray(words).reshape(g, 128, n, -1)
    if fmt == "e4m3":
        vals = words.view(ml_dtypes.float8_e4m3fn).astype(np.float64)
    else:
        nib = np.empty((g, 128, n, 4), np.uint8)
        nib[..., 0::2] = words & 0xF
        nib[..., 1::2] = words >> 4
        vals = E2M1[nib]
    vals = vals * np.repeat(np.exp2(scales.astype(np.float64) - 127.0), 8, axis=1)[..., None]
    return vals.transpose(0, 1, 3, 2).reshape(g * 512, n)


def d_relu2(v):
    return 2.0 * np.maximum(v, 0.0)


K, T, G, C1, E, C2, H = 512, 1024, 2, 512, 4, 256, 512
N = 512


def by_expert(wq, xq, E, C):
    return np.concatenate([wq[e].T @ xq[:, e * C:(e + 1) * C] for e in range(E)], axis=1)


def setup_inputs():
    n = np.random.standard_normal
    v = mx_kscale(N)
    u = mx_kscale(H)
    slots1 = np.random.permutation(T)
    slots2 = np.concatenate([q * C1 + np.random.permutation(C1) for q in range(G)])
    dy = pack_weight(n((N, T)) * v[:, None], "e4m3")
    wet = [pack_weight(m, "e2m1") for m in n((E, N, H)) / np.sqrt(N) / v[None, :, None] * u]
    wgt = [pack_weight(m, "e2m1") for m in n((G, H, K)) / np.sqrt(H) / u[None, :, None]]
    return {
        "dy_words": dy[0],
        "dy_scales": dy[1],
        "wet_words": np.stack([m[0] for m in wet]),
        "wet_scales": np.stack([m[1] for m in wet]),
        "wgt_words": np.stack([m[0] for m in wgt]),
        "wgt_scales": np.stack([m[1] for m in wgt]),
        "a": (n((H, T))).astype(np.float32),
        "gate": (np.tile(np.random.uniform(0.2, 1.0, T), (128, 1))).astype(np.float32),
        "offs": striped(slots1),
        "offs2": striped(slots2),
        "dst": striped(slots1[slots2]),
    }


def reference(dy_words, dy_scales, wet_words, wet_scales, wgt_words, wgt_scales, a, gate, offs, offs2, dst):
    wet = np.stack([unpack_weight(wet_words[e], wet_scales[e], "e2m1") for e in range(E)])
    wgt = np.stack([unpack_weight(wgt_words[e], wgt_scales[e], "e2m1") for e in range(G)])
    gq = unpack_weight(dy_words, dy_scales, "e4m3")[:, unstriped(dst)]
    z = f64(gate[:1]) * by_expert(wet, gq, E, C2)
    da = np.zeros((H, T))
    da[:, unstriped(offs2)] = z
    dx = by_expert(wgt, mxq(da * d_relu2(f64(a)), 0, "e4m3"), G, C1)
    out = np.zeros((K, T))
    out[:, unstriped(offs)] = dx
    return out

@@ -1,0 +1,201 @@
+from contextlib import ExitStack
+
+import concourse.mybir as mybir
+from concourse.masks import make_identity
+
+K, T, G, C1, E, C2, H, N = 512, 1024, 2, 512, 4, 256, 512, 512
+FLOPS = 2 * T * N * H + 2 * T * H * K
+
+F32 = mybir.dt.float32
+BF16 = mybir.dt.bfloat16
+I32 = mybir.dt.int32
+U32 = mybir.dt.uint32
+U16 = mybir.dt.uint16
+U8 = mybir.dt.uint8
+FP8X4 = mybir.dt.float8_e4m3fn_x4
+FP4X4 = mybir.dt.float4_e2m1fn_x4
+COPY = mybir.ActivationFunctionType.Copy
+MAX = mybir.AluOpType.max
+MULT = mybir.AluOpType.mult
+
+P = 128
+PACK = 4
+PER_COL = 16
+BLOCKS = C1 // P
+
+
+def tile_moe_hib_relu2_kernel(tc, dy_words, dy_scales, wet_words, wet_scales, wgt_words, wgt_scales, a, gate, offs, offs2, dst, out):
+    nc = tc.nc
+    with ExitStack() as ctx:
+        lists = ctx.enter_context(tc.tile_pool(name="lists", bufs=1))
+        keep = ctx.enter_context(tc.tile_pool(name="keep", bufs=1))
+        psum = ctx.enter_context(tc.psum_pool(name="psum", bufs=1))
+
+        def entries(tile, first, count):
+            return tile[:, first // PER_COL : (first + count) // PER_COL]
+
+        def load_scale_rows(plane, rows):
+            for quad in range(4):
+                nc.sync.dma_start(
+                    plane[32 * quad : 32 * quad + 4, :, :].bitcast(I32),
+                    rows[:, 4 * quad : 4 * quad + 4, :].rearrange("m b c -> b m c").bitcast(I32),
+                )
+
+        dst_sb = lists.tile([P, T // PER_COL], U16, name="dst_sb")
+        offs2_sb = lists.tile([P, T // PER_COL], U16, name="offs2_sb")
+        offs_sb = lists.tile([P, T // PER_COL], U16, name="offs_sb")
+
+        dy_scale_sb = keep.tile([P, 1, T], U8, name="dy_scale_sb", align_bytes=64)
+        wet_scale_sb = keep.tile([P, E, H], U8, name="wet_scale_sb", align_bytes=64)
+        wgt_scale_sb = keep.tile([P, G, K], U8, name="wgt_scale_sb", align_bytes=64)
+        gate_rows = keep.tile([P, P], F32, name="gate_rows", tag="a0")
+        nc.gpsimd.memset(dy_scale_sb[:].bitcast(I32), 0)
+        nc.gpsimd.memset(gate_rows[:], 0.0)
+        nc.gpsimd.memset(wet_scale_sb[:].bitcast(I32), 0)
+        ident = keep.tile([P, P], F32, name="ident")
+        make_identity(nc, ident[:])
+        nc.gpsimd.memset(wgt_scale_sb[:].bitcast(I32), 0)
+
+        dy_word_sb = keep.tile([P, T], I32, name="dy_word_sb", tag="a1", align_bytes=64)
+        wet_sb = keep.tile([P, E, 2 * H], U8, name="wet_sb", tag="weights", align_bytes=64)
+
+        nc.sync.dma_start(dst_sb[:], dst)
+        load_scale_rows(dy_scale_sb, dy_scales)
+        nc.sync.dma_start(dy_word_sb[:], dy_words[0].rearrange("p t d -> p (t d)").bitcast(I32))
+        nc.sync.dma_start(gate_rows[0 : T // P, :], gate[0].rearrange("(c m) -> c m", m=P))
+        nc.sync.dma_start(wet_sb[:].bitcast(I32), wet_words.rearrange("e s p c -> p (e s) c").bitcast(I32))
+        load_scale_rows(wet_scale_sb, wet_scales.rearrange("e s b c -> (e s) b c"))
+        nc.sync.dma_start(offs2_sb[:], offs2)
+        load_scale_rows(wgt_scale_sb, wgt_scales.rearrange("f s b c -> (f s) b c"))
+        nc.sync.dma_start(offs_sb[:], offs)
+
+        gate_ps = psum.tile([P, P], F32, name="gate_ps", tag="sum", bufs=4)
+        nc.tensor.transpose(gate_ps[:], gate_rows[:], ident[:])
+        gate2 = keep.tile([P, T // P], F32, name="gate2")
+        nc.scalar.activation(gate2[:], gate_ps[:, 0 : T // P], COPY, scale=2.0)
+
+        g_scale = [keep.tile([P, C1], U8, name=f"g_scale{f}", align_bytes=64) for f in range(G)]
+        g_word = [keep.tile([P, C1], U32, name=f"g_word{f}", align_bytes=64) for f in range(G)]
+
+        def gather_scales(f):
+            nc.vector.tensor_copy(g_scale[f][:], dy_scale_sb[:, 0, :].indirect(entries(dst_sb, f * C1, C1)))
+
+        def gather_words(first, count):
+            f, at = divmod(first, C1)
+            nc.vector.tensor_copy(g_word[f][:, at : at + count], dy_word_sb[:].bitcast(U32).indirect(entries(dst_sb, first, count)))
+
+        gather_scales(0)
+        gather_words(0, C2)
+        gather_words(C2, C2)
+        gather_scales(1)
+        gather_words(C1, C1)
+
+        z = [[keep.tile([P, C1], F32, name=f"z{f}_{r}") for r in range(PACK)] for f in range(G)]
+
+        def first_product(e):
+            f, at = divmod(e * C2, C1)
+            z_rows = keep.tile([P, C2 // P, PACK, P], F32, name=f"z_rows{e}", tag="z_rows")
+            for b in range(C2 // P):
+                slots = slice(at + b * P, at + (b + 1) * P)
+                acc = psum.tile([P, H], F32, name=f"acc1_{e}_{b}", tag="sum", bufs=4)
+                nc.tensor.matmul_mx(
+                    acc[:],
+                    lhsT=g_word[f][:, slots].bitcast(FP8X4),
+                    lhsT_scale=g_scale[f][:, slots],
+                    rhs=wet_sb[:, e, :].bitcast(FP4X4),
+                    rhs_scale=wet_scale_sb[:, e, :],
+                    start=True,
+                    stop=True,
+                )
+                col = e * C2 // P + b
+                nc.scalar.activation(z_rows[:, b, :, :], acc[:].rearrange("m (q r) -> m r q", r=PACK), COPY, scale=gate2[:, col : col + 1])
+            for r in range(PACK):
+                turned = psum.tile([P, C2], F32, name=f"turned{e}_{r}", tag=f"turned{r}")
+                for b in range(C2 // P):
+                    nc.tensor.transpose(turned[:, b * P : (b + 1) * P], z_rows[:, b, r, :], ident[:])
+                nc.scalar.copy(z[f][r][:, at : at + C2], turned[:])
+
+        def z_window(f, r, tag):
+            return keep.tile([P, T], F32, name=f"z_back{f}_{r}", tag=tag, align_bytes=64)
+
+        def scatter_z(window, r, first, count):
+            f, at = divmod(first, C1)
+            nc.vector.tensor_copy(window[:].indirect(entries(offs2_sb, first, count)), z[f][r][:, at : at + count])
+
+        def times_slope(f, r, window, planes):
+            nc.vector.scalar_tensor_tensor(planes[:, r, :], a_sb[f][:, r, :], 0.0, window[:, f * C1 : (f + 1) * C1], MAX, MULT)
+
+        def weave(f, planes):
+            woven = keep.tile([P, C1, PACK], BF16, name=f"woven{f}", tag=f"woven{f}", align_bytes=64)
+            nc.scalar.copy(
+                woven[:].rearrange("p (c i) t -> p c t i", i=4),
+                planes[:].rearrange("p t (c i) -> p c t i", i=4),
+            )
+            return woven
+
+        def quantise(f, woven):
+            words = keep.tile([P, C1], U32, name=f"da_words{f}", align_bytes=64)
+            scales = keep.tile([P, C1], U8, name=f"da_scales{f}", align_bytes=64)
+            nc.vector.quantize_mx(words[:].bitcast(FP8X4), scales[:], woven[:].rearrange("p j t -> p (j t)"))
+            return words, scales
+
+        def second_product(f, words, scales):
+            dx = []
+            for kb in range(K // P):
+                acc = psum.tile([P, C1], F32, name=f"acc2_{f}_{kb}", tag="sum", bufs=4)
+                nc.tensor.matmul_mx(
+                    acc[:],
+                    lhsT=wgt_sb[:, f, 2 * kb * P : 2 * (kb + 1) * P].bitcast(FP4X4),
+                    lhsT_scale=wgt_scale_sb[:, f, kb * P : (kb + 1) * P],
+                    rhs=words[:].bitcast(FP8X4),
+                    rhs_scale=scales[:],
+                    start=True,
+                    stop=True,
+                )
+                rows = keep.tile([P, C1], F32, name=f"dx{f}_{kb}")
+                nc.scalar.copy(rows[:], acc[:])
+                dx.append(rows)
+            return dx
+
+        def scatter_dx(f, window, rows):
+            nc.vector.tensor_copy(window[:].indirect(entries(offs_sb, f * C1, C1)), rows[:])
+
+        for e in range(E):
+            first_product(e)
+        a_view = a.rearrange("(q r) j -> q r j", r=PACK)
+        a_sb = [keep.tile([P, PACK, C1], F32, name="a_sb0", tag="a0"), keep.tile([P, PACK, C1], F32, name="a_sb1", tag="a1", align_bytes=64)]
+        for f in range(G):
+            nc.sync.dma_start(a_sb[f][:], a_view[:, :, f * C1 : (f + 1) * C1])
+        wgt_sb = keep.tile([P, G, 2 * K], U8, name="wgt_sb", tag="weights", align_bytes=64)
+        nc.sync.dma_start(wgt_sb[:].bitcast(I32), wgt_words.rearrange("f s p c -> p (f s) c").bitcast(I32))
+        planes = [keep.tile([P, PACK, C1], BF16, name=f"planes{f}") for f in range(G)]
+
+        back0 = [z_window(0, r, f"back0_{r}") for r in range(PACK)]
+        for first in (0, C2):
+            for r in range(PACK):
+                scatter_z(back0[r], r, first, C2)
+        for r in range(PACK):
+            times_slope(0, r, back0[r], planes[0])
+        woven0 = weave(0, planes[0])
+        back1 = [z_window(1, r, f"back1_{r}") for r in range(2)]
+        for r in range(2):
+            scatter_z(back1[r], r, C1, C1)
+        dx0 = second_product(0, *quantise(0, woven0))
+        back1.append(z_window(1, 2, "woven0"))
+        back1.append(z_window(1, 3, "back1_3"))
+        for r in range(2, 4):
+            scatter_z(back1[r], r, C1, C1)
+        for r in range(PACK):
+            times_slope(1, r, back1[r], planes[1])
+        woven1 = weave(1, planes[1])
+        tokens = [keep.tile([P, T], F32, name=f"tokens{kb}") for kb in range(2)]
+        for kb in range(2):
+            scatter_dx(0, tokens[kb], dx0[kb])
+        dx1 = second_product(1, *quantise(1, woven1))
+        tokens.append(keep.tile([P, T], F32, name="tokens2", tag="woven1", align_bytes=64))
+        tokens.append(keep.tile([P, T], F32, name="tokens3"))
+        for kb in range(2, 4):
+            scatter_dx(0, tokens[kb], dx0[kb])
+        for kb in range(K // P):
+            scatter_dx(1, tokens[kb], dx1[kb])
+            nc.sync.dma_start(out[kb * P : (kb + 1) * P, :], tokens[kb][:])

@@ -15,7 +15,7 @@ U8 = mybir.dt.uint8
 FP8X4 = mybir.dt.float8_e4m3fn_x4
 FP4X4 = mybir.dt.float4_e2m1fn_x4
 COPY = mybir.ActivationFunctionType.Copy
-MAX = mybir.AluOpType.max
+RELU = mybir.ActivationFunctionType.Relu
 MULT = mybir.AluOpType.mult
 
 P = 128
@@ -69,7 +69,7 @@ def tile_moe_hib_relu2_kernel(tc, dy_words, dy_scales, wet_words, wet_scales, wg
         load_scale_rows(wgt_scale_sb, wgt_scales.rearrange("f s b c -> (f s) b c"))
         nc.sync.dma_start(offs_sb[:], offs)
 
-        gate_ps = psum.tile([P, P], F32, name="gate_ps", tag="sum", bufs=4)
+        gate_ps = psum.tile([P, P], F32, name="gate_ps", tag="dx", bufs=2)
         nc.tensor.transpose(gate_ps[:], gate_rows[:], ident[:])
         gate2 = keep.tile([P, T // P], F32, name="gate2")
         nc.scalar.activation(gate2[:], gate_ps[:, 0 : T // P], COPY, scale=2.0)
@@ -97,7 +97,7 @@ def tile_moe_hib_relu2_kernel(tc, dy_words, dy_scales, wet_words, wet_scales, wg
             z_rows = keep.tile([P, C2 // P, PACK, P], F32, name=f"z_rows{e}", tag="z_rows")
             for b in range(C2 // P):
                 slots = slice(at + b * P, at + (b + 1) * P)
-                acc = psum.tile([P, H], F32, name=f"acc1_{e}_{b}", tag="sum", bufs=4)
+                acc = psum.tile([P, H], F32, name=f"acc1_{e}_{b}", tag="sum", bufs=2)
                 nc.tensor.matmul_mx(
                     acc[:],
                     lhsT=g_word[f][:, slots].bitcast(FP8X4),
@@ -123,7 +123,7 @@ def tile_moe_hib_relu2_kernel(tc, dy_words, dy_scales, wet_words, wet_scales, wg
             nc.vector.tensor_copy(window[:].indirect(entries(offs2_sb, first, count)), z[f][r][:, at : at + count])
 
         def times_slope(f, r, window, planes):
-            nc.vector.scalar_tensor_tensor(planes[:, r, :], a_sb[f][:, r, :], 0.0, window[:, f * C1 : (f + 1) * C1], MAX, MULT)
+            nc.gpsimd.tensor_tensor(planes[:, r, :], window[:, f * C1 : (f + 1) * C1], slope[f][:, r, :], MULT)
 
         def weave(f, planes):
             woven = keep.tile([P, C1, PACK], BF16, name=f"woven{f}", tag=f"woven{f}", align_bytes=64)
@@ -142,7 +142,7 @@ def tile_moe_hib_relu2_kernel(tc, dy_words, dy_scales, wet_words, wet_scales, wg
         def second_product(f, words, scales):
             dx = []
             for kb in range(K // P):
-                acc = psum.tile([P, C1], F32, name=f"acc2_{f}_{kb}", tag="sum", bufs=4)
+                acc = psum.tile([P, C1], F32, name=f"acc2_{f}_{kb}", tag="dx", bufs=2)
                 nc.tensor.matmul_mx(
                     acc[:],
                     lhsT=wgt_sb[:, f, 2 * kb * P : 2 * (kb + 1) * P].bitcast(FP4X4),
@@ -166,6 +166,10 @@ def tile_moe_hib_relu2_kernel(tc, dy_words, dy_scales, wet_words, wet_scales, wg
         a_sb = [keep.tile([P, PACK, C1], F32, name="a_sb0", tag="a0"), keep.tile([P, PACK, C1], F32, name="a_sb1", tag="a1", align_bytes=64)]
         for f in range(G):
             nc.sync.dma_start(a_sb[f][:], a_view[:, :, f * C1 : (f + 1) * C1])
+        slope = [keep.tile([P, PACK, C1], F32, name=f"slope{f}") for f in range(G)]
+        for f in range(G):
+            for r in range(PACK):
+                nc.scalar.activation(slope[f][:, r, :], a_sb[f][:, r, :], RELU)
         wgt_sb = keep.tile([P, G, 2 * K], U8, name="wgt_sb", tag="weights", align_bytes=64)
         nc.sync.dma_start(wgt_sb[:].bitcast(I32), wgt_words.rearrange("f s p c -> p (f s) c").bitcast(I32))
         planes = [keep.tile([P, PACK, C1], BF16, name=f"planes{f}") for f in range(G)]

@@ -51,21 +51,24 @@ def tile_moe_hib_relu2_kernel(tc, dy_words, dy_scales, wet_words, wet_scales, wg
         gate_rows = keep.tile([P, P], F32, name="gate_rows", tag="a0")
         nc.gpsimd.memset(dy_scale_sb[:].bitcast(I32), 0)
         nc.gpsimd.memset(gate_rows[:], 0.0)
-        nc.gpsimd.memset(wet_scale_sb[:].bitcast(I32), 0)
+        nc.vector.memset(wet_scale_sb[:].bitcast(I32), 0)
         ident = keep.tile([P, P], F32, name="ident")
         make_identity(nc, ident[:])
         nc.gpsimd.memset(wgt_scale_sb[:].bitcast(I32), 0)
 
         dy_word_sb = keep.tile([P, T], I32, name="dy_word_sb", tag="a1", align_bytes=64)
-        wet_sb = keep.tile([P, E, 2 * H], U8, name="wet_sb", tag="weights", align_bytes=64)
+        wet_first = keep.tile([P, 2 * H], U8, name="wet_first", align_bytes=64)
+        wet_rest = keep.tile([P, E - 1, 2 * H], U8, name="wet_rest", tag="weights", align_bytes=64)
+        wet_of = [wet_first[:]] + [wet_rest[:, e, :] for e in range(E - 1)]
 
         nc.sync.dma_start(dst_sb[:], dst)
         load_scale_rows(dy_scale_sb, dy_scales)
         nc.sync.dma_start(dy_word_sb[:], dy_words[0].rearrange("p t d -> p (t d)").bitcast(I32))
         nc.sync.dma_start(gate_rows[0 : T // P, :], gate[0].rearrange("(c m) -> c m", m=P))
-        nc.sync.dma_start(wet_sb[:].bitcast(I32), wet_words.rearrange("e s p c -> p (e s) c").bitcast(I32))
+        nc.sync.dma_start(wet_first[:].bitcast(I32), wet_words[0, 0].bitcast(I32))
         load_scale_rows(wet_scale_sb, wet_scales.rearrange("e s b c -> (e s) b c"))
         nc.sync.dma_start(offs2_sb[:], offs2)
+        nc.sync.dma_start(wet_rest[:].bitcast(I32), wet_words[1:E].rearrange("e s p c -> p (e s) c").bitcast(I32))
         load_scale_rows(wgt_scale_sb, wgt_scales.rearrange("f s b c -> (f s) b c"))
         nc.sync.dma_start(offs_sb[:], offs)
 
@@ -85,35 +88,36 @@ def tile_moe_hib_relu2_kernel(tc, dy_words, dy_scales, wet_words, wet_scales, wg
             nc.vector.tensor_copy(g_word[f][:, at : at + count], dy_word_sb[:].bitcast(U32).indirect(entries(dst_sb, first, count)))
 
         gather_scales(0)
-        gather_words(0, C2)
-        gather_words(C2, C2)
+        gather_words(0, P)
+        gather_words(P, C1 - P)
         gather_scales(1)
         gather_words(C1, C1)
 
         z = [[keep.tile([P, C1], F32, name=f"z{f}_{r}") for r in range(PACK)] for f in range(G)]
 
-        def first_product(e):
-            f, at = divmod(e * C2, C1)
-            z_rows = keep.tile([P, C2 // P, PACK, P], F32, name=f"z_rows{e}", tag="z_rows")
-            for b in range(C2 // P):
+        def first_product(first, count):
+            f, at = divmod(first, C1)
+            turned = [psum.tile([P, count], F32, name=f"turned{first}_{r}", tag=f"turned{r}") for r in range(PACK)]
+            for b in range(count // P):
+                block = first // P + b
+                e = block * P // C2
                 slots = slice(at + b * P, at + (b + 1) * P)
-                acc = psum.tile([P, H], F32, name=f"acc1_{e}_{b}", tag="sum", bufs=2)
+                acc = psum.tile([P, H], F32, name=f"acc1_{block}", tag="sum", bufs=2)
                 nc.tensor.matmul_mx(
                     acc[:],
                     lhsT=g_word[f][:, slots].bitcast(FP8X4),
                     lhsT_scale=g_scale[f][:, slots],
-                    rhs=wet_sb[:, e, :].bitcast(FP4X4),
+                    rhs=wet_of[e].bitcast(FP4X4),
                     rhs_scale=wet_scale_sb[:, e, :],
                     start=True,
                     stop=True,
                 )
-                col = e * C2 // P + b
-                nc.scalar.activation(z_rows[:, b, :, :], acc[:].rearrange("m (q r) -> m r q", r=PACK), COPY, scale=gate2[:, col : col + 1])
+                z_rows = keep.tile([P, PACK, P], F32, name=f"z_rows{block}", tag="z_rows", bufs=2)
+                nc.scalar.activation(z_rows[:], acc[:].rearrange("m (q r) -> m r q", r=PACK), COPY, scale=gate2[:, block : block + 1])
+                for r in range(PACK):
+                    nc.tensor.transpose(turned[r][:, b * P : (b + 1) * P], z_rows[:, r, :], ident[:])
             for r in range(PACK):
-                turned = psum.tile([P, C2], F32, name=f"turned{e}_{r}", tag=f"turned{r}")
-                for b in range(C2 // P):
-                    nc.tensor.transpose(turned[:, b * P : (b + 1) * P], z_rows[:, b, r, :], ident[:])
-                nc.scalar.copy(z[f][r][:, at : at + C2], turned[:])
+                nc.scalar.copy(z[f][r][:, at : at + count], turned[r][:])
 
         def z_window(f, r, tag):
             return keep.tile([P, T], F32, name=f"z_back{f}_{r}", tag=tag, align_bytes=64)
@@ -160,8 +164,9 @@ def tile_moe_hib_relu2_kernel(tc, dy_words, dy_scales, wet_words, wet_scales, wg
         def scatter_dx(f, window, rows):
             nc.vector.tensor_copy(window[:].indirect(entries(offs_sb, f * C1, C1)), rows[:])
 
-        for e in range(E):
-            first_product(e)
+        pieces = [(0, P), (P, C1 - P), (C1, C1)]
+        for first, count in pieces:
+            first_product(first, count)
         a_view = a.rearrange("(q r) j -> q r j", r=PACK)
         a_sb = [keep.tile([P, PACK, C1], F32, name="a_sb0", tag="a0"), keep.tile([P, PACK, C1], F32, name="a_sb1", tag="a1", align_bytes=64)]
         for f in range(G):
@@ -175,31 +180,27 @@ def tile_moe_hib_relu2_kernel(tc, dy_words, dy_scales, wet_words, wet_scales, wg
         planes = [keep.tile([P, PACK, C1], BF16, name=f"planes{f}") for f in range(G)]
 
         back0 = [z_window(0, r, f"back0_{r}") for r in range(PACK)]
-        for first in (0, C2):
+        for first, count in pieces[:2]:
             for r in range(PACK):
-                scatter_z(back0[r], r, first, C2)
+                scatter_z(back0[r], r, first, count)
         for r in range(PACK):
             times_slope(0, r, back0[r], planes[0])
         woven0 = weave(0, planes[0])
-        back1 = [z_window(1, r, f"back1_{r}") for r in range(2)]
-        for r in range(2):
+        back1 = [z_window(1, r, f"back1_{r}") for r in range(3)]
+        for r in range(3):
             scatter_z(back1[r], r, C1, C1)
         dx0 = second_product(0, *quantise(0, woven0))
-        back1.append(z_window(1, 2, "woven0"))
-        back1.append(z_window(1, 3, "back1_3"))
-        for r in range(2, 4):
-            scatter_z(back1[r], r, C1, C1)
+        back1.append(z_window(1, 3, "woven0"))
+        scatter_z(back1[3], 3, C1, C1)
         for r in range(PACK):
             times_slope(1, r, back1[r], planes[1])
         woven1 = weave(1, planes[1])
-        tokens = [keep.tile([P, T], F32, name=f"tokens{kb}") for kb in range(2)]
-        for kb in range(2):
+        tokens = [keep.tile([P, T], F32, name=f"tokens{kb}") for kb in range(3)]
+        for kb in range(3):
             scatter_dx(0, tokens[kb], dx0[kb])
         dx1 = second_product(1, *quantise(1, woven1))
-        tokens.append(keep.tile([P, T], F32, name="tokens2", tag="woven1", align_bytes=64))
-        tokens.append(keep.tile([P, T], F32, name="tokens3"))
-        for kb in range(2, 4):
-            scatter_dx(0, tokens[kb], dx0[kb])
+        tokens.append(keep.tile([P, T], F32, name="tokens3", tag="woven1", align_bytes=64))
+        scatter_dx(0, tokens[3], dx0[3])
         for kb in range(K // P):
             scatter_dx(1, tokens[kb], dx1[kb])
             nc.sync.dma_start(out[kb * P : (kb + 1) * P, :], tokens[kb][:])

@@ -113,7 +113,9 @@ def tile_moe_hib_relu2_kernel(tc, dy_words, dy_scales, wet_words, wet_scales, wg
                     stop=True,
                 )
                 z_rows = keep.tile([P, PACK, P], F32, name=f"z_rows{block}", tag="z_rows", bufs=2)
-                nc.scalar.activation(z_rows[:], acc[:].rearrange("m (q r) -> m r q", r=PACK), COPY, scale=gate2[:, block : block + 1])
+                by_plane = acc[:].rearrange("m (q r) -> m r q", r=PACK)
+                for planes_out in ([slice(0, 1), slice(1, PACK)] if block == 0 else [slice(0, PACK)]):
+                    nc.scalar.activation(z_rows[:, planes_out, :], by_plane[:, planes_out, :], COPY, scale=gate2[:, block : block + 1])
                 for r in range(PACK):
                     nc.tensor.transpose(turned[r][:, b * P : (b + 1) * P], z_rows[:, r, :], ident[:])
             for r in range(PACK):
@@ -203,4 +205,5 @@ def tile_moe_hib_relu2_kernel(tc, dy_words, dy_scales, wet_words, wet_scales, wg
         scatter_dx(0, tokens[3], dx0[3])
         for kb in range(K // P):
             scatter_dx(1, tokens[kb], dx1[kb])
-            nc.sync.dma_start(out[kb * P : (kb + 1) * P, :], tokens[kb][:])
+            for queue, cols in ((nc.sync, slice(0, T // 2)), (nc.scalar, slice(T // 2, T))):
+                queue.dma_start(out[kb * P : (kb + 1) * P, cols], tokens[kb][:, cols])

@@ -57,18 +57,18 @@ def tile_moe_hib_relu2_kernel(tc, dy_words, dy_scales, wet_words, wet_scales, wg
         nc.gpsimd.memset(wgt_scale_sb[:].bitcast(I32), 0)
 
         dy_word_sb = keep.tile([P, T], I32, name="dy_word_sb", tag="a1", align_bytes=64)
-        wet_first = keep.tile([P, 2 * H], U8, name="wet_first", align_bytes=64)
-        wet_rest = keep.tile([P, E - 1, 2 * H], U8, name="wet_rest", tag="weights", align_bytes=64)
-        wet_of = [wet_first[:]] + [wet_rest[:, e, :] for e in range(E - 1)]
+        wet_first = keep.tile([P, 2, 2 * H], U8, name="wet_first", align_bytes=64)
+        wet_rest = keep.tile([P, 2, 2 * H], U8, name="wet_rest", tag="weights", align_bytes=64)
+        wet_of = [wet_first[:, e, :] for e in range(2)] + [wet_rest[:, e, :] for e in range(2)]
 
         nc.sync.dma_start(dst_sb[:], dst)
         load_scale_rows(dy_scale_sb, dy_scales)
         nc.sync.dma_start(dy_word_sb[:], dy_words[0].rearrange("p t d -> p (t d)").bitcast(I32))
         nc.sync.dma_start(gate_rows[0 : T // P, :], gate[0].rearrange("(c m) -> c m", m=P))
-        nc.sync.dma_start(wet_first[:].bitcast(I32), wet_words[0, 0].bitcast(I32))
+        nc.sync.dma_start(wet_first[:].bitcast(I32), wet_words[0:2].rearrange("e s p c -> p (e s) c").bitcast(I32))
         load_scale_rows(wet_scale_sb, wet_scales.rearrange("e s b c -> (e s) b c"))
         nc.sync.dma_start(offs2_sb[:], offs2)
-        nc.sync.dma_start(wet_rest[:].bitcast(I32), wet_words[1:E].rearrange("e s p c -> p (e s) c").bitcast(I32))
+        nc.sync.dma_start(wet_rest[:].bitcast(I32), wet_words[2:E].rearrange("e s p c -> p (e s) c").bitcast(I32))
         load_scale_rows(wgt_scale_sb, wgt_scales.rearrange("f s b c -> (f s) b c"))
         nc.sync.dma_start(offs_sb[:], offs)
 

@@ -14,14 +14,13 @@ U16 = mybir.dt.uint16
 U8 = mybir.dt.uint8
 FP8X4 = mybir.dt.float8_e4m3fn_x4
 FP4X4 = mybir.dt.float4_e2m1fn_x4
-COPY = mybir.ActivationFunctionType.Copy
 RELU = mybir.ActivationFunctionType.Relu
 MULT = mybir.AluOpType.mult
 
 P = 128
-PACK = 4
 PER_COL = 16
-BLOCKS = C1 // P
+ROWS = H // P
+WIDE = 1408
 
 
 def tile_moe_hib_relu2_kernel(tc, dy_words, dy_scales, wet_words, wet_scales, wgt_words, wgt_scales, a, gate, offs, offs2, dst, out):
@@ -29,6 +28,7 @@ def tile_moe_hib_relu2_kernel(tc, dy_words, dy_scales, wet_words, wet_scales, wg
     with ExitStack() as ctx:
         lists = ctx.enter_context(tc.tile_pool(name="lists", bufs=1))
         keep = ctx.enter_context(tc.tile_pool(name="keep", bufs=1))
+        laid = ctx.enter_context(tc.tile_pool(name="laid", bufs=1))
         psum = ctx.enter_context(tc.psum_pool(name="psum", bufs=1))
 
         def entries(tile, first, count):
@@ -45,110 +45,118 @@ def tile_moe_hib_relu2_kernel(tc, dy_words, dy_scales, wet_words, wet_scales, wg
         offs2_sb = lists.tile([P, T // PER_COL], U16, name="offs2_sb")
         offs_sb = lists.tile([P, T // PER_COL], U16, name="offs_sb")
 
-        dy_scale_sb = keep.tile([P, 1, T], U8, name="dy_scale_sb", align_bytes=64)
+        dy_scale_sb = keep.tile([P, WIDE], U8, name="dy_scale_sb", tag="gate1", align_bytes=64)
         wet_scale_sb = keep.tile([P, E, H], U8, name="wet_scale_sb", align_bytes=64)
         wgt_scale_sb = keep.tile([P, G, K], U8, name="wgt_scale_sb", align_bytes=64)
-        gate_rows = keep.tile([P, P], F32, name="gate_rows", tag="a0")
-        nc.gpsimd.memset(dy_scale_sb[:].bitcast(I32), 0)
-        nc.gpsimd.memset(gate_rows[:], 0.0)
         nc.vector.memset(wet_scale_sb[:].bitcast(I32), 0)
+        nc.gpsimd.memset(wgt_scale_sb[:].bitcast(I32), 0)
         ident = keep.tile([P, P], F32, name="ident")
         make_identity(nc, ident[:])
-        nc.gpsimd.memset(wgt_scale_sb[:].bitcast(I32), 0)
+        ident_bf = keep.tile([P, P], BF16, name="ident_bf")
+        make_identity(nc, ident_bf[:])
 
-        dy_word_sb = keep.tile([P, T], I32, name="dy_word_sb", tag="a1", align_bytes=64)
-        wet_first = keep.tile([P, 2, 2 * H], U8, name="wet_first", align_bytes=64)
+        dy_word_sb = keep.tile([P, T], I32, name="dy_word_sb", tag="a0", align_bytes=64)
+        wet_first = keep.tile([P, 2, 2 * H], U8, name="wet_first", tag="a1", align_bytes=64)
         wet_rest = keep.tile([P, 2, 2 * H], U8, name="wet_rest", tag="weights", align_bytes=64)
         wet_of = [wet_first[:, e, :] for e in range(2)] + [wet_rest[:, e, :] for e in range(2)]
+        gate_sb = [keep.tile([P, C1], F32, name="gate_sb0")]
 
         nc.sync.dma_start(dst_sb[:], dst)
-        load_scale_rows(dy_scale_sb, dy_scales)
+        for quad in range(4):
+            rows = dy_scales[0, 4 * quad : 4 * quad + 4, :].bitcast(I32)
+            nc.sync.dma_start(dy_scale_sb[32 * quad : 32 * quad + 32, 0:T].bitcast(I32), rows.unsqueeze(0).to_broadcast([8, 4, T // 4]))
         nc.sync.dma_start(dy_word_sb[:], dy_words[0].rearrange("p t d -> p (t d)").bitcast(I32))
-        nc.sync.dma_start(gate_rows[0 : T // P, :], gate[0].rearrange("(c m) -> c m", m=P))
         nc.sync.dma_start(wet_first[:].bitcast(I32), wet_words[0:2].rearrange("e s p c -> p (e s) c").bitcast(I32))
         load_scale_rows(wet_scale_sb, wet_scales.rearrange("e s b c -> (e s) b c"))
+        nc.sync.dma_start(gate_sb[0][:], gate[:, 0:C1])
         nc.sync.dma_start(offs2_sb[:], offs2)
         nc.sync.dma_start(wet_rest[:].bitcast(I32), wet_words[2:E].rearrange("e s p c -> p (e s) c").bitcast(I32))
         load_scale_rows(wgt_scale_sb, wgt_scales.rearrange("f s b c -> (f s) b c"))
         nc.sync.dma_start(offs_sb[:], offs)
 
-        gate_ps = psum.tile([P, P], F32, name="gate_ps", tag="dx", bufs=2)
-        nc.tensor.transpose(gate_ps[:], gate_rows[:], ident[:])
-        gate2 = keep.tile([P, T // P], F32, name="gate2")
-        nc.scalar.activation(gate2[:], gate_ps[:, 0 : T // P], COPY, scale=2.0)
+        g_scale = keep.tile([P, T], U8, name="g_scale", align_bytes=64)
+        nc.vector.tensor_copy(g_scale[:], dy_scale_sb[:].indirect(dst_sb[:]))
+        g_word = []
+        for first, count in ((0, C2), (C2, C2), (C1, C1)):
+            words = keep.tile([P, count], U32, name=f"g_word{first}", align_bytes=64)
+            nc.vector.tensor_copy(words[:], dy_word_sb[:].bitcast(U32).indirect(entries(dst_sb, first, count)))
+            g_word.extend(words[:, at : at + C2] for at in range(0, count, C2))
 
-        g_scale = [keep.tile([P, C1], U8, name=f"g_scale{f}", align_bytes=64) for f in range(G)]
-        g_word = [keep.tile([P, C1], U32, name=f"g_word{f}", align_bytes=64) for f in range(G)]
+        gate_sb.append(keep.tile([P, C1], F32, name="gate_sb1", tag="gate1", align_bytes=64))
+        nc.sync.dma_start(gate_sb[1][:], gate[:, C1:T])
 
-        def gather_scales(f):
-            nc.vector.tensor_copy(g_scale[f][:], dy_scale_sb[:, 0, :].indirect(entries(dst_sb, f * C1, C1)))
-
-        def gather_words(first, count):
-            f, at = divmod(first, C1)
-            nc.vector.tensor_copy(g_word[f][:, at : at + count], dy_word_sb[:].bitcast(U32).indirect(entries(dst_sb, first, count)))
-
-        gather_scales(0)
-        gather_words(0, P)
-        gather_words(P, C1 - P)
-        gather_scales(1)
-        gather_words(C1, C1)
-
-        z = [[keep.tile([P, C1], F32, name=f"z{f}_{r}") for r in range(PACK)] for f in range(G)]
-
-        def first_product(first, count):
-            f, at = divmod(first, C1)
-            turned = [psum.tile([P, count], F32, name=f"turned{first}_{r}", tag=f"turned{r}") for r in range(PACK)]
-            for b in range(count // P):
-                block = first // P + b
-                e = block * P // C2
-                slots = slice(at + b * P, at + (b + 1) * P)
-                acc = psum.tile([P, H], F32, name=f"acc1_{block}", tag="sum", bufs=2)
-                nc.tensor.matmul_mx(
-                    acc[:],
-                    lhsT=g_word[f][:, slots].bitcast(FP8X4),
-                    lhsT_scale=g_scale[f][:, slots],
-                    rhs=wet_of[e].bitcast(FP4X4),
-                    rhs_scale=wet_scale_sb[:, e, :],
-                    start=True,
-                    stop=True,
-                )
-                z_rows = keep.tile([P, PACK, P], F32, name=f"z_rows{block}", tag="z_rows", bufs=2)
-                by_plane = acc[:].rearrange("m (q r) -> m r q", r=PACK)
-                for planes_out in ([slice(0, 1), slice(1, PACK)] if block == 0 else [slice(0, PACK)]):
-                    nc.scalar.activation(z_rows[:, planes_out, :], by_plane[:, planes_out, :], COPY, scale=gate2[:, block : block + 1])
-                for r in range(PACK):
-                    nc.tensor.transpose(turned[r][:, b * P : (b + 1) * P], z_rows[:, r, :], ident[:])
-            for r in range(PACK):
-                nc.scalar.copy(z[f][r][:, at : at + count], turned[r][:])
-
-        def z_window(f, r, tag):
-            return keep.tile([P, T], F32, name=f"z_back{f}_{r}", tag=tag, align_bytes=64)
-
-        def scatter_z(window, r, first, count):
-            f, at = divmod(first, C1)
-            nc.vector.tensor_copy(window[:].indirect(entries(offs2_sb, first, count)), z[f][r][:, at : at + count])
-
-        def times_slope(f, r, window, planes):
-            nc.gpsimd.tensor_tensor(planes[:, r, :], window[:, f * C1 : (f + 1) * C1], slope[f][:, r, :], MULT)
-
-        def weave(f, planes):
-            woven = keep.tile([P, C1, PACK], BF16, name=f"woven{f}", tag=f"woven{f}", align_bytes=64)
-            nc.scalar.copy(
-                woven[:].rearrange("p (c i) t -> p c t i", i=4),
-                planes[:].rearrange("p t (c i) -> p c t i", i=4),
+        def expert_sums(acc, e, t):
+            nc.tensor.matmul_mx(
+                acc,
+                lhsT=wet_of[e][:, 2 * t * P : 2 * (t + 1) * P].bitcast(FP4X4),
+                lhsT_scale=wet_scale_sb[:, e, t * P : (t + 1) * P],
+                rhs=g_word[e].bitcast(FP8X4),
+                rhs_scale=g_scale[:, e * C2 : (e + 1) * C2],
+                start=True,
+                stop=True,
             )
-            return woven
+
+        def first_product(f, t, experts_per_bank):
+            sums = keep.tile([P, C1], F32, name=f"sums{f}_{t}")
+            z = keep.tile([P, C1], F32, name=f"z{f}_{t}")
+            for first in range(0, 2, experts_per_bank):
+                acc = psum.tile([P, experts_per_bank * C2], F32, name=f"acc1_{f}_{t}_{first}", tag="sum", bufs=4)
+                for u in range(experts_per_bank):
+                    expert_sums(acc[:, u * C2 : (u + 1) * C2], 2 * f + first + u, t)
+                cols = slice(first * C2, (first + experts_per_bank) * C2)
+                nc.scalar.copy(sums[:, cols], acc[:])
+                nc.gpsimd.tensor_tensor(z[:, cols], sums[:, cols], gate_sb[f][:, cols], MULT)
+            return z
+
+        z = [[first_product(f, t, 1 if (f, t) == (0, 0) else 2) for t in range(ROWS)] for f in range(G)]
+
+        a_view = a.rearrange("(t p) j -> p t j", p=P)
+        a_sb = [keep.tile([P, ROWS, C1], F32, name=f"a_sb{f}", tag=f"a{f}", align_bytes=64) for f in range(G)]
+        for f in range(G):
+            nc.sync.dma_start(a_sb[f][:], a_view[:, :, f * C1 : (f + 1) * C1])
+        slope = [keep.tile([P, ROWS, C1], F32, name=f"slope{f}") for f in range(G)]
+        for f in range(G):
+            for t in range(ROWS):
+                nc.scalar.activation(slope[f][:, t, :], a_sb[f][:, t, :], RELU, scale=2.0)
+        wgt_sb = keep.tile([P, G, 2 * K], U8, name="wgt_sb", tag="weights", align_bytes=64)
+        nc.sync.dma_start(wgt_sb[:].bitcast(I32), wgt_words.rearrange("f s p c -> p (f s) c").bitcast(I32))
+
+        def scatter_z(f, t, window):
+            count = C2 if (f, t) == (0, 0) else C1
+            for at in range(0, C1, count):
+                nc.vector.tensor_copy(window[:].indirect(entries(offs2_sb, f * C1 + at, count)), z[f][t][:, at : at + count])
+
+        def turn_banks(f):
+            return [psum.tile([P, 2, H], BF16, name=f"by_slot{f}_{h}", tag=f"by_slot{h}") for h in range(2)]
+
+        def times_slope(f, t, window, da, by_slot):
+            nc.gpsimd.tensor_tensor(da[:], window[:, f * C1 : (f + 1) * C1], slope[f][:, t, :], MULT)
+            for b in range(4):
+                nc.tensor.transpose(by_slot[b // 2][:, b % 2, t * P : (t + 1) * P], da[:, b * P : (b + 1) * P], ident_bf[:])
+
+        def weave(f, by_slot, woven):
+            woven_words = woven[:].rearrange("p j r -> p (j r)").bitcast(F32)
+            for h in range(2):
+                pairs = keep.tile([P, 2, 2, P], F32, name=f"pairs{f}_{h}")
+                nc.scalar.copy(pairs[:], by_slot[h][:].bitcast(F32).rearrange("j b (q u) -> j b u q", u=2))
+                by_word = psum.tile([P, 2, 2, P], F32, name=f"by_word{f}_{h}", tag=f"by_word{h}")
+                for b in range(2):
+                    for u in range(2):
+                        nc.tensor.transpose(by_word[:, b, u, :], pairs[:, b, u, :], ident[:])
+                nc.scalar.copy(
+                    woven_words[:, h * C1 : (h + 1) * C1].rearrange("q (b j u) -> q b j u", b=2, u=2),
+                    by_word[:].rearrange("q b u j -> q b j u"),
+                )
 
         def quantise(f, woven):
             words = keep.tile([P, C1], U32, name=f"da_words{f}", align_bytes=64)
             scales = keep.tile([P, C1], U8, name=f"da_scales{f}", align_bytes=64)
-            nc.vector.quantize_mx(words[:].bitcast(FP8X4), scales[:], woven[:].rearrange("p j t -> p (j t)"))
+            nc.vector.quantize_mx(words[:].bitcast(FP8X4), scales[:], woven[:].rearrange("p j r -> p (j r)"))
             return words, scales
 
-        def second_product(f, words, scales):
-            dx = []
+        def second_product(f, words, scales, rows_of):
             for kb in range(K // P):
-                acc = psum.tile([P, C1], F32, name=f"acc2_{f}_{kb}", tag="dx", bufs=2)
+                acc = psum.tile([P, C1], F32, name=f"acc2_{f}_{kb}", tag="sum", bufs=4)
                 nc.tensor.matmul_mx(
                     acc[:],
                     lhsT=wgt_sb[:, f, 2 * kb * P : 2 * (kb + 1) * P].bitcast(FP4X4),
@@ -158,52 +166,52 @@ def tile_moe_hib_relu2_kernel(tc, dy_words, dy_scales, wet_words, wet_scales, wg
                     start=True,
                     stop=True,
                 )
-                rows = keep.tile([P, C1], F32, name=f"dx{f}_{kb}")
-                nc.scalar.copy(rows[:], acc[:])
-                dx.append(rows)
-            return dx
+                nc.scalar.copy(rows_of[kb][:, f * C1 : (f + 1) * C1], acc[:])
 
-        def scatter_dx(f, window, rows):
-            nc.vector.tensor_copy(window[:].indirect(entries(offs_sb, f * C1, C1)), rows[:])
+        def scatter_dx(kb, window, first, count):
+            nc.vector.tensor_copy(window[:].indirect(entries(offs_sb, first, count)), dx[kb][:, first : first + count])
 
-        pieces = [(0, P), (P, C1 - P), (C1, C1)]
-        for first, count in pieces:
-            first_product(first, count)
-        a_view = a.rearrange("(q r) j -> q r j", r=PACK)
-        a_sb = [keep.tile([P, PACK, C1], F32, name="a_sb0", tag="a0"), keep.tile([P, PACK, C1], F32, name="a_sb1", tag="a1", align_bytes=64)]
-        for f in range(G):
-            nc.sync.dma_start(a_sb[f][:], a_view[:, :, f * C1 : (f + 1) * C1])
-        slope = [keep.tile([P, PACK, C1], F32, name=f"slope{f}") for f in range(G)]
-        for f in range(G):
-            for r in range(PACK):
-                nc.scalar.activation(slope[f][:, r, :], a_sb[f][:, r, :], RELU)
-        wgt_sb = keep.tile([P, G, 2 * K], U8, name="wgt_sb", tag="weights", align_bytes=64)
-        nc.sync.dma_start(wgt_sb[:].bitcast(I32), wgt_words.rearrange("f s p c -> p (f s) c").bitcast(I32))
-        planes = [keep.tile([P, PACK, C1], BF16, name=f"planes{f}") for f in range(G)]
-
-        back0 = [z_window(0, r, f"back0_{r}") for r in range(PACK)]
-        for first, count in pieces[:2]:
-            for r in range(PACK):
-                scatter_z(back0[r], r, first, count)
-        for r in range(PACK):
-            times_slope(0, r, back0[r], planes[0])
-        woven0 = weave(0, planes[0])
-        back1 = [z_window(1, r, f"back1_{r}") for r in range(3)]
-        for r in range(3):
-            scatter_z(back1[r], r, C1, C1)
-        dx0 = second_product(0, *quantise(0, woven0))
-        back1.append(z_window(1, 3, "woven0"))
-        scatter_z(back1[3], 3, C1, C1)
-        for r in range(PACK):
-            times_slope(1, r, back1[r], planes[1])
-        woven1 = weave(1, planes[1])
-        tokens = [keep.tile([P, T], F32, name=f"tokens{kb}") for kb in range(3)]
-        for kb in range(3):
-            scatter_dx(0, tokens[kb], dx0[kb])
-        dx1 = second_product(1, *quantise(1, woven1))
-        tokens.append(keep.tile([P, T], F32, name="tokens3", tag="woven1", align_bytes=64))
-        scatter_dx(0, tokens[3], dx0[3])
-        for kb in range(K // P):
-            scatter_dx(1, tokens[kb], dx1[kb])
+        def store(kb, window):
             for queue, cols in ((nc.sync, slice(0, T // 2)), (nc.scalar, slice(T // 2, T))):
-                queue.dma_start(out[kb * P : (kb + 1) * P, cols], tokens[kb][:, cols])
+                queue.dma_start(out[kb * P : (kb + 1) * P, cols], window[:, cols])
+
+        dx = [keep.tile([P, T], F32, name=f"dx{kb}") for kb in range(K // P)]
+
+        by_slot0 = turn_banks(0)
+        for t in range(ROWS):
+            window = keep.tile([P, T], F32, name=f"back0_{t}")
+            scatter_z(0, t, window)
+            times_slope(0, t, window, keep.tile([P, C1], BF16, name=f"da0_{t}"), by_slot0)
+        woven0 = laid.tile([P, C1, 4], BF16, name="woven0", offset=3072, align_bytes=64)
+        weave(0, by_slot0, woven0)
+
+        back1 = [keep.tile([P, T], F32, name=f"back1_{t}") for t in range(2)]
+        for t in range(2):
+            scatter_z(1, t, back1[t])
+        second_product(0, *quantise(0, woven0), dx)
+        back1.append(laid.tile([P, T], F32, name="back1_2", offset=0, align_bytes=64))
+        back1.append(laid.tile([P, T], F32, name="back1_3", offset=5120, align_bytes=64))
+        for t in range(2, ROWS):
+            scatter_z(1, t, back1[t])
+        by_slot1 = turn_banks(1)
+        for t in range(ROWS):
+            if t == 1:
+                da = laid.tile([P, C1], BF16, name="da1_1", offset=4096, align_bytes=64)
+            else:
+                da = keep.tile([P, C1], BF16, name=f"da1_{t}")
+            times_slope(1, t, back1[t], da, by_slot1)
+        woven1 = keep.tile([P, C1, 4], BF16, name="woven1", tag="woven1", align_bytes=64)
+        weave(1, by_slot1, woven1)
+
+        tokens = [keep.tile([P, T], F32, name=f"tokens{kb}") for kb in range(2)]
+        for kb in range(2):
+            scatter_dx(kb, tokens[kb], 0, C1)
+        second_product(1, *quantise(1, woven1), dx)
+        tokens.append(keep.tile([P, T], F32, name="tokens2", tag="woven1", align_bytes=64))
+        scatter_dx(2, tokens[2], 0, C1)
+        for kb in range(3):
+            scatter_dx(kb, tokens[kb], C1, C1)
+            store(kb, tokens[kb])
+        tokens.append(keep.tile([P, WIDE], F32, name="tokens3"))
+        scatter_dx(3, tokens[3], 0, T)
+        store(3, tokens[3])

@@ -45,10 +45,12 @@ def tile_moe_hib_relu2_kernel(tc, dy_words, dy_scales, wet_words, wet_scales, wg
         offs2_sb = lists.tile([P, T // PER_COL], U16, name="offs2_sb")
         offs_sb = lists.tile([P, T // PER_COL], U16, name="offs_sb")
 
-        dy_scale_sb = keep.tile([P, WIDE], U8, name="dy_scale_sb", tag="gate1", align_bytes=64)
-        wet_scale_sb = keep.tile([P, E, H], U8, name="wet_scale_sb", align_bytes=64)
+        dy_scale_sb = keep.tile([P, T], U8, name="dy_scale_sb", tag="gate1", align_bytes=64)
+        scale_first = keep.tile([P, E, P], U8, name="scale_first", align_bytes=64)
+        scale_rest = keep.tile([P, E, H - P], U8, name="scale_rest", align_bytes=64)
         wgt_scale_sb = keep.tile([P, G, K], U8, name="wgt_scale_sb", align_bytes=64)
-        nc.vector.memset(wet_scale_sb[:].bitcast(I32), 0)
+        nc.gpsimd.memset(scale_first[:].bitcast(I32), 0)
+        nc.vector.memset(scale_rest[:].bitcast(I32), 0)
         nc.gpsimd.memset(wgt_scale_sb[:].bitcast(I32), 0)
         ident = keep.tile([P, P], F32, name="ident")
         make_identity(nc, ident[:])
@@ -56,42 +58,58 @@ def tile_moe_hib_relu2_kernel(tc, dy_words, dy_scales, wet_words, wet_scales, wg
         make_identity(nc, ident_bf[:])
 
         dy_word_sb = keep.tile([P, T], I32, name="dy_word_sb", tag="a0", align_bytes=64)
-        wet_first = keep.tile([P, 2, 2 * H], U8, name="wet_first", tag="a1", align_bytes=64)
+        wet_first = keep.tile([P, 2, 2 * P], U8, name="wet_first", tag="wet_first", align_bytes=64)
+        wet_next = keep.tile([P, 2, 2 * (H - P)], U8, name="wet_next", tag="a1", align_bytes=64)
         wet_rest = keep.tile([P, 2, 2 * H], U8, name="wet_rest", tag="weights", align_bytes=64)
-        wet_of = [wet_first[:, e, :] for e in range(2)] + [wet_rest[:, e, :] for e in range(2)]
         gate_sb = [keep.tile([P, C1], F32, name="gate_sb0")]
+        wet_view = wet_words.rearrange("e s p c -> p (e s) c")
+        wet_scale_view = wet_scales.rearrange("e s b c -> (e s) b c")
+
+        def wet_block(e, t):
+            if e >= 2:
+                words = wet_rest[:, e - 2, 2 * t * P : 2 * (t + 1) * P]
+            elif t == 0:
+                words = wet_first[:, e, :]
+            else:
+                words = wet_next[:, e, 2 * (t - 1) * P : 2 * t * P]
+            return words, scale_first[:, e, :] if t == 0 else scale_rest[:, e, (t - 1) * P : t * P]
 
         nc.sync.dma_start(dst_sb[:], dst)
         for quad in range(4):
             rows = dy_scales[0, 4 * quad : 4 * quad + 4, :].bitcast(I32)
             nc.sync.dma_start(dy_scale_sb[32 * quad : 32 * quad + 32, 0:T].bitcast(I32), rows.unsqueeze(0).to_broadcast([8, 4, T // 4]))
         nc.sync.dma_start(dy_word_sb[:], dy_words[0].rearrange("p t d -> p (t d)").bitcast(I32))
-        nc.sync.dma_start(wet_first[:].bitcast(I32), wet_words[0:2].rearrange("e s p c -> p (e s) c").bitcast(I32))
-        load_scale_rows(wet_scale_sb, wet_scales.rearrange("e s b c -> (e s) b c"))
-        nc.sync.dma_start(gate_sb[0][:], gate[:, 0:C1])
+        nc.sync.dma_start(wet_first[:].bitcast(I32), wet_view[:, 0:2, 0 : 2 * P].bitcast(I32))
+        load_scale_rows(scale_first, wet_scale_view[:, :, 0:P])
+        nc.sync.dma_start(gate_sb[0][:, 0:C2], gate[:, 0:C2])
         nc.sync.dma_start(offs2_sb[:], offs2)
-        nc.sync.dma_start(wet_rest[:].bitcast(I32), wet_words[2:E].rearrange("e s p c -> p (e s) c").bitcast(I32))
+        nc.sync.dma_start(gate_sb[0][:, C2:C1], gate[:, C2:C1])
+        nc.sync.dma_start(wet_next[:].bitcast(I32), wet_view[:, 0:2, 2 * P : 2 * H].bitcast(I32))
+        load_scale_rows(scale_rest, wet_scale_view[:, :, P:H])
+        nc.sync.dma_start(wet_rest[:].bitcast(I32), wet_view[:, 2:E, :].bitcast(I32))
         load_scale_rows(wgt_scale_sb, wgt_scales.rearrange("f s b c -> (f s) b c"))
         nc.sync.dma_start(offs_sb[:], offs)
 
-        g_scale = keep.tile([P, T], U8, name="g_scale", align_bytes=64)
-        nc.vector.tensor_copy(g_scale[:], dy_scale_sb[:].indirect(dst_sb[:]))
+        def gather_scales(f, tag):
+            scales = keep.tile([P, C1], U8, name=f"g_scale{f}", tag=tag, align_bytes=64)
+            nc.vector.tensor_copy(scales[:], dy_scale_sb[:].indirect(entries(dst_sb, f * C1, C1)))
+            return [scales[:, u * C2 : (u + 1) * C2] for u in range(2)]
+
+        g_scale = gather_scales(0, "g_scale0")
         g_word = []
         for first, count in ((0, C2), (C2, C2), (C1, C1)):
             words = keep.tile([P, count], U32, name=f"g_word{first}", align_bytes=64)
             nc.vector.tensor_copy(words[:], dy_word_sb[:].bitcast(U32).indirect(entries(dst_sb, first, count)))
             g_word.extend(words[:, at : at + C2] for at in range(0, count, C2))
 
-        gate_sb.append(keep.tile([P, C1], F32, name="gate_sb1", tag="gate1", align_bytes=64))
-        nc.sync.dma_start(gate_sb[1][:], gate[:, C1:T])
-
         def expert_sums(acc, e, t):
+            words, scales = wet_block(e, t)
             nc.tensor.matmul_mx(
                 acc,
-                lhsT=wet_of[e][:, 2 * t * P : 2 * (t + 1) * P].bitcast(FP4X4),
-                lhsT_scale=wet_scale_sb[:, e, t * P : (t + 1) * P],
+                lhsT=words.bitcast(FP4X4),
+                lhsT_scale=scales,
                 rhs=g_word[e].bitcast(FP8X4),
-                rhs_scale=g_scale[:, e * C2 : (e + 1) * C2],
+                rhs_scale=g_scale[e],
                 start=True,
                 stop=True,
             )
@@ -108,7 +126,12 @@ def tile_moe_hib_relu2_kernel(tc, dy_words, dy_scales, wet_words, wet_scales, wg
                 nc.gpsimd.tensor_tensor(z[:, cols], sums[:, cols], gate_sb[f][:, cols], MULT)
             return z
 
-        z = [[first_product(f, t, 1 if (f, t) == (0, 0) else 2) for t in range(ROWS)] for f in range(G)]
+        z = [[first_product(0, 0, 1)]]
+        g_scale.extend(gather_scales(1, "wet_first"))
+        gate_sb.append(keep.tile([P, C1], F32, name="gate_sb1", tag="gate1", align_bytes=64))
+        nc.sync.dma_start(gate_sb[1][:], gate[:, C1:T])
+        z[0].extend(first_product(0, t, 2) for t in range(1, ROWS))
+        z.append([first_product(1, t, 2) for t in range(ROWS)])
 
         a_view = a.rearrange("(t p) j -> p t j", p=P)
         a_sb = [keep.tile([P, ROWS, C1], F32, name=f"a_sb{f}", tag=f"a{f}", align_bytes=64) for f in range(G)]

@@ -46,10 +46,10 @@ def tile_moe_hib_relu2_kernel(tc, dy_words, dy_scales, wet_words, wet_scales, wg
         offs_sb = lists.tile([P, T // PER_COL], U16, name="offs_sb")
 
         dy_scale_sb = keep.tile([P, T], U8, name="dy_scale_sb", tag="gate1", align_bytes=64)
-        scale_first = keep.tile([P, E, P], U8, name="scale_first", align_bytes=64)
-        scale_rest = keep.tile([P, E, H - P], U8, name="scale_rest", align_bytes=64)
+        scale_first = keep.tile([P, E, H // 2], U8, name="scale_first", align_bytes=64)
+        scale_rest = keep.tile([P, E, H // 2], U8, name="scale_rest", align_bytes=64)
         wgt_scale_sb = keep.tile([P, G, K], U8, name="wgt_scale_sb", align_bytes=64)
-        nc.gpsimd.memset(scale_first[:].bitcast(I32), 0)
+        nc.vector.memset(scale_first[:].bitcast(I32), 0)
         nc.vector.memset(scale_rest[:].bitcast(I32), 0)
         nc.gpsimd.memset(wgt_scale_sb[:].bitcast(I32), 0)
         ident = keep.tile([P, P], F32, name="ident")
@@ -72,20 +72,20 @@ def tile_moe_hib_relu2_kernel(tc, dy_words, dy_scales, wet_words, wet_scales, wg
                 words = wet_first[:, e, :]
             else:
                 words = wet_next[:, e, 2 * (t - 1) * P : 2 * t * P]
-            return words, scale_first[:, e, :] if t == 0 else scale_rest[:, e, (t - 1) * P : t * P]
+            return words, (scale_first, scale_rest)[t // 2][:, e, t % 2 * P : (t % 2 + 1) * P]
 
         nc.sync.dma_start(dst_sb[:], dst)
         for quad in range(4):
             rows = dy_scales[0, 4 * quad : 4 * quad + 4, :].bitcast(I32)
-            nc.sync.dma_start(dy_scale_sb[32 * quad : 32 * quad + 32, 0:T].bitcast(I32), rows.unsqueeze(0).to_broadcast([8, 4, T // 4]))
+            (nc.sync if quad < 2 else nc.scalar).dma_start(dy_scale_sb[32 * quad : 32 * quad + 32, 0:T].bitcast(I32), rows.unsqueeze(0).to_broadcast([8, 4, T // 4]))
         nc.sync.dma_start(dy_word_sb[:], dy_words[0].rearrange("p t d -> p (t d)").bitcast(I32))
         nc.sync.dma_start(wet_first[:].bitcast(I32), wet_view[:, 0:2, 0 : 2 * P].bitcast(I32))
-        load_scale_rows(scale_first, wet_scale_view[:, :, 0:P])
+        load_scale_rows(scale_first, wet_scale_view[:, :, 0 : H // 2])
         nc.sync.dma_start(gate_sb[0][:, 0:C2], gate[:, 0:C2])
         nc.sync.dma_start(offs2_sb[:], offs2)
         nc.sync.dma_start(gate_sb[0][:, C2:C1], gate[:, C2:C1])
         nc.sync.dma_start(wet_next[:].bitcast(I32), wet_view[:, 0:2, 2 * P : 2 * H].bitcast(I32))
-        load_scale_rows(scale_rest, wet_scale_view[:, :, P:H])
+        load_scale_rows(scale_rest, wet_scale_view[:, :, H // 2 : H])
         nc.sync.dma_start(wet_rest[:].bitcast(I32), wet_view[:, 2:E, :].bitcast(I32))
         load_scale_rows(wgt_scale_sb, wgt_scales.rearrange("f s b c -> (f s) b c"))
         nc.sync.dma_start(offs_sb[:], offs)
@@ -116,22 +116,23 @@ def tile_moe_hib_relu2_kernel(tc, dy_words, dy_scales, wet_words, wet_scales, wg
 
         def first_product(f, t, experts_per_bank):
             sums = keep.tile([P, C1], F32, name=f"sums{f}_{t}")
-            z = keep.tile([P, C1], F32, name=f"z{f}_{t}")
             for first in range(0, 2, experts_per_bank):
                 acc = psum.tile([P, experts_per_bank * C2], F32, name=f"acc1_{f}_{t}_{first}", tag="sum", bufs=4)
                 for u in range(experts_per_bank):
                     expert_sums(acc[:, u * C2 : (u + 1) * C2], 2 * f + first + u, t)
                 cols = slice(first * C2, (first + experts_per_bank) * C2)
                 nc.scalar.copy(sums[:, cols], acc[:])
-                nc.gpsimd.tensor_tensor(z[:, cols], sums[:, cols], gate_sb[f][:, cols], MULT)
-            return z
+                nc.gpsimd.tensor_tensor(z[t][:, f, cols], sums[:, cols], gate_sb[f][:, cols], MULT)
 
-        z = [[first_product(0, 0, 1)]]
+        z = [keep.tile([P, G, C1], F32, name=f"z{t}") for t in range(ROWS)]
+        first_product(0, 0, 1)
         g_scale.extend(gather_scales(1, "wet_first"))
         gate_sb.append(keep.tile([P, C1], F32, name="gate_sb1", tag="gate1", align_bytes=64))
         nc.sync.dma_start(gate_sb[1][:], gate[:, C1:T])
-        z[0].extend(first_product(0, t, 2) for t in range(1, ROWS))
-        z.append([first_product(1, t, 2) for t in range(ROWS)])
+        for t in range(1, ROWS):
+            first_product(0, t, 2)
+        for t in (3, 0, 1, 2):
+            first_product(1, t, 2)
 
         a_view = a.rearrange("(t p) j -> p t j", p=P)
         a_sb = [keep.tile([P, ROWS, C1], F32, name=f"a_sb{f}", tag=f"a{f}", align_bytes=64) for f in range(G)]
@@ -144,10 +145,9 @@ def tile_moe_hib_relu2_kernel(tc, dy_words, dy_scales, wet_words, wet_scales, wg
         wgt_sb = keep.tile([P, G, 2 * K], U8, name="wgt_sb", tag="weights", align_bytes=64)
         nc.sync.dma_start(wgt_sb[:].bitcast(I32), wgt_words.rearrange("f s p c -> p (f s) c").bitcast(I32))
 
-        def scatter_z(f, t, window):
-            count = C2 if (f, t) == (0, 0) else C1
-            for at in range(0, C1, count):
-                nc.vector.tensor_copy(window[:].indirect(entries(offs2_sb, f * C1 + at, count)), z[f][t][:, at : at + count])
+        def scatter_z(t, window, first, count):
+            slots = z[t][:].rearrange("p f j -> p (f j)")
+            nc.vector.tensor_copy(window[:].indirect(entries(offs2_sb, first, count)), slots[:, first : first + count])
 
         def turn_banks(f):
             return [psum.tile([P, 2, H], BF16, name=f"by_slot{f}_{h}", tag=f"by_slot{h}") for h in range(2)]
@@ -201,23 +201,25 @@ def tile_moe_hib_relu2_kernel(tc, dy_words, dy_scales, wet_words, wet_scales, wg
         dx = [keep.tile([P, T], F32, name=f"dx{kb}") for kb in range(K // P)]
 
         by_slot0 = turn_banks(0)
-        for t in range(ROWS):
-            window = keep.tile([P, T], F32, name=f"back0_{t}")
-            scatter_z(0, t, window)
+        back0 = [keep.tile([P, T], F32, name=f"back0_{t}") for t in range(3)]
+        both = keep.tile([P, WIDE], F32, name="back_both")
+        for t in range(3):
+            scatter_z(t, back0[t], 0, C1)
+        scatter_z(3, both, 0, T)
+        for t, window in enumerate(back0 + [both]):
             times_slope(0, t, window, keep.tile([P, C1], BF16, name=f"da0_{t}"), by_slot0)
-        woven0 = laid.tile([P, C1, 4], BF16, name="woven0", offset=3072, align_bytes=64)
+        woven0 = laid.tile([P, C1, 4], BF16, name="woven0", offset=2048, align_bytes=64)
         weave(0, by_slot0, woven0)
 
         back1 = [keep.tile([P, T], F32, name=f"back1_{t}") for t in range(2)]
         for t in range(2):
-            scatter_z(1, t, back1[t])
+            scatter_z(t, back1[t], C1, C1)
         second_product(0, *quantise(0, woven0), dx)
         back1.append(laid.tile([P, T], F32, name="back1_2", offset=0, align_bytes=64))
-        back1.append(laid.tile([P, T], F32, name="back1_3", offset=5120, align_bytes=64))
-        for t in range(2, ROWS):
-            scatter_z(1, t, back1[t])
+        scatter_z(2, back1[2], C1, C1)
+        back1.append(both)
         by_slot1 = turn_banks(1)
-        for t in range(ROWS):
+        for t in (3, 0, 1, 2):
             if t == 1:
                 da = laid.tile([P, C1], BF16, name="da1_1", offset=4096, align_bytes=64)
             else:

@@ -122,9 +122,14 @@ def tile_moe_hib_relu2_kernel(tc, dy_words, dy_scales, wet_words, wet_scales, wg
                     expert_sums(acc[:, u * C2 : (u + 1) * C2], 2 * f + first + u, t)
                 cols = slice(first * C2, (first + experts_per_bank) * C2)
                 nc.scalar.copy(sums[:, cols], acc[:])
-                nc.gpsimd.tensor_tensor(z[t][:, f, cols], sums[:, cols], gate_sb[f][:, cols], MULT)
+                if (f, t) in z:
+                    nc.gpsimd.tensor_tensor(z[f, t][:, cols], sums[:, cols], gate_sb[f][:, cols], MULT)
+            return sums
 
-        z = [keep.tile([P, G, C1], F32, name=f"z{t}") for t in range(ROWS)]
+        z_both = keep.tile([P, T], F32, name="z_both")
+        z = {(f, 3): z_both[:, f * C1 : (f + 1) * C1] for f in range(G)}
+        for f, t in ((0, 0), (0, 1), (0, 2), (1, 0), (1, 1), (1, 2)):
+            z[f, t] = keep.tile([P, C1], F32, name=f"z{f}_{t}")[:]
         first_product(0, 0, 1)
         g_scale.extend(gather_scales(1, "wet_first"))
         gate_sb.append(keep.tile([P, C1], F32, name="gate_sb1", tag="gate1", align_bytes=64))
@@ -145,9 +150,8 @@ def tile_moe_hib_relu2_kernel(tc, dy_words, dy_scales, wet_words, wet_scales, wg
         wgt_sb = keep.tile([P, G, 2 * K], U8, name="wgt_sb", tag="weights", align_bytes=64)
         nc.sync.dma_start(wgt_sb[:].bitcast(I32), wgt_words.rearrange("f s p c -> p (f s) c").bitcast(I32))
 
-        def scatter_z(t, window, first, count):
-            slots = z[t][:].rearrange("p f j -> p (f j)")
-            nc.vector.tensor_copy(window[:].indirect(entries(offs2_sb, first, count)), slots[:, first : first + count])
+        def scatter_z(window, first, values):
+            nc.vector.tensor_copy(window[:].indirect(entries(offs2_sb, first, values.shape[1])), values)
 
         def turn_banks(f):
             return [psum.tile([P, 2, H], BF16, name=f"by_slot{f}_{h}", tag=f"by_slot{h}") for h in range(2)]
@@ -160,7 +164,7 @@ def tile_moe_hib_relu2_kernel(tc, dy_words, dy_scales, wet_words, wet_scales, wg
         def weave(f, by_slot, woven):
             woven_words = woven[:].rearrange("p j r -> p (j r)").bitcast(F32)
             for h in range(2):
-                pairs = keep.tile([P, 2, 2, P], F32, name=f"pairs{f}_{h}")
+                pairs = keep.tile([P, 2, 2, P], F32, name=f"pairs{f}_{h}", tag=f"pairs{f}_{h}")
                 nc.scalar.copy(pairs[:], by_slot[h][:].bitcast(F32).rearrange("j b (q u) -> j b u q", u=2))
                 by_word = psum.tile([P, 2, 2, P], F32, name=f"by_word{f}_{h}", tag=f"by_word{h}")
                 for b in range(2):
@@ -177,7 +181,8 @@ def tile_moe_hib_relu2_kernel(tc, dy_words, dy_scales, wet_words, wet_scales, wg
             nc.vector.quantize_mx(words[:].bitcast(FP8X4), scales[:], woven[:].rearrange("p j r -> p (j r)"))
             return words, scales
 
-        def second_product(f, words, scales, rows_of):
+        def second_product(f, words, scales):
+            accs = []
             for kb in range(K // P):
                 acc = psum.tile([P, C1], F32, name=f"acc2_{f}_{kb}", tag="sum", bufs=4)
                 nc.tensor.matmul_mx(
@@ -189,23 +194,29 @@ def tile_moe_hib_relu2_kernel(tc, dy_words, dy_scales, wet_words, wet_scales, wg
                     start=True,
                     stop=True,
                 )
-                nc.scalar.copy(rows_of[kb][:, f * C1 : (f + 1) * C1], acc[:])
+                if (f, kb) in dx:
+                    nc.scalar.copy(dx[f, kb], acc[:])
+                accs.append(acc)
+            return accs
 
-        def scatter_dx(kb, window, first, count):
-            nc.vector.tensor_copy(window[:].indirect(entries(offs_sb, first, count)), dx[kb][:, first : first + count])
+        def scatter_dx(window, first, values):
+            nc.vector.tensor_copy(window[:].indirect(entries(offs_sb, first, values.shape[1])), values)
 
         def store(kb, window):
             for queue, cols in ((nc.sync, slice(0, T // 2)), (nc.scalar, slice(T // 2, T))):
                 queue.dma_start(out[kb * P : (kb + 1) * P, cols], window[:, cols])
 
-        dx = [keep.tile([P, T], F32, name=f"dx{kb}") for kb in range(K // P)]
+        dx_both = keep.tile([P, T], F32, name="dx_both")
+        dx = {(f, 3): dx_both[:, f * C1 : (f + 1) * C1] for f in range(G)}
+        for f, kb in ((0, 0), (0, 1), (1, 0), (1, 1), (1, 2)):
+            dx[f, kb] = keep.tile([P, C1], F32, name=f"dx{f}_{kb}")[:]
 
         by_slot0 = turn_banks(0)
         back0 = [keep.tile([P, T], F32, name=f"back0_{t}") for t in range(3)]
         both = keep.tile([P, WIDE], F32, name="back_both")
         for t in range(3):
-            scatter_z(t, back0[t], 0, C1)
-        scatter_z(3, both, 0, T)
+            scatter_z(back0[t], 0, z[0, t])
+        scatter_z(both, 0, z_both[:])
         for t, window in enumerate(back0 + [both]):
             times_slope(0, t, window, keep.tile([P, C1], BF16, name=f"da0_{t}"), by_slot0)
         woven0 = laid.tile([P, C1, 4], BF16, name="woven0", offset=2048, align_bytes=64)
@@ -213,10 +224,10 @@ def tile_moe_hib_relu2_kernel(tc, dy_words, dy_scales, wet_words, wet_scales, wg
 
         back1 = [keep.tile([P, T], F32, name=f"back1_{t}") for t in range(2)]
         for t in range(2):
-            scatter_z(t, back1[t], C1, C1)
-        second_product(0, *quantise(0, woven0), dx)
+            scatter_z(back1[t], C1, z[1, t])
+        accs0 = second_product(0, *quantise(0, woven0))
         back1.append(laid.tile([P, T], F32, name="back1_2", offset=0, align_bytes=64))
-        scatter_z(2, back1[2], C1, C1)
+        scatter_z(back1[2], C1, z[1, 2])
         back1.append(both)
         by_slot1 = turn_banks(1)
         for t in (3, 0, 1, 2):
@@ -225,18 +236,19 @@ def tile_moe_hib_relu2_kernel(tc, dy_words, dy_scales, wet_words, wet_scales, wg
             else:
                 da = keep.tile([P, C1], BF16, name=f"da1_{t}")
             times_slope(1, t, back1[t], da, by_slot1)
-        woven1 = keep.tile([P, C1, 4], BF16, name="woven1", tag="woven1", align_bytes=64)
+        woven1 = keep.tile([P, C1, 4], BF16, name="woven1", align_bytes=64)
         weave(1, by_slot1, woven1)
+        late_dx = keep.tile([P, C1], F32, name="late_dx", tag="pairs1_1")
+        nc.scalar.copy(late_dx[:], accs0[2][:])
 
-        tokens = [keep.tile([P, T], F32, name=f"tokens{kb}") for kb in range(2)]
+        tokens = [keep.tile([P, T], F32, name=f"tokens{kb}") for kb in range(3)]
         for kb in range(2):
-            scatter_dx(kb, tokens[kb], 0, C1)
-        second_product(1, *quantise(1, woven1), dx)
-        tokens.append(keep.tile([P, T], F32, name="tokens2", tag="woven1", align_bytes=64))
-        scatter_dx(2, tokens[2], 0, C1)
+            scatter_dx(tokens[kb], 0, dx[0, kb])
+        second_product(1, *quantise(1, woven1))
+        scatter_dx(tokens[2], 0, late_dx[:])
         for kb in range(3):
-            scatter_dx(kb, tokens[kb], C1, C1)
+            scatter_dx(tokens[kb], C1, dx[1, kb])
             store(kb, tokens[kb])
         tokens.append(keep.tile([P, WIDE], F32, name="tokens3"))
-        scatter_dx(3, tokens[3], 0, T)
+        scatter_dx(tokens[3], 0, dx_both[:])
         store(3, tokens[3])

@@ -28,7 +28,6 @@ def tile_moe_hib_relu2_kernel(tc, dy_words, dy_scales, wet_words, wet_scales, wg
     with ExitStack() as ctx:
         lists = ctx.enter_context(tc.tile_pool(name="lists", bufs=1))
         keep = ctx.enter_context(tc.tile_pool(name="keep", bufs=1))
-        laid = ctx.enter_context(tc.tile_pool(name="laid", bufs=1))
         psum = ctx.enter_context(tc.psum_pool(name="psum", bufs=1))
 
         def entries(tile, first, count):
@@ -136,19 +135,23 @@ def tile_moe_hib_relu2_kernel(tc, dy_words, dy_scales, wet_words, wet_scales, wg
         nc.sync.dma_start(gate_sb[1][:], gate[:, C1:T])
         for t in range(1, ROWS):
             first_product(0, t, 2)
-        for t in (3, 0, 1, 2):
+        for t in (3, 1, 2, 0):
             first_product(1, t, 2)
 
         a_view = a.rearrange("(t p) j -> p t j", p=P)
-        a_sb = [keep.tile([P, ROWS, C1], F32, name=f"a_sb{f}", tag=f"a{f}", align_bytes=64) for f in range(G)]
-        for f in range(G):
-            nc.sync.dma_start(a_sb[f][:], a_view[:, :, f * C1 : (f + 1) * C1])
-        slope = [keep.tile([P, ROWS, C1], F32, name=f"slope{f}") for f in range(G)]
-        for f in range(G):
-            for t in range(ROWS):
-                nc.scalar.activation(slope[f][:, t, :], a_sb[f][:, t, :], RELU, scale=2.0)
+        a_sb = [keep.tile([P, ROWS, C1], F32, name="a_sb0", tag="a0", align_bytes=64)]
+        a_sb.append(keep.tile([P, ROWS - 1, C1], F32, name="a_sb1", tag="a1", align_bytes=64))
+        a_late = keep.tile([P, C1], F32, name="a_late", tag="a_late")
+        nc.sync.dma_start(a_sb[0][:], a_view[:, :, 0:C1])
+        nc.sync.dma_start(a_sb[1][:], a_view[:, 1:ROWS, C1:T])
+        slope = {}
+        for f, t in [(0, t) for t in range(ROWS)] + [(1, t) for t in range(1, ROWS)]:
+            slope[f, t] = keep.tile([P, C1], F32, name=f"slope{f}_{t}")
+            nc.scalar.activation(slope[f, t][:], a_sb[f][:, t - f, :], RELU, scale=2.0)
         wgt_sb = keep.tile([P, G, 2 * K], U8, name="wgt_sb", tag="weights", align_bytes=64)
         nc.sync.dma_start(wgt_sb[:].bitcast(I32), wgt_words.rearrange("f s p c -> p (f s) c").bitcast(I32))
+
+        nc.sync.dma_start(a_late[:], a_view[:, 0, C1:T])
 
         def scatter_z(window, first, values):
             nc.vector.tensor_copy(window[:].indirect(entries(offs2_sb, first, values.shape[1])), values)
@@ -157,7 +160,7 @@ def tile_moe_hib_relu2_kernel(tc, dy_words, dy_scales, wet_words, wet_scales, wg
             return [psum.tile([P, 2, H], BF16, name=f"by_slot{f}_{h}", tag=f"by_slot{h}") for h in range(2)]
 
         def times_slope(f, t, window, da, by_slot):
-            nc.gpsimd.tensor_tensor(da[:], window[:, f * C1 : (f + 1) * C1], slope[f][:, t, :], MULT)
+            nc.gpsimd.tensor_tensor(da[:], window[:, f * C1 : (f + 1) * C1], slope[f, t][:], MULT)
             for b in range(4):
                 nc.tensor.transpose(by_slot[b // 2][:, b % 2, t * P : (t + 1) * P], da[:, b * P : (b + 1) * P], ident_bf[:])
 
@@ -219,20 +222,22 @@ def tile_moe_hib_relu2_kernel(tc, dy_words, dy_scales, wet_words, wet_scales, wg
         scatter_z(both, 0, z_both[:])
         for t, window in enumerate(back0 + [both]):
             times_slope(0, t, window, keep.tile([P, C1], BF16, name=f"da0_{t}"), by_slot0)
-        woven0 = laid.tile([P, C1, 4], BF16, name="woven0", offset=2048, align_bytes=64)
+        woven0 = keep.tile([P, C1, 4], BF16, name="woven0", tag="woven0", align_bytes=64)
         weave(0, by_slot0, woven0)
+        slope[1, 0] = keep.tile([P, C1], F32, name="slope1_0", tag="pairs0_1")
+        nc.scalar.activation(slope[1, 0][:], a_late[:], RELU, scale=2.0)
 
-        back1 = [keep.tile([P, T], F32, name=f"back1_{t}") for t in range(2)]
-        for t in range(2):
+        back1 = {3: both}
+        for t in (1, 2):
+            back1[t] = keep.tile([P, T], F32, name=f"back1_{t}")
             scatter_z(back1[t], C1, z[1, t])
         accs0 = second_product(0, *quantise(0, woven0))
-        back1.append(laid.tile([P, T], F32, name="back1_2", offset=0, align_bytes=64))
-        scatter_z(back1[2], C1, z[1, 2])
-        back1.append(both)
+        back1[0] = keep.tile([P, T], F32, name="back1_0", tag="a_late")
+        scatter_z(back1[0], C1, z[1, 0])
         by_slot1 = turn_banks(1)
-        for t in (3, 0, 1, 2):
-            if t == 1:
-                da = laid.tile([P, C1], BF16, name="da1_1", offset=4096, align_bytes=64)
+        for t in (3, 1, 2, 0):
+            if t == 2:
+                da = keep.tile([P, C1], BF16, name="da1_2", tag="woven0", align_bytes=64)
             else:
                 da = keep.tile([P, C1], BF16, name=f"da1_{t}")
             times_slope(1, t, back1[t], da, by_slot1)

@@ -49,7 +49,7 @@ def tile_moe_hib_relu2_kernel(tc, dy_words, dy_scales, wet_words, wet_scales, wg
         scale_rest = keep.tile([P, E, H // 2], U8, name="scale_rest", align_bytes=64)
         wgt_scale_sb = keep.tile([P, G, K], U8, name="wgt_scale_sb", align_bytes=64)
         nc.vector.memset(scale_first[:].bitcast(I32), 0)
-        nc.vector.memset(scale_rest[:].bitcast(I32), 0)
+        nc.gpsimd.memset(scale_rest[:].bitcast(I32), 0)
         nc.gpsimd.memset(wgt_scale_sb[:].bitcast(I32), 0)
         ident = keep.tile([P, P], F32, name="ident")
         make_identity(nc, ident[:])

@@ -15,11 +15,13 @@ U8 = mybir.dt.uint8
 FP8X4 = mybir.dt.float8_e4m3fn_x4
 FP4X4 = mybir.dt.float4_e2m1fn_x4
 RELU = mybir.ActivationFunctionType.Relu
+COPY = mybir.ActivationFunctionType.Copy
 MULT = mybir.AluOpType.mult
 
 P = 128
 PER_COL = 16
-ROWS = H // P
+PLANES = 4
+RUNS = T // P
 WIDE = 1408
 
 
@@ -44,139 +46,130 @@ def tile_moe_hib_relu2_kernel(tc, dy_words, dy_scales, wet_words, wet_scales, wg
         offs2_sb = lists.tile([P, T // PER_COL], U16, name="offs2_sb")
         offs_sb = lists.tile([P, T // PER_COL], U16, name="offs_sb")
 
-        dy_scale_sb = keep.tile([P, T], U8, name="dy_scale_sb", tag="gate1", align_bytes=64)
-        scale_first = keep.tile([P, E, H // 2], U8, name="scale_first", align_bytes=64)
-        scale_rest = keep.tile([P, E, H // 2], U8, name="scale_rest", align_bytes=64)
+        dy_scale_sb = keep.tile([P, T], U8, name="dy_scale_sb", tag="dy_scale", align_bytes=64)
+        wet_scale_sb = [keep.tile([P, 2, H], U8, name=f"wet_scale_sb{f}", align_bytes=64) for f in range(G)]
         wgt_scale_sb = keep.tile([P, G, K], U8, name="wgt_scale_sb", align_bytes=64)
-        nc.vector.memset(scale_first[:].bitcast(I32), 0)
-        nc.gpsimd.memset(scale_rest[:].bitcast(I32), 0)
-        nc.gpsimd.memset(wgt_scale_sb[:].bitcast(I32), 0)
+        nc.vector.memset(wet_scale_sb[0][:].bitcast(I32), 0)
         ident = keep.tile([P, P], F32, name="ident")
         make_identity(nc, ident[:])
-        ident_bf = keep.tile([P, P], BF16, name="ident_bf")
-        make_identity(nc, ident_bf[:])
+        nc.gpsimd.memset(wet_scale_sb[1][:].bitcast(I32), 0)
+        nc.gpsimd.memset(wgt_scale_sb[:].bitcast(I32), 0)
 
-        dy_word_sb = keep.tile([P, T], I32, name="dy_word_sb", tag="a0", align_bytes=64)
-        wet_first = keep.tile([P, 2, 2 * P], U8, name="wet_first", tag="wet_first", align_bytes=64)
-        wet_next = keep.tile([P, 2, 2 * (H - P)], U8, name="wet_next", tag="a1", align_bytes=64)
-        wet_rest = keep.tile([P, 2, 2 * H], U8, name="wet_rest", tag="weights", align_bytes=64)
-        gate_sb = [keep.tile([P, C1], F32, name="gate_sb0")]
+        dy_word_sb = keep.tile([P, T], I32, name="dy_word_sb", tag="dy_word", align_bytes=64)
+        wet_sb = [keep.tile([P, 2 * H], U8, name=f"wet_sb{e}", tag=f"wet{e}", align_bytes=64) for e in range(2)]
+        wet_rest = keep.tile([P, 2, 2 * H], U8, name="wet_rest", tag="wet_rest", align_bytes=64)
+        gate_col = keep.tile([P, RUNS], F32, name="gate_col")
         wet_view = wet_words.rearrange("e s p c -> p (e s) c")
         wet_scale_view = wet_scales.rearrange("e s b c -> (e s) b c")
-
-        def wet_block(e, t):
-            if e >= 2:
-                words = wet_rest[:, e - 2, 2 * t * P : 2 * (t + 1) * P]
-            elif t == 0:
-                words = wet_first[:, e, :]
-            else:
-                words = wet_next[:, e, 2 * (t - 1) * P : 2 * t * P]
-            return words, (scale_first, scale_rest)[t // 2][:, e, t % 2 * P : (t % 2 + 1) * P]
 
         nc.sync.dma_start(dst_sb[:], dst)
         for quad in range(4):
             rows = dy_scales[0, 4 * quad : 4 * quad + 4, :].bitcast(I32)
-            (nc.sync if quad < 2 else nc.scalar).dma_start(dy_scale_sb[32 * quad : 32 * quad + 32, 0:T].bitcast(I32), rows.unsqueeze(0).to_broadcast([8, 4, T // 4]))
+            (nc.sync if quad < 2 else nc.scalar).dma_start(dy_scale_sb[32 * quad : 32 * quad + 32, :].bitcast(I32), rows.unsqueeze(0).to_broadcast([8, 4, T // 4]))
         nc.sync.dma_start(dy_word_sb[:], dy_words[0].rearrange("p t d -> p (t d)").bitcast(I32))
-        nc.sync.dma_start(wet_first[:].bitcast(I32), wet_view[:, 0:2, 0 : 2 * P].bitcast(I32))
-        load_scale_rows(scale_first, wet_scale_view[:, :, 0 : H // 2])
-        nc.sync.dma_start(gate_sb[0][:, 0:C2], gate[:, 0:C2])
+        with nc.allow_non_contiguous_dma(reason="one weight a partition and run"):
+            nc.sync.dma_start(gate_col[:], gate[0].rearrange("(c x) -> x c", x=P))
+        nc.sync.dma_start(wet_sb[0][:].bitcast(I32), wet_view[:, 0, :].bitcast(I32))
+        load_scale_rows(wet_scale_sb[0], wet_scale_view[0:2])
         nc.sync.dma_start(offs2_sb[:], offs2)
-        nc.sync.dma_start(gate_sb[0][:, C2:C1], gate[:, C2:C1])
-        nc.sync.dma_start(wet_next[:].bitcast(I32), wet_view[:, 0:2, 2 * P : 2 * H].bitcast(I32))
-        load_scale_rows(scale_rest, wet_scale_view[:, :, H // 2 : H])
+        nc.sync.dma_start(wet_sb[1][:].bitcast(I32), wet_view[:, 1, :].bitcast(I32))
+        load_scale_rows(wet_scale_sb[1], wet_scale_view[2:E])
         nc.sync.dma_start(wet_rest[:].bitcast(I32), wet_view[:, 2:E, :].bitcast(I32))
         load_scale_rows(wgt_scale_sb, wgt_scales.rearrange("f s b c -> (f s) b c"))
         nc.sync.dma_start(offs_sb[:], offs)
 
+        gate_twice = keep.tile([P, RUNS], F32, name="gate_twice")
+        nc.scalar.activation(gate_twice[:], gate_col[:], COPY, scale=2.0)
+
         def gather_scales(f, tag):
             scales = keep.tile([P, C1], U8, name=f"g_scale{f}", tag=tag, align_bytes=64)
             nc.vector.tensor_copy(scales[:], dy_scale_sb[:].indirect(entries(dst_sb, f * C1, C1)))
-            return [scales[:, u * C2 : (u + 1) * C2] for u in range(2)]
+            return [scales[:, at : at + P] for at in range(0, C1, P)]
 
         g_scale = gather_scales(0, "g_scale0")
         g_word = []
-        for first, count in ((0, C2), (C2, C2), (C1, C1)):
+        for first, count in ((0, P), (P, C1 - P), (C1, C1)):
             words = keep.tile([P, count], U32, name=f"g_word{first}", align_bytes=64)
             nc.vector.tensor_copy(words[:], dy_word_sb[:].bitcast(U32).indirect(entries(dst_sb, first, count)))
-            g_word.extend(words[:, at : at + C2] for at in range(0, count, C2))
+            g_word.extend(words[:, at : at + P] for at in range(0, count, P))
+        g_scale.extend(gather_scales(1, "g_word0"))
 
-        def expert_sums(acc, e, t):
-            words, scales = wet_block(e, t)
+        by_slot = {}
+
+        def run_sums(run, cuts):
+            e = run // 2
+            acc = psum.tile([P, H], F32, name=f"acc1_{run}", tag=f"sum{run if run < 2 else 2 + run % 2}")
             nc.tensor.matmul_mx(
-                acc,
-                lhsT=words.bitcast(FP4X4),
-                lhsT_scale=scales,
-                rhs=g_word[e].bitcast(FP8X4),
-                rhs_scale=g_scale[e],
+                acc[:],
+                lhsT=g_word[run].bitcast(FP8X4),
+                lhsT_scale=g_scale[run],
+                rhs=(wet_sb[e][:] if e < 2 else wet_rest[:, e - 2, :]).bitcast(FP4X4),
+                rhs_scale=wet_scale_sb[e // 2][:, e % 2, :],
                 start=True,
                 stop=True,
             )
+            by_slot[run] = keep.tile([P, PLANES, P], F32, name=f"by_slot{run}", align_bytes=64)
+            for planes in cuts:
+                nc.scalar.activation(by_slot[run][:, planes, :], acc[:].rearrange("s (q r) -> s r q", r=PLANES)[:, planes, :], COPY, scale=gate_twice[:, run : run + 1])
 
-        def first_product(f, t, experts_per_bank):
-            sums = keep.tile([P, C1], F32, name=f"sums{f}_{t}")
-            for first in range(0, 2, experts_per_bank):
-                acc = psum.tile([P, experts_per_bank * C2], F32, name=f"acc1_{f}_{t}_{first}", tag="sum", bufs=4)
-                for u in range(experts_per_bank):
-                    expert_sums(acc[:, u * C2 : (u + 1) * C2], 2 * f + first + u, t)
-                cols = slice(first * C2, (first + experts_per_bank) * C2)
-                nc.scalar.copy(sums[:, cols], acc[:])
-                if (f, t) in z:
-                    nc.gpsimd.tensor_tensor(z[f, t][:, cols], sums[:, cols], gate_sb[f][:, cols], MULT)
-            return sums
+        z = [keep.tile([P, T], F32, name=f"z{r}") for r in range(PLANES)]
+        banks = {}
 
-        z_both = keep.tile([P, T], F32, name="z_both")
-        z = {(f, 3): z_both[:, f * C1 : (f + 1) * C1] for f in range(G)}
-        for f, t in ((0, 0), (0, 1), (0, 2), (1, 0), (1, 1), (1, 2)):
-            z[f, t] = keep.tile([P, C1], F32, name=f"z{f}_{t}")[:]
-        first_product(0, 0, 1)
-        g_scale.extend(gather_scales(1, "wet_first"))
-        gate_sb.append(keep.tile([P, C1], F32, name="gate_sb1", tag="gate1", align_bytes=64))
-        nc.sync.dma_start(gate_sb[1][:], gate[:, C1:T])
-        for t in range(1, ROWS):
-            first_product(0, t, 2)
-        for t in (3, 1, 2, 0):
-            first_product(1, t, 2)
+        def turn(r, first, count):
+            f = first // 4
+            if (f, r) not in banks:
+                banks[f, r] = psum.tile([P, C1], F32, name=f"plane{f}_{r}", tag=f"plane{r}")
+            for run in range(first, first + count):
+                nc.tensor.transpose(banks[f, r][:, run % 4 * P : (run % 4 + 1) * P], by_slot[run][:, r, :], ident[:])
+            nc.scalar.copy(z[r][:, first * P : (first + count) * P], banks[f, r][:, first % 4 * P : (first % 4 + count) * P])
 
-        a_view = a.rearrange("(t p) j -> p t j", p=P)
-        a_sb = [keep.tile([P, ROWS, C1], F32, name="a_sb0", tag="a0", align_bytes=64)]
-        a_sb.append(keep.tile([P, ROWS - 1, C1], F32, name="a_sb1", tag="a1", align_bytes=64))
+        whole = [slice(0, PLANES)]
+        run_sums(0, [slice(0, 1), slice(1, PLANES)])
+        for r in range(2):
+            piece = psum.tile([P, P], F32, name=f"piece{r}", tag=f"sum{r + 2}")
+            nc.tensor.transpose(piece[:], by_slot[0][:, r, :], ident[:])
+            nc.scalar.copy(z[r][:, 0:P], piece[:])
+        turn(2, 0, 1)
+        run_sums(1, whole)
+        turn(3, 0, 2)
+        run_sums(2, whole)
+        run_sums(3, whole)
+        for r in range(3):
+            turn(r, 1, 3)
+        turn(3, 2, 2)
+        for run in range(4, RUNS):
+            run_sums(run, whole)
+        for r in (3, 1, 2, 0):
+            turn(r, 4, 4)
+
+        a_view = a.rearrange("(q r) j -> q r j", r=PLANES)
+        a_sb = [keep.tile([P, PLANES, C1], F32, name="a_sb0", tag="dy_word", align_bytes=64)]
+        a_sb.append(keep.tile([P, PLANES - 1, C1], F32, name="a_sb1", tag="wet1", align_bytes=64))
         a_late = keep.tile([P, C1], F32, name="a_late", tag="a_late")
         nc.sync.dma_start(a_sb[0][:], a_view[:, :, 0:C1])
-        nc.sync.dma_start(a_sb[1][:], a_view[:, 1:ROWS, C1:T])
+        nc.sync.dma_start(a_sb[1][:], a_view[:, 1:PLANES, C1:T])
         slope = {}
-        for f, t in [(0, t) for t in range(ROWS)] + [(1, t) for t in range(1, ROWS)]:
-            slope[f, t] = keep.tile([P, C1], F32, name=f"slope{f}_{t}")
-            nc.scalar.activation(slope[f, t][:], a_sb[f][:, t - f, :], RELU, scale=2.0)
-        wgt_sb = keep.tile([P, G, 2 * K], U8, name="wgt_sb", tag="weights", align_bytes=64)
-        nc.sync.dma_start(wgt_sb[:].bitcast(I32), wgt_words.rearrange("f s p c -> p (f s) c").bitcast(I32))
 
+        def make_slope(f, r, source, tag):
+            slope[f, r] = keep.tile([P, C1], F32, name=f"slope{f}_{r}", tag=tag, align_bytes=64)
+            nc.scalar.activation(slope[f, r][:], source, RELU)
+
+        for run, (f, r) in enumerate([(0, r) for r in range(PLANES)] + [(1, 3), (1, 1)], 2):
+            make_slope(f, r, a_sb[f][:, r - f, :], f"by_slot{run}")
+        wgt_sb = keep.tile([P, G, 2 * K], U8, name="wgt_sb", tag="wet_rest", align_bytes=64)
+        nc.sync.dma_start(wgt_sb[:].bitcast(I32), wgt_words.rearrange("f s p c -> p (f s) c").bitcast(I32))
         nc.sync.dma_start(a_late[:], a_view[:, 0, C1:T])
 
-        def scatter_z(window, first, values):
-            nc.vector.tensor_copy(window[:].indirect(entries(offs2_sb, first, values.shape[1])), values)
+        def scatter_z(window, r, first, count):
+            nc.vector.tensor_copy(window[:].indirect(entries(offs2_sb, first, count)), z[r][:, first : first + count])
 
-        def turn_banks(f):
-            return [psum.tile([P, 2, H], BF16, name=f"by_slot{f}_{h}", tag=f"by_slot{h}") for h in range(2)]
+        def times_slope(f, r, window, da):
+            nc.gpsimd.tensor_tensor(da[:, r, :], window[:, f * C1 : (f + 1) * C1], slope[f, r][:], MULT)
 
-        def times_slope(f, t, window, da, by_slot):
-            nc.gpsimd.tensor_tensor(da[:], window[:, f * C1 : (f + 1) * C1], slope[f, t][:], MULT)
-            for b in range(4):
-                nc.tensor.transpose(by_slot[b // 2][:, b % 2, t * P : (t + 1) * P], da[:, b * P : (b + 1) * P], ident_bf[:])
-
-        def weave(f, by_slot, woven):
-            woven_words = woven[:].rearrange("p j r -> p (j r)").bitcast(F32)
-            for h in range(2):
-                pairs = keep.tile([P, 2, 2, P], F32, name=f"pairs{f}_{h}", tag=f"pairs{f}_{h}")
-                nc.scalar.copy(pairs[:], by_slot[h][:].bitcast(F32).rearrange("j b (q u) -> j b u q", u=2))
-                by_word = psum.tile([P, 2, 2, P], F32, name=f"by_word{f}_{h}", tag=f"by_word{h}")
-                for b in range(2):
-                    for u in range(2):
-                        nc.tensor.transpose(by_word[:, b, u, :], pairs[:, b, u, :], ident[:])
-                nc.scalar.copy(
-                    woven_words[:, h * C1 : (h + 1) * C1].rearrange("q (b j u) -> q b j u", b=2, u=2),
-                    by_word[:].rearrange("q b u j -> q b j u"),
-                )
+        def weave(f, da):
+            woven = keep.tile([P, C1, PLANES], BF16, name=f"woven{f}", tag=f"woven{f}", align_bytes=64)
+            nc.scalar.copy(woven[:].rearrange("q (c i) r -> q c r i", i=4), da[:].rearrange("q r (c i) -> q c r i", i=4))
+            return woven
 
         def quantise(f, woven):
             words = keep.tile([P, C1], U32, name=f"da_words{f}", align_bytes=64)
@@ -187,7 +180,7 @@ def tile_moe_hib_relu2_kernel(tc, dy_words, dy_scales, wet_words, wet_scales, wg
         def second_product(f, words, scales):
             accs = []
             for kb in range(K // P):
-                acc = psum.tile([P, C1], F32, name=f"acc2_{f}_{kb}", tag="sum", bufs=4)
+                acc = psum.tile([P, C1], F32, name=f"acc2_{f}_{kb}", tag=f"sum{kb}")
                 nc.tensor.matmul_mx(
                     acc[:],
                     lhsT=wgt_sb[:, f, 2 * kb * P : 2 * (kb + 1) * P].bitcast(FP4X4),
@@ -214,36 +207,32 @@ def tile_moe_hib_relu2_kernel(tc, dy_words, dy_scales, wet_words, wet_scales, wg
         for f, kb in ((0, 0), (0, 1), (1, 0), (1, 1), (1, 2)):
             dx[f, kb] = keep.tile([P, C1], F32, name=f"dx{f}_{kb}")[:]
 
-        by_slot0 = turn_banks(0)
-        back0 = [keep.tile([P, T], F32, name=f"back0_{t}") for t in range(3)]
-        both = keep.tile([P, WIDE], F32, name="back_both")
-        for t in range(3):
-            scatter_z(back0[t], 0, z[0, t])
-        scatter_z(both, 0, z_both[:])
-        for t, window in enumerate(back0 + [both]):
-            times_slope(0, t, window, keep.tile([P, C1], BF16, name=f"da0_{t}"), by_slot0)
-        woven0 = keep.tile([P, C1, 4], BF16, name="woven0", tag="woven0", align_bytes=64)
-        weave(0, by_slot0, woven0)
-        slope[1, 0] = keep.tile([P, C1], F32, name="slope1_0", tag="pairs0_1")
-        nc.scalar.activation(slope[1, 0][:], a_late[:], RELU, scale=2.0)
+        back0 = [keep.tile([P, T], F32, name=f"back0_{r}") for r in range(PLANES)]
+        for r in range(3):
+            scatter_z(back0[r], r, 0, P)
+        scatter_z(back0[3], 3, 0, C2)
+        for r in range(3):
+            scatter_z(back0[r], r, P, C1 - P)
+        scatter_z(back0[3], 3, C2, T - C2)
+        da0 = keep.tile([P, PLANES, C1], BF16, name="da0", tag="da0", align_bytes=64)
+        for r in range(PLANES):
+            times_slope(0, r, back0[r], da0)
+        woven0 = weave(0, da0)
+        make_slope(1, 0, a_late[:], "da0")
 
-        back1 = {3: both}
-        for t in (1, 2):
-            back1[t] = keep.tile([P, T], F32, name=f"back1_{t}")
-            scatter_z(back1[t], C1, z[1, t])
+        back1 = {3: back0[3]}
+        for r in (1, 2):
+            back1[r] = keep.tile([P, T], F32, name=f"back1_{r}")
+            scatter_z(back1[r], r, C1, C1)
         accs0 = second_product(0, *quantise(0, woven0))
+        make_slope(1, 2, a_sb[1][:, 1, :], "woven0")
         back1[0] = keep.tile([P, T], F32, name="back1_0", tag="a_late")
-        scatter_z(back1[0], C1, z[1, 0])
-        by_slot1 = turn_banks(1)
-        for t in (3, 1, 2, 0):
-            if t == 2:
-                da = keep.tile([P, C1], BF16, name="da1_2", tag="woven0", align_bytes=64)
-            else:
-                da = keep.tile([P, C1], BF16, name=f"da1_{t}")
-            times_slope(1, t, back1[t], da, by_slot1)
-        woven1 = keep.tile([P, C1, 4], BF16, name="woven1", align_bytes=64)
-        weave(1, by_slot1, woven1)
-        late_dx = keep.tile([P, C1], F32, name="late_dx", tag="pairs1_1")
+        scatter_z(back1[0], 0, C1, C1)
+        da1 = keep.tile([P, PLANES, C1], BF16, name="da1", tag="da1", align_bytes=64)
+        for r in (3, 1, 2, 0):
+            times_slope(1, r, back1[r], da1)
+        woven1 = weave(1, da1)
+        late_dx = keep.tile([P, C1], F32, name="late_dx", tag="da1", align_bytes=64)
         nc.scalar.copy(late_dx[:], accs0[2][:])
 
         tokens = [keep.tile([P, T], F32, name=f"tokens{kb}") for kb in range(3)]

@@ -58,28 +58,37 @@ def tile_moe_hib_relu2_kernel(tc, dy_words, dy_scales, wet_words, wet_scales, wg
         dy_word_sb = keep.tile([P, T], I32, name="dy_word_sb", tag="dy_word", align_bytes=64)
         wet_sb = [keep.tile([P, 2 * H], U8, name=f"wet_sb{e}", tag=f"wet{e}", align_bytes=64) for e in range(2)]
         wet_rest = keep.tile([P, 2, 2 * H], U8, name="wet_rest", tag="wet_rest", align_bytes=64)
-        gate_col = keep.tile([P, RUNS], F32, name="gate_col")
+        gate_twice = []
         wet_view = wet_words.rearrange("e s p c -> p (e s) c")
         wet_scale_view = wet_scales.rearrange("e s b c -> (e s) b c")
+
+        def load_gate(first, last):
+            column = keep.tile([P, last - first], F32, name=f"gate_col{first}")
+            with nc.allow_non_contiguous_dma(reason="one weight a partition and run"):
+                nc.sync.dma_start(column[:], gate[0].rearrange("(c x) -> x c", x=P)[:, first:last])
+            return column
+
+        def double_gate(column, tag):
+            count = column.shape[1]
+            twice = keep.tile([P, count], F32, name=f"gate_twice{count}", tag=tag, align_bytes=64)
+            nc.scalar.activation(twice[:], column[:], COPY, scale=2.0)
+            gate_twice.extend(twice[:, c : c + 1] for c in range(count))
 
         nc.sync.dma_start(dst_sb[:], dst)
         for quad in range(4):
             rows = dy_scales[0, 4 * quad : 4 * quad + 4, :].bitcast(I32)
             (nc.sync if quad < 2 else nc.scalar).dma_start(dy_scale_sb[32 * quad : 32 * quad + 32, :].bitcast(I32), rows.unsqueeze(0).to_broadcast([8, 4, T // 4]))
         nc.sync.dma_start(dy_word_sb[:], dy_words[0].rearrange("p t d -> p (t d)").bitcast(I32))
-        with nc.allow_non_contiguous_dma(reason="one weight a partition and run"):
-            nc.sync.dma_start(gate_col[:], gate[0].rearrange("(c x) -> x c", x=P))
         nc.sync.dma_start(wet_sb[0][:].bitcast(I32), wet_view[:, 0, :].bitcast(I32))
         load_scale_rows(wet_scale_sb[0], wet_scale_view[0:2])
+        double_gate(load_gate(0, 2), "gate_twice")
         nc.sync.dma_start(offs2_sb[:], offs2)
         nc.sync.dma_start(wet_sb[1][:].bitcast(I32), wet_view[:, 1, :].bitcast(I32))
+        gate_rest = load_gate(2, RUNS)
         load_scale_rows(wet_scale_sb[1], wet_scale_view[2:E])
         nc.sync.dma_start(wet_rest[:].bitcast(I32), wet_view[:, 2:E, :].bitcast(I32))
         load_scale_rows(wgt_scale_sb, wgt_scales.rearrange("f s b c -> (f s) b c"))
         nc.sync.dma_start(offs_sb[:], offs)
-
-        gate_twice = keep.tile([P, RUNS], F32, name="gate_twice")
-        nc.scalar.activation(gate_twice[:], gate_col[:], COPY, scale=2.0)
 
         def gather_scales(f, tag):
             scales = keep.tile([P, C1], U8, name=f"g_scale{f}", tag=tag, align_bytes=64)
@@ -110,7 +119,7 @@ def tile_moe_hib_relu2_kernel(tc, dy_words, dy_scales, wet_words, wet_scales, wg
             )
             by_slot[run] = keep.tile([P, PLANES, P], F32, name=f"by_slot{run}", align_bytes=64)
             for planes in cuts:
-                nc.scalar.activation(by_slot[run][:, planes, :], acc[:].rearrange("s (q r) -> s r q", r=PLANES)[:, planes, :], COPY, scale=gate_twice[:, run : run + 1])
+                nc.scalar.activation(by_slot[run][:, planes, :], acc[:].rearrange("s (q r) -> s r q", r=PLANES)[:, planes, :], COPY, scale=gate_twice[run])
 
         z = [keep.tile([P, T], F32, name=f"z{r}") for r in range(PLANES)]
         banks = {}
@@ -132,6 +141,7 @@ def tile_moe_hib_relu2_kernel(tc, dy_words, dy_scales, wet_words, wet_scales, wg
         turn(2, 0, 1)
         run_sums(1, whole)
         turn(3, 0, 2)
+        double_gate(gate_rest, "by_slot0")
         run_sums(2, whole)
         run_sums(3, whole)
         for r in range(3):

@@ -149,32 +149,28 @@ def tile_moe_hib_relu2_kernel(tc, dy_words, dy_scales, wet_words, wet_scales, wg
         turn(3, 2, 2)
         for run in range(4, RUNS):
             run_sums(run, whole)
-        for r in (3, 1, 2, 0):
+        for r in (3, 1, 2):
             turn(r, 4, 4)
+        late_bank = psum.tile([P, C1], F32, name="late_bank", tag="plane0")
+        for run in range(4, RUNS):
+            nc.tensor.transpose(late_bank[:, run % 4 * P : (run % 4 + 1) * P], by_slot[run][:, 0, :], ident[:])
 
         a_view = a.rearrange("(q r) j -> q r j", r=PLANES)
         a_sb = [keep.tile([P, PLANES, C1], F32, name="a_sb0", tag="dy_word", align_bytes=64)]
-        a_sb.append(keep.tile([P, PLANES - 1, C1], F32, name="a_sb1", tag="wet1", align_bytes=64))
-        a_late = keep.tile([P, C1], F32, name="a_late", tag="a_late")
-        nc.sync.dma_start(a_sb[0][:], a_view[:, :, 0:C1])
-        nc.sync.dma_start(a_sb[1][:], a_view[:, 1:PLANES, C1:T])
-        slope = {}
-
-        def make_slope(f, r, source, tag):
-            slope[f, r] = keep.tile([P, C1], F32, name=f"slope{f}_{r}", tag=tag, align_bytes=64)
-            nc.scalar.activation(slope[f, r][:], source, RELU)
-
-        for run, (f, r) in enumerate([(0, r) for r in range(PLANES)] + [(1, 3), (1, 1)], 2):
-            make_slope(f, r, a_sb[f][:, r - f, :], f"by_slot{run}")
+        a_sb.append(keep.tile([P, PLANES, C1], F32, name="a_sb1", tag="wet1", align_bytes=64))
+        slope = []
+        for f in range(G):
+            nc.sync.dma_start(a_sb[f][:], a_view[:, :, f * C1 : (f + 1) * C1])
+            slope.append(keep.tile([P, PLANES, C1], F32, name=f"slope{f}", tag=f"by_slot{4 * f + 3}", align_bytes=64))
+            nc.scalar.activation(slope[f][:], a_sb[f][:], RELU)
         wgt_sb = keep.tile([P, G, 2 * K], U8, name="wgt_sb", tag="wet_rest", align_bytes=64)
         nc.sync.dma_start(wgt_sb[:].bitcast(I32), wgt_words.rearrange("f s p c -> p (f s) c").bitcast(I32))
-        nc.sync.dma_start(a_late[:], a_view[:, 0, C1:T])
 
         def scatter_z(window, r, first, count):
             nc.vector.tensor_copy(window[:].indirect(entries(offs2_sb, first, count)), z[r][:, first : first + count])
 
         def times_slope(f, r, window, da):
-            nc.gpsimd.tensor_tensor(da[:, r, :], window[:, f * C1 : (f + 1) * C1], slope[f, r][:], MULT)
+            nc.gpsimd.tensor_tensor(da[:, r, :], window[:, f * C1 : (f + 1) * C1], slope[f][:, r, :], MULT)
 
         def weave(f, da):
             woven = keep.tile([P, C1, PLANES], BF16, name=f"woven{f}", tag=f"woven{f}", align_bytes=64)
@@ -209,8 +205,7 @@ def tile_moe_hib_relu2_kernel(tc, dy_words, dy_scales, wet_words, wet_scales, wg
             nc.vector.tensor_copy(window[:].indirect(entries(offs_sb, first, values.shape[1])), values)
 
         def store(kb, window):
-            for queue, cols in ((nc.sync, slice(0, T // 2)), (nc.scalar, slice(T // 2, T))):
-                queue.dma_start(out[kb * P : (kb + 1) * P, cols], window[:, cols])
+            nc.sync.dma_start(out[kb * P : (kb + 1) * P, :], window[:, 0:T])
 
         dx_both = keep.tile([P, T], F32, name="dx_both")
         dx = {(f, 3): dx_both[:, f * C1 : (f + 1) * C1] for f in range(G)}
@@ -228,16 +223,16 @@ def tile_moe_hib_relu2_kernel(tc, dy_words, dy_scales, wet_words, wet_scales, wg
         for r in range(PLANES):
             times_slope(0, r, back0[r], da0)
         woven0 = weave(0, da0)
-        make_slope(1, 0, a_late[:], "da0")
+        z_late = keep.tile([P, C1], F32, name="z_late", tag="da0", align_bytes=64)
+        nc.scalar.copy(z_late[:], late_bank[:])
 
         back1 = {3: back0[3]}
         for r in (1, 2):
             back1[r] = keep.tile([P, T], F32, name=f"back1_{r}")
             scatter_z(back1[r], r, C1, C1)
         accs0 = second_product(0, *quantise(0, woven0))
-        make_slope(1, 2, a_sb[1][:, 1, :], "woven0")
-        back1[0] = keep.tile([P, T], F32, name="back1_0", tag="a_late")
-        scatter_z(back1[0], 0, C1, C1)
+        back1[0] = keep.tile([P, T], F32, name="back1_0")
+        nc.vector.tensor_copy(back1[0][:].indirect(entries(offs2_sb, C1, C1)), z_late[:])
         da1 = keep.tile([P, PLANES, C1], BF16, name="da1", tag="da1", align_bytes=64)
         for r in (3, 1, 2, 0):
             times_slope(1, r, back1[r], da1)

@@ -138,15 +138,16 @@ def tile_moe_hib_relu2_kernel(tc, dy_words, dy_scales, wet_words, wet_scales, wg
             piece = psum.tile([P, P], F32, name=f"piece{r}", tag=f"sum{r + 2}")
             nc.tensor.transpose(piece[:], by_slot[0][:, r, :], ident[:])
             nc.scalar.copy(z[r][:, 0:P], piece[:])
-        turn(2, 0, 1)
         run_sums(1, whole)
-        turn(3, 0, 2)
+        for r in (2, 3):
+            turn(r, 0, 2)
         double_gate(gate_rest, "by_slot0")
         run_sums(2, whole)
         run_sums(3, whole)
-        for r in range(3):
+        for r in range(2):
             turn(r, 1, 3)
-        turn(3, 2, 2)
+        for r in (2, 3):
+            turn(r, 2, 2)
         for run in range(4, RUNS):
             run_sums(run, whole)
         for r in (3, 1, 2):
@@ -213,12 +214,11 @@ def tile_moe_hib_relu2_kernel(tc, dy_words, dy_scales, wet_words, wet_scales, wg
             dx[f, kb] = keep.tile([P, C1], F32, name=f"dx{f}_{kb}")[:]
 
         back0 = [keep.tile([P, T], F32, name=f"back0_{r}") for r in range(PLANES)]
-        for r in range(3):
-            scatter_z(back0[r], r, 0, P)
-        scatter_z(back0[3], 3, 0, C2)
-        for r in range(3):
-            scatter_z(back0[r], r, P, C1 - P)
-        scatter_z(back0[3], 3, C2, T - C2)
+        early = (P, P, C2, C2)
+        for r in range(PLANES):
+            scatter_z(back0[r], r, 0, early[r])
+        for r in range(PLANES):
+            scatter_z(back0[r], r, early[r], (T if r == 3 else C1) - early[r])
         da0 = keep.tile([P, PLANES, C1], BF16, name="da0", tag="da0", align_bytes=64)
         for r in range(PLANES):
             times_slope(0, r, back0[r], da0)

@@ -1,7 +1,6 @@
 from contextlib import ExitStack
 
 import concourse.mybir as mybir
-from concourse.masks import make_identity
 
 K, T, G, C1, E, C2, H, N = 512, 1024, 2, 512, 4, 256, 512, 512
 FLOPS = 2 * T * N * H + 2 * T * H * K
@@ -14,15 +13,13 @@ U16 = mybir.dt.uint16
 U8 = mybir.dt.uint8
 FP8X4 = mybir.dt.float8_e4m3fn_x4
 FP4X4 = mybir.dt.float4_e2m1fn_x4
-RELU = mybir.ActivationFunctionType.Relu
 COPY = mybir.ActivationFunctionType.Copy
 MULT = mybir.AluOpType.mult
+MAX = mybir.AluOpType.max
 
 P = 128
 PER_COL = 16
 PLANES = 4
-RUNS = T // P
-WIDE = 1408
 
 
 def tile_moe_hib_relu2_kernel(tc, dy_words, dy_scales, wet_words, wet_scales, wgt_words, wgt_scales, a, gate, offs, offs2, dst, out):
@@ -30,6 +27,7 @@ def tile_moe_hib_relu2_kernel(tc, dy_words, dy_scales, wet_words, wet_scales, wg
     with ExitStack() as ctx:
         lists = ctx.enter_context(tc.tile_pool(name="lists", bufs=1))
         keep = ctx.enter_context(tc.tile_pool(name="keep", bufs=1))
+        reuse = ctx.enter_context(tc.tile_pool(name="reuse", bufs=1))
         psum = ctx.enter_context(tc.psum_pool(name="psum", bufs=1))
 
         def entries(tile, first, count):
@@ -46,148 +44,109 @@ def tile_moe_hib_relu2_kernel(tc, dy_words, dy_scales, wet_words, wet_scales, wg
         offs2_sb = lists.tile([P, T // PER_COL], U16, name="offs2_sb")
         offs_sb = lists.tile([P, T // PER_COL], U16, name="offs_sb")
 
-        dy_scale_sb = keep.tile([P, T], U8, name="dy_scale_sb", tag="dy_scale", align_bytes=64)
-        wet_scale_sb = [keep.tile([P, 2, H], U8, name=f"wet_scale_sb{f}", align_bytes=64) for f in range(G)]
+        dy_scale_sb = keep.tile([P, T], U8, name="dy_scale_sb", align_bytes=64)
+        dy_word_sb = keep.tile([P, T], I32, name="dy_word_sb", align_bytes=64)
+        wet_scale_sb = keep.tile([P, E, H], U8, name="wet_scale_sb", align_bytes=64)
         wgt_scale_sb = keep.tile([P, G, K], U8, name="wgt_scale_sb", align_bytes=64)
-        nc.vector.memset(wet_scale_sb[0][:].bitcast(I32), 0)
-        ident = keep.tile([P, P], F32, name="ident")
-        make_identity(nc, ident[:])
-        nc.gpsimd.memset(wet_scale_sb[1][:].bitcast(I32), 0)
-        nc.gpsimd.memset(wgt_scale_sb[:].bitcast(I32), 0)
+        nc.vector.memset(wet_scale_sb[:].bitcast(I32), 0)
+        nc.vector.memset(wgt_scale_sb[:].bitcast(I32), 0)
 
-        dy_word_sb = keep.tile([P, T], I32, name="dy_word_sb", tag="dy_word", align_bytes=64)
-        wet_sb = [keep.tile([P, 2 * H], U8, name=f"wet_sb{e}", tag=f"wet{e}", align_bytes=64) for e in range(2)]
-        wet_rest = keep.tile([P, 2, 2 * H], U8, name="wet_rest", tag="wet_rest", align_bytes=64)
-        gate_twice = []
         wet_view = wet_words.rearrange("e s p c -> p (e s) c")
-        wet_scale_view = wet_scales.rearrange("e s b c -> (e s) b c")
-
-        def load_gate(first, last):
-            column = keep.tile([P, last - first], F32, name=f"gate_col{first}")
-            with nc.allow_non_contiguous_dma(reason="one weight a partition and run"):
-                nc.sync.dma_start(column[:], gate[0].rearrange("(c x) -> x c", x=P)[:, first:last])
-            return column
-
-        def double_gate(column, tag):
-            count = column.shape[1]
-            twice = keep.tile([P, count], F32, name=f"gate_twice{count}", tag=tag, align_bytes=64)
-            nc.scalar.activation(twice[:], column[:], COPY, scale=2.0)
-            gate_twice.extend(twice[:, c : c + 1] for c in range(count))
+        wet_sb = [keep.tile([P, 2, 2 * H], U8, name=f"wet_sb{f}", align_bytes=64) for f in range(G)]
+        gate_sb = [keep.tile([P, C1], F32, name=f"gate_sb{f}") for f in range(G)]
+        a_view = a.rearrange("(q r) j -> q r j", r=PLANES)
+        a_sb = [keep.tile([P, 2, T], F32, name="a_sb0"), reuse.tile([P, 2, T], F32, name="a_sb1", offset=0, align_bytes=64)]
+        wgt_sb = keep.tile([P, G, 2 * K], U8, name="wgt_sb", align_bytes=64)
 
         nc.sync.dma_start(dst_sb[:], dst)
         for quad in range(4):
             rows = dy_scales[0, 4 * quad : 4 * quad + 4, :].bitcast(I32)
             (nc.sync if quad < 2 else nc.scalar).dma_start(dy_scale_sb[32 * quad : 32 * quad + 32, :].bitcast(I32), rows.unsqueeze(0).to_broadcast([8, 4, T // 4]))
         nc.sync.dma_start(dy_word_sb[:], dy_words[0].rearrange("p t d -> p (t d)").bitcast(I32))
-        nc.sync.dma_start(wet_sb[0][:].bitcast(I32), wet_view[:, 0, :].bitcast(I32))
-        load_scale_rows(wet_scale_sb[0], wet_scale_view[0:2])
-        double_gate(load_gate(0, 2), "gate_twice")
+        nc.sync.dma_start(wet_sb[0][:].bitcast(I32), wet_view[:, 0:2, :].bitcast(I32))
+        load_scale_rows(wet_scale_sb, wet_scales.rearrange("e s b c -> (e s) b c"))
+        nc.sync.dma_start(gate_sb[0][:], gate[:, 0:C1])
         nc.sync.dma_start(offs2_sb[:], offs2)
-        nc.sync.dma_start(wet_sb[1][:].bitcast(I32), wet_view[:, 1, :].bitcast(I32))
-        gate_rest = load_gate(2, RUNS)
-        load_scale_rows(wet_scale_sb[1], wet_scale_view[2:E])
-        nc.sync.dma_start(wet_rest[:].bitcast(I32), wet_view[:, 2:E, :].bitcast(I32))
+        nc.sync.dma_start(wet_sb[1][:].bitcast(I32), wet_view[:, 2:E, :].bitcast(I32))
+        for pair in range(2):
+            nc.sync.dma_start(a_sb[pair][:], a_view[:, 2 * pair : 2 * pair + 2, :])
+        nc.sync.dma_start(gate_sb[1][:], gate[:, C1:T])
         load_scale_rows(wgt_scale_sb, wgt_scales.rearrange("f s b c -> (f s) b c"))
+        nc.sync.dma_start(wgt_sb[:].bitcast(I32), wgt_words.rearrange("f s p c -> p (f s) c").bitcast(I32))
         nc.sync.dma_start(offs_sb[:], offs)
 
-        def gather_scales(f, tag):
-            scales = keep.tile([P, C1], U8, name=f"g_scale{f}", tag=tag, align_bytes=64)
-            nc.vector.tensor_copy(scales[:], dy_scale_sb[:].indirect(entries(dst_sb, f * C1, C1)))
-            return [scales[:, at : at + P] for at in range(0, C1, P)]
-
-        g_scale = gather_scales(0, "g_scale0")
-        g_word = []
-        for first, count in ((0, P), (P, C1 - P), (C1, C1)):
-            words = keep.tile([P, count], U32, name=f"g_word{first}", align_bytes=64)
-            nc.vector.tensor_copy(words[:], dy_word_sb[:].bitcast(U32).indirect(entries(dst_sb, first, count)))
-            g_word.extend(words[:, at : at + P] for at in range(0, count, P))
-        g_scale.extend(gather_scales(1, "g_word0"))
-
-        by_slot = {}
-
-        def run_sums(run, cuts):
-            e = run // 2
-            acc = psum.tile([P, H], F32, name=f"acc1_{run}", tag=f"sum{run if run < 2 else 2 + run % 2}")
-            nc.tensor.matmul_mx(
-                acc[:],
-                lhsT=g_word[run].bitcast(FP8X4),
-                lhsT_scale=g_scale[run],
-                rhs=(wet_sb[e][:] if e < 2 else wet_rest[:, e - 2, :]).bitcast(FP4X4),
-                rhs_scale=wet_scale_sb[e // 2][:, e % 2, :],
-                start=True,
-                stop=True,
+        sorted_words, sorted_scales = {}, {}
+        for e in range(E):
+            words = keep.tile([P, PLANES, P], U16, name=f"sorted_words{e}", align_bytes=64)
+            nc.scalar.copy(
+                words[:].rearrange("p r (c i) -> p c r i", i=8),
+                wet_sb[e // 2][:, e % 2, :].bitcast(U16).rearrange("p (c i r) -> p c r i", i=8, r=PLANES),
             )
-            by_slot[run] = keep.tile([P, PLANES, P], F32, name=f"by_slot{run}", align_bytes=64)
-            for planes in cuts:
-                nc.scalar.activation(by_slot[run][:, planes, :], acc[:].rearrange("s (q r) -> s r q", r=PLANES)[:, planes, :], COPY, scale=gate_twice[run])
+            for r in range(PLANES):
+                sorted_words[e, r] = words[:, r, :]
+        for e, first, count in ((0, 0, 2), (1, 0, 2), (0, 2, 2), (1, 2, 2), (2, 0, 4), (3, 0, 4)):
+            scales = keep.tile([P, count, P], U8, name=f"sorted_scales{e}_{first}", align_bytes=64)
+            nc.gpsimd.tensor_copy(
+                scales[:].rearrange("p r (c i) -> p c r i", i=16),
+                wet_scale_sb[:, e, :].rearrange("p (c i r) -> p c r i", i=16, r=PLANES)[:, :, first : first + count, :],
+            )
+            for r in range(count):
+                sorted_scales[e, first + r] = scales[:, r, :]
 
-        z = [keep.tile([P, T], F32, name=f"z{r}") for r in range(PLANES)]
-        banks = {}
+        z = {(f, pair): keep.tile([P, 2, C1], F32, name=f"z{f}_{pair}") for f in range(G) for pair in range(2)}
 
-        def turn(r, first, count):
-            f = first // 4
-            if (f, r) not in banks:
-                banks[f, r] = psum.tile([P, C1], F32, name=f"plane{f}_{r}", tag=f"plane{r}")
-            for run in range(first, first + count):
-                nc.tensor.transpose(banks[f, r][:, run % 4 * P : (run % 4 + 1) * P], by_slot[run][:, r, :], ident[:])
-            nc.scalar.copy(z[r][:, first * P : (first + count) * P], banks[f, r][:, first % 4 * P : (first % 4 + count) * P])
+        def gather_scales(f):
+            scales = keep.tile([P, C1], U8, name=f"g_scale{f}", align_bytes=64)
+            nc.vector.tensor_copy(scales[:], dy_scale_sb[:].indirect(entries(dst_sb, f * C1, C1)))
+            return scales
 
-        whole = [slice(0, PLANES)]
-        run_sums(0, [slice(0, 1), slice(1, PLANES)])
-        for r in range(2):
-            piece = psum.tile([P, P], F32, name=f"piece{r}", tag=f"sum{r + 2}")
-            nc.tensor.transpose(piece[:], by_slot[0][:, r, :], ident[:])
-            nc.scalar.copy(z[r][:, 0:P], piece[:])
-        run_sums(1, whole)
-        for r in (2, 3):
-            turn(r, 0, 2)
-        double_gate(gate_rest, "by_slot0")
-        run_sums(2, whole)
-        run_sums(3, whole)
-        for r in range(2):
-            turn(r, 1, 3)
-        for r in (2, 3):
-            turn(r, 2, 2)
-        for run in range(4, RUNS):
-            run_sums(run, whole)
-        for r in (3, 1, 2):
-            turn(r, 4, 4)
-        late_bank = psum.tile([P, C1], F32, name="late_bank", tag="plane0")
-        for run in range(4, RUNS):
-            nc.tensor.transpose(late_bank[:, run % 4 * P : (run % 4 + 1) * P], by_slot[run][:, 0, :], ident[:])
+        def gather_words(e):
+            words = keep.tile([P, C2], U32, name=f"g_word{e}", tag=f"g_word{e % 2}", align_bytes=64)
+            nc.vector.tensor_copy(words[:], dy_word_sb[:].bitcast(U32).indirect(entries(dst_sb, e * C2, C2)))
+            return words
 
-        a_view = a.rearrange("(q r) j -> q r j", r=PLANES)
-        a_sb = [keep.tile([P, PLANES, C1], F32, name="a_sb0", tag="dy_word", align_bytes=64)]
-        a_sb.append(keep.tile([P, PLANES, C1], F32, name="a_sb1", tag="wet1", align_bytes=64))
-        slope = []
-        for f in range(G):
-            nc.sync.dma_start(a_sb[f][:], a_view[:, :, f * C1 : (f + 1) * C1])
-            slope.append(keep.tile([P, PLANES, C1], F32, name=f"slope{f}", tag=f"by_slot{4 * f + 3}", align_bytes=64))
-            nc.scalar.activation(slope[f][:], a_sb[f][:], RELU)
-        wgt_sb = keep.tile([P, G, 2 * K], U8, name="wgt_sb", tag="wet_rest", align_bytes=64)
-        nc.sync.dma_start(wgt_sb[:].bitcast(I32), wgt_words.rearrange("f s p c -> p (f s) c").bitcast(I32))
+        def first_product(e, pair, words, scales):
+            acc = psum.tile([P, 2, C2], F32, name=f"acc1_{e}_{pair}", tag=f"bank{2 * e + pair}")
+            for half in range(2):
+                nc.tensor.matmul_mx(
+                    acc[:, half, :],
+                    lhsT=sorted_words[e, 2 * pair + half].bitcast(U8).bitcast(FP4X4),
+                    lhsT_scale=sorted_scales[e, 2 * pair + half],
+                    rhs=words[:].bitcast(FP8X4),
+                    rhs_scale=scales[:, e % 2 * C2 : (e % 2 + 1) * C2],
+                    start=True,
+                    stop=True,
+                )
+            cols = slice(e % 2 * C2, (e % 2 + 1) * C2)
+            nc.vector.tensor_tensor(z[e // 2, pair][:, :, cols], acc[:], gate_sb[e // 2][:, cols].unsqueeze(1).to_broadcast([P, 2, C2]), MULT)
 
-        def scatter_z(window, r, first, count):
-            nc.vector.tensor_copy(window[:].indirect(entries(offs2_sb, first, count)), z[r][:, first : first + count])
+        def on_vector(window, offsets, first, values):
+            nc.vector.tensor_copy(window[:].indirect(entries(offsets, first, values.shape[1])), values)
 
-        def times_slope(f, r, window, da):
-            nc.gpsimd.tensor_tensor(da[:, r, :], window[:, f * C1 : (f + 1) * C1], slope[f][:, r, :], MULT)
+        def on_scalar(window, offsets, first, values):
+            nc.scalar.activation(window[:].indirect(entries(offsets, first, values.shape[1])), values, COPY)
 
-        def weave(f, da):
-            woven = keep.tile([P, C1, PLANES], BF16, name=f"woven{f}", tag=f"woven{f}", align_bytes=64)
-            nc.scalar.copy(woven[:].rearrange("q (c i) r -> q c r i", i=4), da[:].rearrange("q r (c i) -> q c r i", i=4))
+        back = [keep.tile([P, T], F32, name=f"back{r}", tag=f"back{r}") if r != 2 else reuse.tile([P, T], F32, name="back2", offset=0, align_bytes=64) for r in range(PLANES)]
+
+        def z_half(e, r):
+            on_scalar(back[r], offs2_sb, e * C2, z[e // 2, r // 2][:, r % 2, e % 2 * C2 : (e % 2 + 1) * C2])
+
+        def z_whole(f, r):
+            on_vector(back[r], offs2_sb, f * C1, z[f, r // 2][:, r % 2, :])
+
+        def times_slope(f):
+            woven = reuse.tile([P, C1, PLANES], BF16, name=f"woven{f}", offset=4 * T, align_bytes=64)
+            for r in range(PLANES):
+                nc.gpsimd.tensor_tensor(woven[:, :, r], back[r][:, f * C1 : (f + 1) * C1], slope[r // 2][:, r % 2, f * C1 : (f + 1) * C1], MULT)
             return woven
 
-        def quantise(f, woven):
+        def second_product(f, woven):
             words = keep.tile([P, C1], U32, name=f"da_words{f}", align_bytes=64)
             scales = keep.tile([P, C1], U8, name=f"da_scales{f}", align_bytes=64)
             nc.vector.quantize_mx(words[:].bitcast(FP8X4), scales[:], woven[:].rearrange("p j r -> p (j r)"))
-            return words, scales
-
-        def second_product(f, words, scales):
             accs = []
             for kb in range(K // P):
-                acc = psum.tile([P, C1], F32, name=f"acc2_{f}_{kb}", tag=f"sum{kb}")
+                acc = psum.tile([P, C1], F32, name=f"acc2_{f}_{kb}", tag=f"bank{4 * f + kb}")
                 nc.tensor.matmul_mx(
                     acc[:],
                     lhsT=wgt_sb[:, f, 2 * kb * P : 2 * (kb + 1) * P].bitcast(FP4X4),
@@ -197,57 +156,60 @@ def tile_moe_hib_relu2_kernel(tc, dy_words, dy_scales, wet_words, wet_scales, wg
                     start=True,
                     stop=True,
                 )
-                if (f, kb) in dx:
-                    nc.scalar.copy(dx[f, kb], acc[:])
                 accs.append(acc)
             return accs
 
-        def scatter_dx(window, first, values):
-            nc.vector.tensor_copy(window[:].indirect(entries(offs_sb, first, values.shape[1])), values)
-
         def store(kb, window):
-            nc.sync.dma_start(out[kb * P : (kb + 1) * P, :], window[:, 0:T])
+            (nc.scalar if kb % 2 else nc.sync).dma_start(out[kb * P : (kb + 1) * P, :], window[:])
 
-        dx_both = keep.tile([P, T], F32, name="dx_both")
-        dx = {(f, 3): dx_both[:, f * C1 : (f + 1) * C1] for f in range(G)}
-        for f, kb in ((0, 0), (0, 1), (1, 0), (1, 1), (1, 2)):
-            dx[f, kb] = keep.tile([P, C1], F32, name=f"dx{f}_{kb}")[:]
+        g_scale = [gather_scales(0)]
+        g_word = [gather_words(0), gather_words(1)]
+        g_scale.append(gather_scales(1))
+        for pair in range(2):
+            for e in range(2):
+                first_product(e, pair, g_word[e], g_scale[0])
+        g_word.extend(gather_words(e) for e in (2, 3))
+        slope = [keep.tile([P, 2, T], F32, name=f"slope{pair}") for pair in range(2)]
+        for pair in range(2):
+            nc.vector.tensor_scalar(slope[pair][:], a_sb[pair][:], 2.0, 0.0, MULT, MAX)
+        for e, r in ((0, 0), (0, 1), (1, 0), (0, 3), (1, 1), (1, 3)):
+            z_half(e, r)
+        first_product(2, 0, g_word[2], g_scale[1])
+        z_whole(0, 2)
+        for e, pair in ((3, 0), (2, 1), (3, 1)):
+            first_product(e, pair, g_word[e], g_scale[1])
+        woven0 = times_slope(0)
+        z_whole(1, 1)
+        accs0 = second_product(0, woven0)
+        z_whole(1, 3)
+        for e, r in ((2, 0), (2, 2), (3, 0), (3, 2)):
+            z_half(e, r)
+        woven1 = times_slope(1)
 
-        back0 = [keep.tile([P, T], F32, name=f"back0_{r}") for r in range(PLANES)]
-        early = (P, P, C2, C2)
-        for r in range(PLANES):
-            scatter_z(back0[r], r, 0, early[r])
-        for r in range(PLANES):
-            scatter_z(back0[r], r, early[r], (T if r == 3 else C1) - early[r])
-        da0 = keep.tile([P, PLANES, C1], BF16, name="da0", tag="da0", align_bytes=64)
-        for r in range(PLANES):
-            times_slope(0, r, back0[r], da0)
-        woven0 = weave(0, da0)
-        z_late = keep.tile([P, C1], F32, name="z_late", tag="da0", align_bytes=64)
-        nc.scalar.copy(z_late[:], late_bank[:])
+        tokens = [keep.tile([P, T], F32, name=f"tokens{kb}", tag="back3" if kb == 2 else f"tokens{kb}") for kb in range(K // P)]
 
-        back1 = {3: back0[3]}
-        for r in (1, 2):
-            back1[r] = keep.tile([P, T], F32, name=f"back1_{r}")
-            scatter_z(back1[r], r, C1, C1)
-        accs0 = second_product(0, *quantise(0, woven0))
-        back1[0] = keep.tile([P, T], F32, name="back1_0")
-        nc.vector.tensor_copy(back1[0][:].indirect(entries(offs2_sb, C1, C1)), z_late[:])
-        da1 = keep.tile([P, PLANES, C1], BF16, name="da1", tag="da1", align_bytes=64)
-        for r in (3, 1, 2, 0):
-            times_slope(1, r, back1[r], da1)
-        woven1 = weave(1, da1)
-        late_dx = keep.tile([P, C1], F32, name="late_dx", tag="da1", align_bytes=64)
-        nc.scalar.copy(late_dx[:], accs0[2][:])
+        def empty(f, accs):
+            dx = [keep.tile([P, C1], F32, name=f"dx{f}_{kb}") for kb in range(K // P)]
+            for kb in range(K // P):
+                if kb == 0 or (f, kb) == (0, 2):
+                    nc.vector.tensor_copy(dx[kb][:], accs[kb][:])
+                else:
+                    nc.scalar.copy(dx[kb][:], accs[kb][:])
+            return dx
 
-        tokens = [keep.tile([P, T], F32, name=f"tokens{kb}") for kb in range(3)]
-        for kb in range(2):
-            scatter_dx(tokens[kb], 0, dx[0, kb])
-        second_product(1, *quantise(1, woven1))
-        scatter_dx(tokens[2], 0, late_dx[:])
-        for kb in range(3):
-            scatter_dx(tokens[kb], C1, dx[1, kb])
+        def dx_halves(f, dx):
+            for half in range(2):
+                for kb in (1, 3):
+                    on_scalar(tokens[kb], offs_sb, f * C1 + half * C2, dx[kb][:, half * C2 : (half + 1) * C2])
+
+        dx0 = empty(0, accs0)
+        on_vector(tokens[0], offs_sb, 0, dx0[0][:])
+        accs1 = second_product(1, woven1)
+        on_vector(tokens[2], offs_sb, 0, dx0[2][:])
+        dx_halves(0, dx0)
+        dx1 = empty(1, accs1)
+        for kb in (0, 2):
+            on_vector(tokens[kb], offs_sb, C1, dx1[kb][:])
+        dx_halves(1, dx1)
+        for kb in (0, 1, 3, 2):
             store(kb, tokens[kb])
-        tokens.append(keep.tile([P, WIDE], F32, name="tokens3"))
-        scatter_dx(tokens[3], 0, dx_both[:])
-        store(3, tokens[3])

@@ -20,6 +20,7 @@ MAX = mybir.AluOpType.max
 P = 128
 PER_COL = 16
 PLANES = 4
+LONG = 384
 
 
 def tile_moe_hib_relu2_kernel(tc, dy_words, dy_scales, wet_words, wet_scales, wgt_words, wgt_scales, a, gate, offs, offs2, dst, out):
@@ -76,27 +77,41 @@ def tile_moe_hib_relu2_kernel(tc, dy_words, dy_scales, wet_words, wet_scales, wg
         nc.sync.dma_start(offs_sb[:], offs)
 
         sorted_words, sorted_scales = {}, {}
-        for e in range(E):
-            words = keep.tile([P, PLANES, P], U16, name=f"sorted_words{e}", align_bytes=64)
-            nc.scalar.copy(
-                words[:].rearrange("p r (c i) -> p c r i", i=8),
-                wet_sb[e // 2][:, e % 2, :].bitcast(U16).rearrange("p (c i r) -> p c r i", i=8, r=PLANES),
-            )
+
+        def sort_words(e):
+            words = keep.tile([P, PLANES, 2 * P], U8, name=f"sorted_words{e}", align_bytes=64)
+            natural = wet_sb[e // 2][:, e % 2, :]
+            if e < 2:
+                nc.scalar.copy(words[:].bitcast(U16).rearrange("p r (c i) -> p c r i", i=8), natural.bitcast(U16).rearrange("p (c i r) -> p c r i", i=8, r=PLANES))
+            else:
+                nc.gpsimd.tensor_copy(words[:].rearrange("p r (c i b) -> p c r i b", i=8, b=2), natural.rearrange("p (c i r b) -> p c r i b", i=8, r=PLANES, b=2))
             for r in range(PLANES):
                 sorted_words[e, r] = words[:, r, :]
-        for e, first, count in ((0, 0, 2), (1, 0, 2), (0, 2, 2), (1, 2, 2), (2, 0, 4), (3, 0, 4)):
-            scales = keep.tile([P, count, P], U8, name=f"sorted_scales{e}_{first}", align_bytes=64)
+
+        def sort_scales(experts, planes):
+            count = planes.stop - planes.start
+            scales = keep.tile([P, experts.stop - experts.start, count, P], U8, name=f"sorted_scales{experts.start}_{planes.start}", tag=f"sorted_scales{experts.start}_{planes.start}", align_bytes=64)
             nc.gpsimd.tensor_copy(
-                scales[:].rearrange("p r (c i) -> p c r i", i=16),
-                wet_scale_sb[:, e, :].rearrange("p (c i r) -> p c r i", i=16, r=PLANES)[:, :, first : first + count, :],
+                scales[:].rearrange("p e r (c i) -> p e c r i", i=16),
+                wet_scale_sb[:, experts, :].rearrange("p e (c i r) -> p e c r i", i=16, r=PLANES)[:, :, :, planes, :],
             )
-            for r in range(count):
-                sorted_scales[e, first + r] = scales[:, r, :]
+            for e in range(experts.start, experts.stop):
+                for r in range(count):
+                    sorted_scales[e, planes.start + r] = scales[:, e - experts.start, r, :]
+
+        sort_words(0)
+        sort_words(1)
+        sort_scales(slice(0, 1), slice(0, 2))
+        sort_scales(slice(0, 1), slice(2, 4))
+        sort_scales(slice(1, 2), slice(0, 4))
+        sort_words(2)
+        sort_scales(slice(2, 4), slice(0, 4))
+        sort_words(3)
 
         z = {(f, pair): keep.tile([P, 2, C1], F32, name=f"z{f}_{pair}") for f in range(G) for pair in range(2)}
 
         def gather_scales(f):
-            scales = keep.tile([P, C1], U8, name=f"g_scale{f}", align_bytes=64)
+            scales = keep.tile([P, C1], U8, name=f"g_scale{f}", tag="sorted_scales0_0" if f else "g_scale0", align_bytes=64)
             nc.vector.tensor_copy(scales[:], dy_scale_sb[:].indirect(entries(dst_sb, f * C1, C1)))
             return scales
 
@@ -110,7 +125,7 @@ def tile_moe_hib_relu2_kernel(tc, dy_words, dy_scales, wet_words, wet_scales, wg
             for half in range(2):
                 nc.tensor.matmul_mx(
                     acc[:, half, :],
-                    lhsT=sorted_words[e, 2 * pair + half].bitcast(U8).bitcast(FP4X4),
+                    lhsT=sorted_words[e, 2 * pair + half].bitcast(FP4X4),
                     lhsT_scale=sorted_scales[e, 2 * pair + half],
                     rhs=words[:].bitcast(FP8X4),
                     rhs_scale=scales[:, e % 2 * C2 : (e % 2 + 1) * C2],
@@ -144,8 +159,8 @@ def tile_moe_hib_relu2_kernel(tc, dy_words, dy_scales, wet_words, wet_scales, wg
             words = keep.tile([P, C1], U32, name=f"da_words{f}", align_bytes=64)
             scales = keep.tile([P, C1], U8, name=f"da_scales{f}", align_bytes=64)
             nc.vector.quantize_mx(words[:].bitcast(FP8X4), scales[:], woven[:].rearrange("p j r -> p (j r)"))
-            accs = []
-            for kb in range(K // P):
+            accs = {}
+            for kb in (1, 3, 0, 2):
                 acc = psum.tile([P, C1], F32, name=f"acc2_{f}_{kb}", tag=f"bank{4 * f + kb}")
                 nc.tensor.matmul_mx(
                     acc[:],
@@ -156,7 +171,7 @@ def tile_moe_hib_relu2_kernel(tc, dy_words, dy_scales, wet_words, wet_scales, wg
                     start=True,
                     stop=True,
                 )
-                accs.append(acc)
+                accs[kb] = acc
             return accs
 
         def store(kb, window):
@@ -164,52 +179,60 @@ def tile_moe_hib_relu2_kernel(tc, dy_words, dy_scales, wet_words, wet_scales, wg
 
         g_scale = [gather_scales(0)]
         g_word = [gather_words(0), gather_words(1)]
-        g_scale.append(gather_scales(1))
-        for pair in range(2):
-            for e in range(2):
+        for e in range(2):
+            for pair in range(2):
                 first_product(e, pair, g_word[e], g_scale[0])
+        g_scale.append(gather_scales(1))
         g_word.extend(gather_words(e) for e in (2, 3))
         slope = [keep.tile([P, 2, T], F32, name=f"slope{pair}") for pair in range(2)]
         for pair in range(2):
             nc.vector.tensor_scalar(slope[pair][:], a_sb[pair][:], 2.0, 0.0, MULT, MAX)
-        for e, r in ((0, 0), (0, 1), (1, 0), (0, 3), (1, 1), (1, 3)):
-            z_half(e, r)
+        for e in range(2):
+            for r in (0, 1, 3):
+                z_half(e, r)
         first_product(2, 0, g_word[2], g_scale[1])
         z_whole(0, 2)
-        for e, pair in ((3, 0), (2, 1), (3, 1)):
+        for e, pair in ((2, 1), (3, 1), (3, 0)):
             first_product(e, pair, g_word[e], g_scale[1])
         woven0 = times_slope(0)
-        z_whole(1, 1)
+        z_whole(1, 2)
         accs0 = second_product(0, woven0)
         z_whole(1, 3)
-        for e, r in ((2, 0), (2, 2), (3, 0), (3, 2)):
-            z_half(e, r)
+        for r in range(2):
+            back[r] = keep.tile([P, T], F32, name=f"back_late{r}")
+        for e in (2, 3):
+            for r in range(2):
+                z_half(e, r)
         woven1 = times_slope(1)
 
         tokens = [keep.tile([P, T], F32, name=f"tokens{kb}", tag="back3" if kb == 2 else f"tokens{kb}") for kb in range(K // P)]
+        dx = {(f, kb): keep.tile([P, C1], F32, name=f"dx{f}_{kb}") for f in range(G) for kb in range(K // P)}
 
-        def empty(f, accs):
-            dx = [keep.tile([P, C1], F32, name=f"dx{f}_{kb}") for kb in range(K // P)]
-            for kb in range(K // P):
-                if kb == 0 or (f, kb) == (0, 2):
-                    nc.vector.tensor_copy(dx[kb][:], accs[kb][:])
-                else:
-                    nc.scalar.copy(dx[kb][:], accs[kb][:])
-            return dx
+        def put(engine, f, kb, first, last):
+            engine(tokens[kb], offs_sb, f * C1 + first, dx[f, kb][:, first:last])
 
-        def dx_halves(f, dx):
-            for half in range(2):
-                for kb in (1, 3):
-                    on_scalar(tokens[kb], offs_sb, f * C1 + half * C2, dx[kb][:, half * C2 : (half + 1) * C2])
-
-        dx0 = empty(0, accs0)
-        on_vector(tokens[0], offs_sb, 0, dx0[0][:])
-        accs1 = second_product(1, woven1)
-        on_vector(tokens[2], offs_sb, 0, dx0[2][:])
-        dx_halves(0, dx0)
-        dx1 = empty(1, accs1)
         for kb in (0, 2):
-            on_vector(tokens[kb], offs_sb, C1, dx1[kb][:])
-        dx_halves(1, dx1)
-        for kb in (0, 1, 3, 2):
+            nc.vector.tensor_copy(dx[0, kb][:], accs0[kb][:])
+        for kb in (1, 3):
+            nc.scalar.copy(dx[0, kb][:], accs0[kb][:])
+        put(on_vector, 0, 0, 0, LONG)
+        accs1 = second_product(1, woven1)
+        put(on_vector, 0, 2, 0, C1)
+        for first in (0, C2):
+            for kb in (1, 3):
+                put(on_scalar, 0, kb, first, first + C2)
+        put(on_scalar, 0, 0, LONG, C1)
+        for kb in (0, 2):
+            nc.vector.tensor_copy(dx[1, kb][:], accs1[kb][:])
+        for kb in (0, 2):
+            put(on_vector, 1, kb, 0, C1)
             store(kb, tokens[kb])
+        nc.scalar.copy(dx[1, 1][:], accs1[1][:])
+        nc.scalar.copy(dx[1, 3][:, 0:C2], accs1[3][:, 0:C2])
+        for kb in (1, 3):
+            put(on_scalar, 1, kb, 0, C2)
+        put(on_scalar, 1, 1, C2, C1)
+        nc.scalar.copy(dx[1, 3][:, C2:C1], accs1[3][:, C2:C1])
+        store(1, tokens[1])
+        put(on_scalar, 1, 3, C2, C1)
+        store(3, tokens[3])

@@ -47,7 +47,7 @@ def tile_moe_hib_relu2_kernel(tc, dy_words, dy_scales, wet_words, wet_scales, wg
 
         dy_scale_sb = keep.tile([P, T], U8, name="dy_scale_sb", align_bytes=64)
         dy_word_sb = keep.tile([P, T], I32, name="dy_word_sb", align_bytes=64)
-        wet_scale_sb = keep.tile([P, E, H], U8, name="wet_scale_sb", align_bytes=64)
+        wet_scale_sb = keep.tile([P, E, H], U8, name="wet_scale_sb", tag="wet_scale", align_bytes=64)
         wgt_scale_sb = keep.tile([P, G, K], U8, name="wgt_scale_sb", align_bytes=64)
         nc.vector.memset(wet_scale_sb[:].bitcast(I32), 0)
         nc.vector.memset(wgt_scale_sb[:].bitcast(I32), 0)
@@ -78,15 +78,14 @@ def tile_moe_hib_relu2_kernel(tc, dy_words, dy_scales, wet_words, wet_scales, wg
 
         sorted_words, sorted_scales = {}, {}
 
-        def sort_words(e):
-            words = keep.tile([P, PLANES, 2 * P], U8, name=f"sorted_words{e}", align_bytes=64)
-            natural = wet_sb[e // 2][:, e % 2, :]
-            if e < 2:
-                nc.scalar.copy(words[:].bitcast(U16).rearrange("p r (c i) -> p c r i", i=8), natural.bitcast(U16).rearrange("p (c i r) -> p c r i", i=8, r=PLANES))
-            else:
-                nc.gpsimd.tensor_copy(words[:].rearrange("p r (c i b) -> p c r i b", i=8, b=2), natural.rearrange("p (c i r b) -> p c r i b", i=8, r=PLANES, b=2))
-            for r in range(PLANES):
-                sorted_words[e, r] = words[:, r, :]
+        def sort_words(copy, experts, tag):
+            count = experts.stop - experts.start
+            words = keep.tile([P, count, PLANES, 2 * P], U8, name=f"sorted_words{experts.start}", tag=tag, align_bytes=64)
+            natural = wet_sb[experts.start // 2][:, experts.start % 2 : experts.start % 2 + count, :]
+            copy(words[:].bitcast(U16).rearrange("p e r (c i) -> p e c r i", i=8), natural.bitcast(U16).rearrange("p e (c i r) -> p e c r i", i=8, r=PLANES))
+            for e in range(count):
+                for r in range(PLANES):
+                    sorted_words[experts.start + e, r] = words[:, e, r, :]
 
         def sort_scales(experts, planes):
             count = planes.stop - planes.start
@@ -99,14 +98,12 @@ def tile_moe_hib_relu2_kernel(tc, dy_words, dy_scales, wet_words, wet_scales, wg
                 for r in range(count):
                     sorted_scales[e, planes.start + r] = scales[:, e - experts.start, r, :]
 
-        sort_words(0)
-        sort_words(1)
+        sort_words(nc.scalar.copy, slice(0, 1), "sorted_words0")
+        sort_words(nc.scalar.copy, slice(1, 2), "sorted_words1")
         sort_scales(slice(0, 1), slice(0, 2))
         sort_scales(slice(0, 1), slice(2, 4))
         sort_scales(slice(1, 2), slice(0, 4))
-        sort_words(2)
         sort_scales(slice(2, 4), slice(0, 4))
-        sort_words(3)
 
         z = {(f, pair): keep.tile([P, 2, C1], F32, name=f"z{f}_{pair}") for f in range(G) for pair in range(2)}
 
@@ -184,6 +181,7 @@ def tile_moe_hib_relu2_kernel(tc, dy_words, dy_scales, wet_words, wet_scales, wg
                 first_product(e, pair, g_word[e], g_scale[0])
         g_scale.append(gather_scales(1))
         g_word.extend(gather_words(e) for e in (2, 3))
+        sort_words(nc.vector.tensor_copy, slice(2, 4), "wet_scale")
         slope = [keep.tile([P, 2, T], F32, name=f"slope{pair}") for pair in range(2)]
         for pair in range(2):
             nc.vector.tensor_scalar(slope[pair][:], a_sb[pair][:], 2.0, 0.0, MULT, MAX)
@@ -195,7 +193,7 @@ def tile_moe_hib_relu2_kernel(tc, dy_words, dy_scales, wet_words, wet_scales, wg
         for e, pair in ((2, 1), (3, 1), (3, 0)):
             first_product(e, pair, g_word[e], g_scale[1])
         woven0 = times_slope(0)
-        z_whole(1, 2)
+        on_vector(back[2], offs2_sb, C1, z[1, 1][:, 0, 0:LONG])
         accs0 = second_product(0, woven0)
         z_whole(1, 3)
         for r in range(2):
@@ -203,6 +201,7 @@ def tile_moe_hib_relu2_kernel(tc, dy_words, dy_scales, wet_words, wet_scales, wg
         for e in (2, 3):
             for r in range(2):
                 z_half(e, r)
+        on_scalar(back[2], offs2_sb, C1 + LONG, z[1, 1][:, 0, LONG:C1])
         woven1 = times_slope(1)
 
         tokens = [keep.tile([P, T], F32, name=f"tokens{kb}", tag="back3" if kb == 2 else f"tokens{kb}") for kb in range(K // P)]
@@ -224,13 +223,13 @@ def tile_moe_hib_relu2_kernel(tc, dy_words, dy_scales, wet_words, wet_scales, wg
         put(on_scalar, 0, 0, LONG, C1)
         for kb in (0, 2):
             nc.vector.tensor_copy(dx[1, kb][:], accs1[kb][:])
-        for kb in (0, 2):
-            put(on_vector, 1, kb, 0, C1)
-            store(kb, tokens[kb])
         nc.scalar.copy(dx[1, 1][:], accs1[1][:])
         nc.scalar.copy(dx[1, 3][:, 0:C2], accs1[3][:, 0:C2])
         for kb in (1, 3):
             put(on_scalar, 1, kb, 0, C2)
+        for kb in (0, 2):
+            put(on_vector, 1, kb, 0, C1)
+            store(kb, tokens[kb])
         put(on_scalar, 1, 1, C2, C1)
         nc.scalar.copy(dx[1, 3][:, C2:C1], accs1[3][:, C2:C1])
         store(1, tokens[1])

@@ -47,9 +47,10 @@ def tile_moe_hib_relu2_kernel(tc, dy_words, dy_scales, wet_words, wet_scales, wg
 
         dy_scale_sb = keep.tile([P, T], U8, name="dy_scale_sb", align_bytes=64)
         dy_word_sb = keep.tile([P, T], I32, name="dy_word_sb", align_bytes=64)
-        wet_scale_sb = keep.tile([P, E, H], U8, name="wet_scale_sb", tag="wet_scale", align_bytes=64)
+        first_scale_sb = keep.tile([P, 1, H], U8, name="first_scale_sb", align_bytes=64)
+        rest_scale_sb = keep.tile([P, E - 1, H], U8, name="rest_scale_sb", tag="wet_scale", align_bytes=64)
         wgt_scale_sb = keep.tile([P, G, K], U8, name="wgt_scale_sb", align_bytes=64)
-        nc.vector.memset(wet_scale_sb[:].bitcast(I32), 0)
+        nc.vector.memset(rest_scale_sb[:].bitcast(I32), 0)
         nc.vector.memset(wgt_scale_sb[:].bitcast(I32), 0)
 
         wet_view = wet_words.rearrange("e s p c -> p (e s) c")
@@ -65,9 +66,12 @@ def tile_moe_hib_relu2_kernel(tc, dy_words, dy_scales, wet_words, wet_scales, wg
             (nc.sync if quad < 2 else nc.scalar).dma_start(dy_scale_sb[32 * quad : 32 * quad + 32, :].bitcast(I32), rows.unsqueeze(0).to_broadcast([8, 4, T // 4]))
         nc.sync.dma_start(dy_word_sb[:], dy_words[0].rearrange("p t d -> p (t d)").bitcast(I32))
         nc.sync.dma_start(wet_sb[0][:].bitcast(I32), wet_view[:, 0:2, :].bitcast(I32))
-        load_scale_rows(wet_scale_sb, wet_scales.rearrange("e s b c -> (e s) b c"))
+        for quad in range(4):
+            rows = wet_scales[0, 0, 4 * quad : 4 * quad + 4, :].bitcast(I32)
+            nc.sync.dma_start(first_scale_sb[32 * quad : 32 * quad + 32, 0, :].bitcast(I32), rows.unsqueeze(0).to_broadcast([8, 4, H // 4]))
         nc.sync.dma_start(gate_sb[0][:], gate[:, 0:C1])
         nc.sync.dma_start(offs2_sb[:], offs2)
+        load_scale_rows(rest_scale_sb, wet_scales.rearrange("e s b c -> (e s) b c")[1:E])
         nc.sync.dma_start(wet_sb[1][:].bitcast(I32), wet_view[:, 2:E, :].bitcast(I32))
         for pair in range(2):
             nc.sync.dma_start(a_sb[pair][:], a_view[:, 2 * pair : 2 * pair + 2, :])
@@ -89,10 +93,11 @@ def tile_moe_hib_relu2_kernel(tc, dy_words, dy_scales, wet_words, wet_scales, wg
 
         def sort_scales(experts, planes):
             count = planes.stop - planes.start
+            natural = rest_scale_sb[:, experts.start - 1 : experts.stop - 1, :] if experts.start else first_scale_sb[:]
             scales = keep.tile([P, experts.stop - experts.start, count, P], U8, name=f"sorted_scales{experts.start}_{planes.start}", tag=f"sorted_scales{experts.start}_{planes.start}", align_bytes=64)
             nc.gpsimd.tensor_copy(
                 scales[:].rearrange("p e r (c i) -> p e c r i", i=16),
-                wet_scale_sb[:, experts, :].rearrange("p e (c i r) -> p e c r i", i=16, r=PLANES)[:, :, :, planes, :],
+                natural.rearrange("p e (c i r) -> p e c r i", i=16, r=PLANES)[:, :, :, planes, :],
             )
             for e in range(experts.start, experts.stop):
                 for r in range(count):

@@ -20,7 +20,8 @@ MAX = mybir.AluOpType.max
 P = 128
 PER_COL = 16
 PLANES = 4
-LONG = 384
+LONG = 320
+EARLY = 448
 
 
 def tile_moe_hib_relu2_kernel(tc, dy_words, dy_scales, wet_words, wet_scales, wgt_words, wgt_scales, a, gate, offs, offs2, dst, out):
@@ -54,7 +55,9 @@ def tile_moe_hib_relu2_kernel(tc, dy_words, dy_scales, wet_words, wet_scales, wg
         nc.vector.memset(wgt_scale_sb[:].bitcast(I32), 0)
 
         wet_view = wet_words.rearrange("e s p c -> p (e s) c")
-        wet_sb = [keep.tile([P, 2, 2 * H], U8, name=f"wet_sb{f}", align_bytes=64) for f in range(G)]
+        first_wet_sb = keep.tile([P, 1, 2 * H], U8, name="first_wet_sb", tag="first_wet", align_bytes=64)
+        second_wet_sb = keep.tile([P, 1, 2 * H], U8, name="second_wet_sb", align_bytes=64)
+        rest_wet_sb = keep.tile([P, 2, 2 * H], U8, name="rest_wet_sb", align_bytes=64)
         gate_sb = [keep.tile([P, C1], F32, name=f"gate_sb{f}") for f in range(G)]
         a_view = a.rearrange("(q r) j -> q r j", r=PLANES)
         a_sb = [keep.tile([P, 2, T], F32, name="a_sb0"), reuse.tile([P, 2, T], F32, name="a_sb1", offset=0, align_bytes=64)]
@@ -65,14 +68,15 @@ def tile_moe_hib_relu2_kernel(tc, dy_words, dy_scales, wet_words, wet_scales, wg
             rows = dy_scales[0, 4 * quad : 4 * quad + 4, :].bitcast(I32)
             (nc.sync if quad < 2 else nc.scalar).dma_start(dy_scale_sb[32 * quad : 32 * quad + 32, :].bitcast(I32), rows.unsqueeze(0).to_broadcast([8, 4, T // 4]))
         nc.sync.dma_start(dy_word_sb[:], dy_words[0].rearrange("p t d -> p (t d)").bitcast(I32))
-        nc.sync.dma_start(wet_sb[0][:].bitcast(I32), wet_view[:, 0:2, :].bitcast(I32))
+        nc.sync.dma_start(first_wet_sb[:].bitcast(I32), wet_view[:, 0:1, :].bitcast(I32))
+        nc.sync.dma_start(second_wet_sb[:].bitcast(I32), wet_view[:, 1:2, :].bitcast(I32))
         for quad in range(4):
             rows = wet_scales[0, 0, 4 * quad : 4 * quad + 4, :].bitcast(I32)
             nc.sync.dma_start(first_scale_sb[32 * quad : 32 * quad + 32, 0, :].bitcast(I32), rows.unsqueeze(0).to_broadcast([8, 4, H // 4]))
         nc.sync.dma_start(gate_sb[0][:], gate[:, 0:C1])
         nc.sync.dma_start(offs2_sb[:], offs2)
         load_scale_rows(rest_scale_sb, wet_scales.rearrange("e s b c -> (e s) b c")[1:E])
-        nc.sync.dma_start(wet_sb[1][:].bitcast(I32), wet_view[:, 2:E, :].bitcast(I32))
+        nc.sync.dma_start(rest_wet_sb[:].bitcast(I32), wet_view[:, 2:E, :].bitcast(I32))
         for pair in range(2):
             nc.sync.dma_start(a_sb[pair][:], a_view[:, 2 * pair : 2 * pair + 2, :])
         nc.sync.dma_start(gate_sb[1][:], gate[:, C1:T])
@@ -85,7 +89,7 @@ def tile_moe_hib_relu2_kernel(tc, dy_words, dy_scales, wet_words, wet_scales, wg
         def sort_words(copy, experts, tag):
             count = experts.stop - experts.start
             words = keep.tile([P, count, PLANES, 2 * P], U8, name=f"sorted_words{experts.start}", tag=tag, align_bytes=64)
-            natural = wet_sb[experts.start // 2][:, experts.start % 2 : experts.start % 2 + count, :]
+            natural = (first_wet_sb, second_wet_sb, rest_wet_sb)[experts.start][:]
             copy(words[:].bitcast(U16).rearrange("p e r (c i) -> p e c r i", i=8), natural.bitcast(U16).rearrange("p e (c i r) -> p e c r i", i=8, r=PLANES))
             for e in range(count):
                 for r in range(PLANES):
@@ -105,37 +109,39 @@ def tile_moe_hib_relu2_kernel(tc, dy_words, dy_scales, wet_words, wet_scales, wg
 
         sort_words(nc.scalar.copy, slice(0, 1), "sorted_words0")
         sort_words(nc.scalar.copy, slice(1, 2), "sorted_words1")
-        sort_scales(slice(0, 1), slice(0, 2))
-        sort_scales(slice(0, 1), slice(2, 4))
+        sort_scales(slice(0, 1), slice(0, 1))
+        sort_scales(slice(0, 1), slice(1, 4))
         sort_scales(slice(1, 2), slice(0, 4))
         sort_scales(slice(2, 4), slice(0, 4))
 
         z = {(f, pair): keep.tile([P, 2, C1], F32, name=f"z{f}_{pair}") for f in range(G) for pair in range(2)}
 
-        def gather_scales(f):
-            scales = keep.tile([P, C1], U8, name=f"g_scale{f}", tag="sorted_scales0_0" if f else "g_scale0", align_bytes=64)
-            nc.vector.tensor_copy(scales[:], dy_scale_sb[:].indirect(entries(dst_sb, f * C1, C1)))
-            return scales
+        def gather_scales(e, count, tag):
+            scales = keep.tile([P, count, C2], U8, name=f"g_scale{e}", tag=tag, align_bytes=64)
+            nc.vector.tensor_copy(scales[:].rearrange("p e c -> p (e c)"), dy_scale_sb[:].indirect(entries(dst_sb, e * C2, count * C2)))
+            return [scales[:, at, :] for at in range(count)]
 
         def gather_words(e):
             words = keep.tile([P, C2], U32, name=f"g_word{e}", tag=f"g_word{e % 2}", align_bytes=64)
             nc.vector.tensor_copy(words[:], dy_word_sb[:].bitcast(U32).indirect(entries(dst_sb, e * C2, C2)))
             return words
 
-        def first_product(e, pair, words, scales):
-            acc = psum.tile([P, 2, C2], F32, name=f"acc1_{e}_{pair}", tag=f"bank{2 * e + pair}")
-            for half in range(2):
+        def first_product(e, planes, bank):
+            words, scales = g_word[e], g_scale[e]
+            acc = psum.tile([P, len(planes), C2], F32, name=f"acc1_{e}_{planes[0]}", tag=f"bank{bank}")
+            for at, r in enumerate(planes):
                 nc.tensor.matmul_mx(
-                    acc[:, half, :],
-                    lhsT=sorted_words[e, 2 * pair + half].bitcast(FP4X4),
-                    lhsT_scale=sorted_scales[e, 2 * pair + half],
+                    acc[:, at, :],
+                    lhsT=sorted_words[e, r].bitcast(FP4X4),
+                    lhsT_scale=sorted_scales[e, r],
                     rhs=words[:].bitcast(FP8X4),
-                    rhs_scale=scales[:, e % 2 * C2 : (e % 2 + 1) * C2],
+                    rhs_scale=scales,
                     start=True,
                     stop=True,
                 )
             cols = slice(e % 2 * C2, (e % 2 + 1) * C2)
-            nc.vector.tensor_tensor(z[e // 2, pair][:, :, cols], acc[:], gate_sb[e // 2][:, cols].unsqueeze(1).to_broadcast([P, 2, C2]), MULT)
+            rows = slice(planes[0] % 2, planes[-1] % 2 + 1)
+            nc.vector.tensor_tensor(z[e // 2, planes[0] // 2][:, rows, cols], acc[:], gate_sb[e // 2][:, cols].unsqueeze(1).to_broadcast([P, len(planes), C2]), MULT)
 
         def on_vector(window, offsets, first, values):
             nc.vector.tensor_copy(window[:].indirect(entries(offsets, first, values.shape[1])), values)
@@ -179,12 +185,12 @@ def tile_moe_hib_relu2_kernel(tc, dy_words, dy_scales, wet_words, wet_scales, wg
         def store(kb, window):
             (nc.scalar if kb % 2 else nc.sync).dma_start(out[kb * P : (kb + 1) * P, :], window[:])
 
-        g_scale = [gather_scales(0)]
+        g_scale = gather_scales(0, 2, "g_scale0")
         g_word = [gather_words(0), gather_words(1)]
-        for e in range(2):
-            for pair in range(2):
-                first_product(e, pair, g_word[e], g_scale[0])
-        g_scale.append(gather_scales(1))
+        g_scale.extend(gather_scales(2, 1, "first_wet"))
+        for e, planes, bank in ((0, (0,), 7), (0, (1,), 0), (0, (2, 3), 1), (1, (0, 1), 2), (1, (2, 3), 3)):
+            first_product(e, planes, bank)
+        g_scale.extend(gather_scales(3, 1, "sorted_scales0_0"))
         g_word.extend(gather_words(e) for e in (2, 3))
         sort_words(nc.vector.tensor_copy, slice(2, 4), "wet_scale")
         slope = [keep.tile([P, 2, T], F32, name=f"slope{pair}") for pair in range(2)]
@@ -193,10 +199,10 @@ def tile_moe_hib_relu2_kernel(tc, dy_words, dy_scales, wet_words, wet_scales, wg
         for e in range(2):
             for r in (0, 1, 3):
                 z_half(e, r)
-        first_product(2, 0, g_word[2], g_scale[1])
+        first_product(2, (0, 1), 4)
         z_whole(0, 2)
         for e, pair in ((2, 1), (3, 1), (3, 0)):
-            first_product(e, pair, g_word[e], g_scale[1])
+            first_product(e, (2 * pair, 2 * pair + 1), 2 * e + pair)
         woven0 = times_slope(0)
         on_vector(back[2], offs2_sb, C1, z[1, 1][:, 0, 0:LONG])
         accs0 = second_product(0, woven0)
@@ -210,31 +216,32 @@ def tile_moe_hib_relu2_kernel(tc, dy_words, dy_scales, wet_words, wet_scales, wg
         woven1 = times_slope(1)
 
         tokens = [keep.tile([P, T], F32, name=f"tokens{kb}", tag="back3" if kb == 2 else f"tokens{kb}") for kb in range(K // P)]
-        dx = {(f, kb): keep.tile([P, C1], F32, name=f"dx{f}_{kb}") for f in range(G) for kb in range(K // P)}
+        dx_rows = [keep.tile([P, T], F32, name=f"dx{kb}") for kb in range(K // P)]
+        dx = {(f, kb): dx_rows[kb][:, f * C1 : (f + 1) * C1] for f in range(G) for kb in range(K // P)}
 
         def put(engine, f, kb, first, last):
-            engine(tokens[kb], offs_sb, f * C1 + first, dx[f, kb][:, first:last])
+            engine(tokens[kb], offs_sb, f * C1 + first, dx_rows[kb][:, f * C1 + first : f * C1 + last])
 
         for kb in (0, 2):
-            nc.vector.tensor_copy(dx[0, kb][:], accs0[kb][:])
+            nc.vector.tensor_copy(dx[0, kb], accs0[kb][:])
         for kb in (1, 3):
-            nc.scalar.copy(dx[0, kb][:], accs0[kb][:])
-        put(on_vector, 0, 0, 0, LONG)
+            nc.scalar.copy(dx[0, kb], accs0[kb][:])
+        put(on_vector, 0, 0, 0, EARLY)
         accs1 = second_product(1, woven1)
         put(on_vector, 0, 2, 0, C1)
         for first in (0, C2):
             for kb in (1, 3):
                 put(on_scalar, 0, kb, first, first + C2)
-        put(on_scalar, 0, 0, LONG, C1)
         for kb in (0, 2):
-            nc.vector.tensor_copy(dx[1, kb][:], accs1[kb][:])
-        nc.scalar.copy(dx[1, 1][:], accs1[1][:])
+            nc.vector.tensor_copy(dx[1, kb], accs1[kb][:])
+        nc.scalar.copy(dx[1, 1], accs1[1][:])
         nc.scalar.copy(dx[1, 3][:, 0:C2], accs1[3][:, 0:C2])
         for kb in (1, 3):
             put(on_scalar, 1, kb, 0, C2)
-        for kb in (0, 2):
-            put(on_vector, 1, kb, 0, C1)
-            store(kb, tokens[kb])
+        put(on_vector, 0, 0, EARLY, T)
+        store(0, tokens[0])
+        put(on_vector, 1, 2, 0, C1)
+        store(2, tokens[2])
         put(on_scalar, 1, 1, C2, C1)
         nc.scalar.copy(dx[1, 3][:, C2:C1], accs1[3][:, C2:C1])
         store(1, tokens[1])

@@ -20,8 +20,7 @@ MAX = mybir.AluOpType.max
 P = 128
 PER_COL = 16
 PLANES = 4
-LONG = 320
-EARLY = 448
+LONG = 384
 
 
 def tile_moe_hib_relu2_kernel(tc, dy_words, dy_scales, wet_words, wet_scales, wgt_words, wgt_scales, a, gate, offs, offs2, dst, out):
@@ -204,6 +203,7 @@ def tile_moe_hib_relu2_kernel(tc, dy_words, dy_scales, wet_words, wet_scales, wg
         for e, pair in ((2, 1), (3, 1), (3, 0)):
             first_product(e, (2 * pair, 2 * pair + 1), 2 * e + pair)
         woven0 = times_slope(0)
+        back[2] = keep.tile([P, T], F32, name="back_late2")
         on_vector(back[2], offs2_sb, C1, z[1, 1][:, 0, 0:LONG])
         accs0 = second_product(0, woven0)
         z_whole(1, 3)
@@ -226,7 +226,7 @@ def tile_moe_hib_relu2_kernel(tc, dy_words, dy_scales, wet_words, wet_scales, wg
             nc.vector.tensor_copy(dx[0, kb], accs0[kb][:])
         for kb in (1, 3):
             nc.scalar.copy(dx[0, kb], accs0[kb][:])
-        put(on_vector, 0, 0, 0, EARLY)
+        put(on_vector, 0, 0, 0, C1)
         accs1 = second_product(1, woven1)
         put(on_vector, 0, 2, 0, C1)
         for first in (0, C2):
@@ -238,7 +238,7 @@ def tile_moe_hib_relu2_kernel(tc, dy_words, dy_scales, wet_words, wet_scales, wg
         nc.scalar.copy(dx[1, 3][:, 0:C2], accs1[3][:, 0:C2])
         for kb in (1, 3):
             put(on_scalar, 1, kb, 0, C2)
-        put(on_vector, 0, 0, EARLY, T)
+        put(on_vector, 1, 0, 0, C1)
         store(0, tokens[0])
         put(on_vector, 1, 2, 0, C1)
         store(2, tokens[2])

@@ -20,7 +20,6 @@ MAX = mybir.AluOpType.max
 P = 128
 PER_COL = 16
 PLANES = 4
-LONG = 384
 
 
 def tile_moe_hib_relu2_kernel(tc, dy_words, dy_scales, wet_words, wet_scales, wgt_words, wgt_scales, a, gate, offs, offs2, dst, out):
@@ -50,8 +49,8 @@ def tile_moe_hib_relu2_kernel(tc, dy_words, dy_scales, wet_words, wet_scales, wg
         first_scale_sb = keep.tile([P, 1, H], U8, name="first_scale_sb", align_bytes=64)
         rest_scale_sb = keep.tile([P, E - 1, H], U8, name="rest_scale_sb", tag="wet_scale", align_bytes=64)
         wgt_scale_sb = keep.tile([P, G, K], U8, name="wgt_scale_sb", align_bytes=64)
-        nc.vector.memset(rest_scale_sb[:].bitcast(I32), 0)
-        nc.vector.memset(wgt_scale_sb[:].bitcast(I32), 0)
+        nc.gpsimd.memset(rest_scale_sb[:].bitcast(I32), 0)
+        nc.gpsimd.memset(wgt_scale_sb[:].bitcast(I32), 0)
 
         wet_view = wet_words.rearrange("e s p c -> p (e s) c")
         first_wet_sb = keep.tile([P, 1, 2 * H], U8, name="first_wet_sb", tag="first_wet", align_bytes=64)
@@ -120,21 +119,20 @@ def tile_moe_hib_relu2_kernel(tc, dy_words, dy_scales, wet_words, wet_scales, wg
             nc.vector.tensor_copy(scales[:].rearrange("p e c -> p (e c)"), dy_scale_sb[:].indirect(entries(dst_sb, e * C2, count * C2)))
             return [scales[:, at, :] for at in range(count)]
 
-        def gather_words(e):
-            words = keep.tile([P, C2], U32, name=f"g_word{e}", tag=f"g_word{e % 2}", align_bytes=64)
-            nc.vector.tensor_copy(words[:], dy_word_sb[:].bitcast(U32).indirect(entries(dst_sb, e * C2, C2)))
-            return words
+        def gather_words(e, count, tag):
+            words = keep.tile([P, count, C2], U32, name=f"g_word{e}", tag=tag, align_bytes=64)
+            nc.vector.tensor_copy(words[:].rearrange("p e c -> p (e c)"), dy_word_sb[:].bitcast(U32).indirect(entries(dst_sb, e * C2, count * C2)))
+            return [words[:, at, :] for at in range(count)]
 
         def first_product(e, planes, bank):
-            words, scales = g_word[e], g_scale[e]
             acc = psum.tile([P, len(planes), C2], F32, name=f"acc1_{e}_{planes[0]}", tag=f"bank{bank}")
             for at, r in enumerate(planes):
                 nc.tensor.matmul_mx(
                     acc[:, at, :],
                     lhsT=sorted_words[e, r].bitcast(FP4X4),
                     lhsT_scale=sorted_scales[e, r],
-                    rhs=words[:].bitcast(FP8X4),
-                    rhs_scale=scales,
+                    rhs=g_word[e].bitcast(FP8X4),
+                    rhs_scale=g_scale[e],
                     start=True,
                     stop=True,
                 )
@@ -185,12 +183,14 @@ def tile_moe_hib_relu2_kernel(tc, dy_words, dy_scales, wet_words, wet_scales, wg
             (nc.scalar if kb % 2 else nc.sync).dma_start(out[kb * P : (kb + 1) * P, :], window[:])
 
         g_scale = gather_scales(0, 2, "g_scale0")
-        g_word = [gather_words(0), gather_words(1)]
+        g_word = gather_words(0, 1, "g_word0") + gather_words(1, 1, "g_word1")
         g_scale.extend(gather_scales(2, 1, "first_wet"))
-        for e, planes, bank in ((0, (0,), 7), (0, (1,), 0), (0, (2, 3), 1), (1, (0, 1), 2), (1, (2, 3), 3)):
-            first_product(e, planes, bank)
+        for planes, bank in (((0,), 7), ((1,), 0), ((2, 3), 1)):
+            first_product(0, planes, bank)
         g_scale.extend(gather_scales(3, 1, "sorted_scales0_0"))
-        g_word.extend(gather_words(e) for e in (2, 3))
+        g_word.extend(gather_words(2, 2, "g_word0"))
+        for pair in range(2):
+            first_product(1, (2 * pair, 2 * pair + 1), 2 + pair)
         sort_words(nc.vector.tensor_copy, slice(2, 4), "wet_scale")
         slope = [keep.tile([P, 2, T], F32, name=f"slope{pair}") for pair in range(2)]
         for pair in range(2):
@@ -204,7 +204,7 @@ def tile_moe_hib_relu2_kernel(tc, dy_words, dy_scales, wet_words, wet_scales, wg
             first_product(e, (2 * pair, 2 * pair + 1), 2 * e + pair)
         woven0 = times_slope(0)
         back[2] = keep.tile([P, T], F32, name="back_late2")
-        on_vector(back[2], offs2_sb, C1, z[1, 1][:, 0, 0:LONG])
+        z_whole(1, 2)
         accs0 = second_product(0, woven0)
         z_whole(1, 3)
         for r in range(2):
@@ -212,7 +212,6 @@ def tile_moe_hib_relu2_kernel(tc, dy_words, dy_scales, wet_words, wet_scales, wg
         for e in (2, 3):
             for r in range(2):
                 z_half(e, r)
-        on_scalar(back[2], offs2_sb, C1 + LONG, z[1, 1][:, 0, LONG:C1])
         woven1 = times_slope(1)
 
         tokens = [keep.tile([P, T], F32, name=f"tokens{kb}", tag="back3" if kb == 2 else f"tokens{kb}") for kb in range(K // P)]

@@ -26,8 +26,10 @@ def tile_moe_hib_relu2_kernel(tc, dy_words, dy_scales, wet_words, wet_scales, wg
     nc = tc.nc
     with ExitStack() as ctx:
         lists = ctx.enter_context(tc.tile_pool(name="lists", bufs=1))
-        keep = ctx.enter_context(tc.tile_pool(name="keep", bufs=1))
         reuse = ctx.enter_context(tc.tile_pool(name="reuse", bufs=1))
+        low = ctx.enter_context(tc.tile_pool(name="low", bufs=1))
+        keep = ctx.enter_context(tc.tile_pool(name="keep", bufs=1))
+        high = ctx.enter_context(tc.tile_pool(name="high", bufs=1))
         psum = ctx.enter_context(tc.psum_pool(name="psum", bufs=1))
 
         def entries(tile, first, count):
@@ -146,7 +148,7 @@ def tile_moe_hib_relu2_kernel(tc, dy_words, dy_scales, wet_words, wet_scales, wg
         def on_scalar(window, offsets, first, values):
             nc.scalar.activation(window[:].indirect(entries(offsets, first, values.shape[1])), values, COPY)
 
-        back = [keep.tile([P, T], F32, name=f"back{r}", tag=f"back{r}") if r != 2 else reuse.tile([P, T], F32, name="back2", offset=0, align_bytes=64) for r in range(PLANES)]
+        back = [(low if r == 3 else high).tile([P, T], F32, name=f"back{r}", tag=f"back{r}") if r != 2 else reuse.tile([P, T], F32, name="back2", offset=0, align_bytes=64) for r in range(PLANES)]
 
         def z_half(e, r):
             on_scalar(back[r], offs2_sb, e * C2, z[e // 2, r // 2][:, r % 2, e % 2 * C2 : (e % 2 + 1) * C2])
@@ -203,18 +205,18 @@ def tile_moe_hib_relu2_kernel(tc, dy_words, dy_scales, wet_words, wet_scales, wg
         for e, pair in ((2, 1), (3, 1), (3, 0)):
             first_product(e, (2 * pair, 2 * pair + 1), 2 * e + pair)
         woven0 = times_slope(0)
-        back[2] = keep.tile([P, T], F32, name="back_late2")
+        back[2] = low.tile([P, T], F32, name="back_late2")
         z_whole(1, 2)
         accs0 = second_product(0, woven0)
         z_whole(1, 3)
         for r in range(2):
-            back[r] = keep.tile([P, T], F32, name=f"back_late{r}")
+            back[r] = high.tile([P, T], F32, name=f"back_late{r}")
         for e in (2, 3):
             for r in range(2):
                 z_half(e, r)
         woven1 = times_slope(1)
 
-        tokens = [keep.tile([P, T], F32, name=f"tokens{kb}", tag="back3" if kb == 2 else f"tokens{kb}") for kb in range(K // P)]
+        tokens = [(high if kb % 2 else low).tile([P, T], F32, name=f"tokens{kb}", tag="back3" if kb == 2 else f"tokens{kb}") for kb in range(K // P)]
         dx_rows = [keep.tile([P, T], F32, name=f"dx{kb}") for kb in range(K // P)]
         dx = {(f, kb): dx_rows[kb][:, f * C1 : (f + 1) * C1] for f in range(G) for kb in range(K // P)}
 

@@ -56,7 +56,7 @@ def tile_moe_hib_relu2_kernel(tc, dy_words, dy_scales, wet_words, wet_scales, wg
 
         wet_view = wet_words.rearrange("e s p c -> p (e s) c")
         first_wet_sb = keep.tile([P, 1, 2 * H], U8, name="first_wet_sb", tag="first_wet", align_bytes=64)
-        second_wet_sb = keep.tile([P, 1, 2 * H], U8, name="second_wet_sb", align_bytes=64)
+        second_wet_sb = high.tile([P, 1, 2 * H], U8, name="second_wet_sb", tag="back0", align_bytes=64)
         rest_wet_sb = keep.tile([P, 2, 2 * H], U8, name="rest_wet_sb", align_bytes=64)
         gate_sb = [keep.tile([P, C1], F32, name=f"gate_sb{f}") for f in range(G)]
         a_view = a.rearrange("(q r) j -> q r j", r=PLANES)
@@ -69,11 +69,11 @@ def tile_moe_hib_relu2_kernel(tc, dy_words, dy_scales, wet_words, wet_scales, wg
             (nc.sync if quad < 2 else nc.scalar).dma_start(dy_scale_sb[32 * quad : 32 * quad + 32, :].bitcast(I32), rows.unsqueeze(0).to_broadcast([8, 4, T // 4]))
         nc.sync.dma_start(dy_word_sb[:], dy_words[0].rearrange("p t d -> p (t d)").bitcast(I32))
         nc.sync.dma_start(first_wet_sb[:].bitcast(I32), wet_view[:, 0:1, :].bitcast(I32))
-        nc.sync.dma_start(second_wet_sb[:].bitcast(I32), wet_view[:, 1:2, :].bitcast(I32))
         for quad in range(4):
             rows = wet_scales[0, 0, 4 * quad : 4 * quad + 4, :].bitcast(I32)
             nc.sync.dma_start(first_scale_sb[32 * quad : 32 * quad + 32, 0, :].bitcast(I32), rows.unsqueeze(0).to_broadcast([8, 4, H // 4]))
         nc.sync.dma_start(gate_sb[0][:], gate[:, 0:C1])
+        nc.sync.dma_start(second_wet_sb[:].bitcast(I32), wet_view[:, 1:2, :].bitcast(I32))
         nc.sync.dma_start(offs2_sb[:], offs2)
         load_scale_rows(rest_scale_sb, wet_scales.rearrange("e s b c -> (e s) b c")[1:E])
         nc.sync.dma_start(rest_wet_sb[:].bitcast(I32), wet_view[:, 2:E, :].bitcast(I32))
@@ -148,7 +148,7 @@ def tile_moe_hib_relu2_kernel(tc, dy_words, dy_scales, wet_words, wet_scales, wg
         def on_scalar(window, offsets, first, values):
             nc.scalar.activation(window[:].indirect(entries(offsets, first, values.shape[1])), values, COPY)
 
-        back = [(low if r == 3 else high).tile([P, T], F32, name=f"back{r}", tag=f"back{r}") if r != 2 else reuse.tile([P, T], F32, name="back2", offset=0, align_bytes=64) for r in range(PLANES)]
+        back = [(low if r == 3 else high).tile([P, T], F32, name=f"back{r}", tag=f"back{r}", align_bytes=64) if r != 2 else reuse.tile([P, T], F32, name="back2", offset=0, align_bytes=64) for r in range(PLANES)]
 
         def z_half(e, r):
             on_scalar(back[r], offs2_sb, e * C2, z[e // 2, r // 2][:, r % 2, e % 2 * C2 : (e % 2 + 1) * C2])
@@ -216,7 +216,7 @@ def tile_moe_hib_relu2_kernel(tc, dy_words, dy_scales, wet_words, wet_scales, wg
                 z_half(e, r)
         woven1 = times_slope(1)
 
-        tokens = [(high if kb % 2 else low).tile([P, T], F32, name=f"tokens{kb}", tag="back3" if kb == 2 else f"tokens{kb}") for kb in range(K // P)]
+        tokens = [(high if kb % 2 else low).tile([P, T], F32, name=f"tokens{kb}", tag="back3" if kb == 2 else f"tokens{kb}", align_bytes=64) for kb in range(K // P)]
         dx_rows = [keep.tile([P, T], F32, name=f"dx{kb}") for kb in range(K // P)]
         dx = {(f, kb): dx_rows[kb][:, f * C1 : (f + 1) * C1] for f in range(G) for kb in range(K // P)}
 

@@ -156,9 +156,9 @@ def tile_moe_hib_relu2_kernel(tc, dy_words, dy_scales, wet_words, wet_scales, wg
         def z_whole(f, r):
             on_vector(back[r], offs2_sb, f * C1, z[f, r // 2][:, r % 2, :])
 
-        def times_slope(f):
+        def times_slope(f, order):
             woven = reuse.tile([P, C1, PLANES], BF16, name=f"woven{f}", offset=4 * T, align_bytes=64)
-            for r in range(PLANES):
+            for r in order:
                 nc.gpsimd.tensor_tensor(woven[:, :, r], back[r][:, f * C1 : (f + 1) * C1], slope[r // 2][:, r % 2, f * C1 : (f + 1) * C1], MULT)
             return woven
 
@@ -204,7 +204,7 @@ def tile_moe_hib_relu2_kernel(tc, dy_words, dy_scales, wet_words, wet_scales, wg
         z_whole(0, 2)
         for e, pair in ((2, 1), (3, 1), (3, 0)):
             first_product(e, (2 * pair, 2 * pair + 1), 2 * e + pair)
-        woven0 = times_slope(0)
+        woven0 = times_slope(0, (0, 1, 2, 3))
         back[2] = low.tile([P, T], F32, name="back_late2")
         z_whole(1, 2)
         accs0 = second_product(0, woven0)
@@ -214,7 +214,7 @@ def tile_moe_hib_relu2_kernel(tc, dy_words, dy_scales, wet_words, wet_scales, wg
         for e in (2, 3):
             for r in range(2):
                 z_half(e, r)
-        woven1 = times_slope(1)
+        woven1 = times_slope(1, (2, 0, 1, 3))
 
         tokens = [(high if kb % 2 else low).tile([P, T], F32, name=f"tokens{kb}", tag="back3" if kb == 2 else f"tokens{kb}", align_bytes=64) for kb in range(K // P)]
         dx_rows = [keep.tile([P, T], F32, name=f"dx{kb}") for kb in range(K // P)]
@@ -223,16 +223,18 @@ def tile_moe_hib_relu2_kernel(tc, dy_words, dy_scales, wet_words, wet_scales, wg
         def put(engine, f, kb, first, last):
             engine(tokens[kb], offs_sb, f * C1 + first, dx_rows[kb][:, f * C1 + first : f * C1 + last])
 
-        for kb in (0, 2):
-            nc.vector.tensor_copy(dx[0, kb], accs0[kb][:])
+        nc.vector.tensor_copy(dx[0, 0], accs0[0][:])
+        nc.vector.tensor_copy(dx[0, 2][:, 0:C2], accs0[2][:, 0:C2])
         for kb in (1, 3):
             nc.scalar.copy(dx[0, kb], accs0[kb][:])
         put(on_vector, 0, 0, 0, C1)
         accs1 = second_product(1, woven1)
+        for kb in (1, 3):
+            put(on_scalar, 0, kb, 0, C2)
+        nc.scalar.copy(dx[0, 2][:, C2:C1], accs0[2][:, C2:C1])
+        for kb in (1, 3):
+            put(on_scalar, 0, kb, C2, C1)
         put(on_vector, 0, 2, 0, C1)
-        for first in (0, C2):
-            for kb in (1, 3):
-                put(on_scalar, 0, kb, first, first + C2)
         for kb in (0, 2):
             nc.vector.tensor_copy(dx[1, kb], accs1[kb][:])
         nc.scalar.copy(dx[1, 1], accs1[1][:])

from contextlib import ExitStack

import concourse.mybir as mybir

K, T, G, C1, E, C2, H, N = 512, 1024, 2, 512, 4, 256, 512, 512
FLOPS = 2 * T * N * H + 2 * T * H * K

F32 = mybir.dt.float32
BF16 = mybir.dt.bfloat16
I32 = mybir.dt.int32
U32 = mybir.dt.uint32
U16 = mybir.dt.uint16
U8 = mybir.dt.uint8
FP8X4 = mybir.dt.float8_e4m3fn_x4
FP4X4 = mybir.dt.float4_e2m1fn_x4
COPY = mybir.ActivationFunctionType.Copy
MULT = mybir.AluOpType.mult
MAX = mybir.AluOpType.max

P = 128
PER_COL = 16
PLANES = 4


def tile_moe_hib_relu2_kernel(tc, dy_words, dy_scales, wet_words, wet_scales, wgt_words, wgt_scales, a, gate, offs, offs2, dst, out):
    nc = tc.nc
    with ExitStack() as ctx:
        lists = ctx.enter_context(tc.tile_pool(name="lists", bufs=1))
        reuse = ctx.enter_context(tc.tile_pool(name="reuse", bufs=1))
        low = ctx.enter_context(tc.tile_pool(name="low", bufs=1))
        keep = ctx.enter_context(tc.tile_pool(name="keep", bufs=1))
        high = ctx.enter_context(tc.tile_pool(name="high", bufs=1))
        psum = ctx.enter_context(tc.psum_pool(name="psum", bufs=1))

        def entries(tile, first, count):
            return tile[:, first // PER_COL : (first + count) // PER_COL]

        def load_scale_rows(plane, rows):
            for quad in range(4):
                nc.sync.dma_start(
                    plane[32 * quad : 32 * quad + 4, :, :].bitcast(I32),
                    rows[:, 4 * quad : 4 * quad + 4, :].rearrange("m b c -> b m c").bitcast(I32),
                )

        dst_sb = lists.tile([P, T // PER_COL], U16, name="dst_sb")
        offs2_sb = lists.tile([P, T // PER_COL], U16, name="offs2_sb")
        offs_sb = lists.tile([P, T // PER_COL], U16, name="offs_sb")

        dy_scale_sb = keep.tile([P, T], U8, name="dy_scale_sb", align_bytes=64)
        dy_word_sb = keep.tile([P, T], I32, name="dy_word_sb", align_bytes=64)
        first_scale_sb = keep.tile([P, 1, H], U8, name="first_scale_sb", align_bytes=64)
        rest_scale_sb = keep.tile([P, E - 1, H], U8, name="rest_scale_sb", tag="wet_scale", align_bytes=64)
        wgt_scale_sb = keep.tile([P, G, K], U8, name="wgt_scale_sb", align_bytes=64)
        nc.gpsimd.memset(rest_scale_sb[:].bitcast(I32), 0)
        nc.gpsimd.memset(wgt_scale_sb[:].bitcast(I32), 0)

        wet_view = wet_words.rearrange("e s p c -> p (e s) c")
        first_wet_sb = keep.tile([P, 1, 2 * H], U8, name="first_wet_sb", tag="first_wet", align_bytes=64)
        second_wet_sb = high.tile([P, 1, 2 * H], U8, name="second_wet_sb", tag="back0", align_bytes=64)
        rest_wet_sb = keep.tile([P, 2, 2 * H], U8, name="rest_wet_sb", align_bytes=64)
        gate_sb = [keep.tile([P, C1], F32, name=f"gate_sb{f}") for f in range(G)]
        a_view = a.rearrange("(q r) j -> q r j", r=PLANES)
        a_sb = [keep.tile([P, 2, T], F32, name="a_sb0"), reuse.tile([P, 2, T], F32, name="a_sb1", offset=0, align_bytes=64)]
        wgt_sb = keep.tile([P, G, 2 * K], U8, name="wgt_sb", align_bytes=64)

        nc.sync.dma_start(dst_sb[:], dst)
        for quad in range(4):
            rows = dy_scales[0, 4 * quad : 4 * quad + 4, :].bitcast(I32)
            (nc.sync if quad < 2 else nc.scalar).dma_start(dy_scale_sb[32 * quad : 32 * quad + 32, :].bitcast(I32), rows.unsqueeze(0).to_broadcast([8, 4, T // 4]))
        nc.sync.dma_start(dy_word_sb[:], dy_words[0].rearrange("p t d -> p (t d)").bitcast(I32))
        nc.sync.dma_start(first_wet_sb[:].bitcast(I32), wet_view[:, 0:1, :].bitcast(I32))
        for quad in range(4):
            rows = wet_scales[0, 0, 4 * quad : 4 * quad + 4, :].bitcast(I32)
            nc.sync.dma_start(first_scale_sb[32 * quad : 32 * quad + 32, 0, :].bitcast(I32), rows.unsqueeze(0).to_broadcast([8, 4, H // 4]))
        nc.sync.dma_start(gate_sb[0][:], gate[:, 0:C1])
        nc.sync.dma_start(second_wet_sb[:].bitcast(I32), wet_view[:, 1:2, :].bitcast(I32))
        nc.sync.dma_start(offs2_sb[:], offs2)
        load_scale_rows(rest_scale_sb, wet_scales.rearrange("e s b c -> (e s) b c")[1:E])
        nc.sync.dma_start(rest_wet_sb[:].bitcast(I32), wet_view[:, 2:E, :].bitcast(I32))
        for pair in range(2):
            nc.sync.dma_start(a_sb[pair][:], a_view[:, 2 * pair : 2 * pair + 2, :])
        nc.sync.dma_start(gate_sb[1][:], gate[:, C1:T])
        load_scale_rows(wgt_scale_sb, wgt_scales.rearrange("f s b c -> (f s) b c"))
        nc.sync.dma_start(wgt_sb[:].bitcast(I32), wgt_words.rearrange("f s p c -> p (f s) c").bitcast(I32))
        nc.sync.dma_start(offs_sb[:], offs)

        sorted_words, sorted_scales = {}, {}

        def sort_words(copy, experts, tag):
            count = experts.stop - experts.start
            words = keep.tile([P, count, PLANES, 2 * P], U8, name=f"sorted_words{experts.start}", tag=tag, align_bytes=64)
            natural = (first_wet_sb, second_wet_sb, rest_wet_sb)[experts.start][:]
            copy(words[:].bitcast(U16).rearrange("p e r (c i) -> p e c r i", i=8), natural.bitcast(U16).rearrange("p e (c i r) -> p e c r i", i=8, r=PLANES))
            for e in range(count):
                for r in range(PLANES):
                    sorted_words[experts.start + e, r] = words[:, e, r, :]

        def sort_scales(experts, planes):
            count = planes.stop - planes.start
            natural = rest_scale_sb[:, experts.start - 1 : experts.stop - 1, :] if experts.start else first_scale_sb[:]
            scales = keep.tile([P, experts.stop - experts.start, count, P], U8, name=f"sorted_scales{experts.start}_{planes.start}", tag=f"sorted_scales{experts.start}_{planes.start}", align_bytes=64)
            nc.gpsimd.tensor_copy(
                scales[:].rearrange("p e r (c i) -> p e c r i", i=16),
                natural.rearrange("p e (c i r) -> p e c r i", i=16, r=PLANES)[:, :, :, planes, :],
            )
            for e in range(experts.start, experts.stop):
                for r in range(count):
                    sorted_scales[e, planes.start + r] = scales[:, e - experts.start, r, :]

        sort_words(nc.scalar.copy, slice(0, 1), "sorted_words0")
        sort_words(nc.scalar.copy, slice(1, 2), "sorted_words1")
        sort_scales(slice(0, 1), slice(0, 1))
        sort_scales(slice(0, 1), slice(1, 4))
        sort_scales(slice(1, 2), slice(0, 4))
        sort_scales(slice(2, 4), slice(0, 4))

        z = {(f, pair): keep.tile([P, 2, C1], F32, name=f"z{f}_{pair}") for f in range(G) for pair in range(2)}

        def gather_scales(e, count, tag):
            scales = keep.tile([P, count, C2], U8, name=f"g_scale{e}", tag=tag, align_bytes=64)
            nc.vector.tensor_copy(scales[:].rearrange("p e c -> p (e c)"), dy_scale_sb[:].indirect(entries(dst_sb, e * C2, count * C2)))
            return [scales[:, at, :] for at in range(count)]

        def gather_words(e, count, tag):
            words = keep.tile([P, count, C2], U32, name=f"g_word{e}", tag=tag, align_bytes=64)
            nc.vector.tensor_copy(words[:].rearrange("p e c -> p (e c)"), dy_word_sb[:].bitcast(U32).indirect(entries(dst_sb, e * C2, count * C2)))
            return [words[:, at, :] for at in range(count)]

        def first_product(e, planes, bank):
            acc = psum.tile([P, len(planes), C2], F32, name=f"acc1_{e}_{planes[0]}", tag=f"bank{bank}")
            for at, r in enumerate(planes):
                nc.tensor.matmul_mx(
                    acc[:, at, :],
                    lhsT=sorted_words[e, r].bitcast(FP4X4),
                    lhsT_scale=sorted_scales[e, r],
                    rhs=g_word[e].bitcast(FP8X4),
                    rhs_scale=g_scale[e],
                    start=True,
                    stop=True,
                )
            cols = slice(e % 2 * C2, (e % 2 + 1) * C2)
            rows = slice(planes[0] % 2, planes[-1] % 2 + 1)
            nc.vector.tensor_tensor(z[e // 2, planes[0] // 2][:, rows, cols], acc[:], gate_sb[e // 2][:, cols].unsqueeze(1).to_broadcast([P, len(planes), C2]), MULT)

        def on_vector(window, offsets, first, values):
            nc.vector.tensor_copy(window[:].indirect(entries(offsets, first, values.shape[1])), values)

        def on_scalar(window, offsets, first, values):
            nc.scalar.activation(window[:].indirect(entries(offsets, first, values.shape[1])), values, COPY)

        back = [(low if r == 3 else high).tile([P, T], F32, name=f"back{r}", tag=f"back{r}", align_bytes=64) if r != 2 else reuse.tile([P, T], F32, name="back2", offset=0, align_bytes=64) for r in range(PLANES)]

        def z_half(e, r):
            on_scalar(back[r], offs2_sb, e * C2, z[e // 2, r // 2][:, r % 2, e % 2 * C2 : (e % 2 + 1) * C2])

        def z_whole(f, r):
            on_vector(back[r], offs2_sb, f * C1, z[f, r // 2][:, r % 2, :])

        def times_slope(f, order):
            woven = reuse.tile([P, C1, PLANES], BF16, name=f"woven{f}", offset=4 * T, align_bytes=64)
            for r in order:
                nc.gpsimd.tensor_tensor(woven[:, :, r], back[r][:, f * C1 : (f + 1) * C1], slope[r // 2][:, r % 2, f * C1 : (f + 1) * C1], MULT)
            return woven

        def second_product(f, woven):
            words = keep.tile([P, C1], U32, name=f"da_words{f}", align_bytes=64)
            scales = keep.tile([P, C1], U8, name=f"da_scales{f}", align_bytes=64)
            nc.vector.quantize_mx(words[:].bitcast(FP8X4), scales[:], woven[:].rearrange("p j r -> p (j r)"))
            accs = {}
            for kb in (1, 3, 0, 2):
                acc = psum.tile([P, C1], F32, name=f"acc2_{f}_{kb}", tag=f"bank{4 * f + kb}")
                nc.tensor.matmul_mx(
                    acc[:],
                    lhsT=wgt_sb[:, f, 2 * kb * P : 2 * (kb + 1) * P].bitcast(FP4X4),
                    lhsT_scale=wgt_scale_sb[:, f, kb * P : (kb + 1) * P],
                    rhs=words[:].bitcast(FP8X4),
                    rhs_scale=scales[:],
                    start=True,
                    stop=True,
                )
                accs[kb] = acc
            return accs

        def store(kb, window):
            (nc.scalar if kb % 2 else nc.sync).dma_start(out[kb * P : (kb + 1) * P, :], window[:])

        g_scale = gather_scales(0, 2, "g_scale0")
        g_word = gather_words(0, 1, "g_word0") + gather_words(1, 1, "g_word1")
        g_scale.extend(gather_scales(2, 1, "first_wet"))
        for planes, bank in (((0,), 7), ((1,), 0), ((2, 3), 1)):
            first_product(0, planes, bank)
        g_scale.extend(gather_scales(3, 1, "sorted_scales0_0"))
        g_word.extend(gather_words(2, 2, "g_word0"))
        for pair in range(2):
            first_product(1, (2 * pair, 2 * pair + 1), 2 + pair)
        sort_words(nc.vector.tensor_copy, slice(2, 4), "wet_scale")
        slope = [keep.tile([P, 2, T], F32, name=f"slope{pair}") for pair in range(2)]
        for pair in range(2):
            nc.vector.tensor_scalar(slope[pair][:], a_sb[pair][:], 2.0, 0.0, MULT, MAX)
        for e in range(2):
            for r in (0, 1, 3):
                z_half(e, r)
        first_product(2, (0, 1), 4)
        z_whole(0, 2)
        for e, pair in ((2, 1), (3, 1), (3, 0)):
            first_product(e, (2 * pair, 2 * pair + 1), 2 * e + pair)
        woven0 = times_slope(0, (0, 1, 2, 3))
        back[2] = low.tile([P, T], F32, name="back_late2")
        z_whole(1, 2)
        accs0 = second_product(0, woven0)
        z_whole(1, 3)
        for r in range(2):
            back[r] = high.tile([P, T], F32, name=f"back_late{r}")
        for e in (2, 3):
            for r in range(2):
                z_half(e, r)
        woven1 = times_slope(1, (2, 0, 1, 3))

        tokens = [(high if kb % 2 else low).tile([P, T], F32, name=f"tokens{kb}", tag="back3" if kb == 2 else f"tokens{kb}", align_bytes=64) for kb in range(K // P)]
        dx_rows = [keep.tile([P, T], F32, name=f"dx{kb}") for kb in range(K // P)]
        dx = {(f, kb): dx_rows[kb][:, f * C1 : (f + 1) * C1] for f in range(G) for kb in range(K // P)}

        def put(engine, f, kb, first, last):
            engine(tokens[kb], offs_sb, f * C1 + first, dx_rows[kb][:, f * C1 + first : f * C1 + last])

        nc.vector.tensor_copy(dx[0, 0], accs0[0][:])
        nc.vector.tensor_copy(dx[0, 2][:, 0:C2], accs0[2][:, 0:C2])
        for kb in (1, 3):
            nc.scalar.copy(dx[0, kb], accs0[kb][:])
        put(on_vector, 0, 0, 0, C1)
        accs1 = second_product(1, woven1)
        for kb in (1, 3):
            put(on_scalar, 0, kb, 0, C2)
        nc.scalar.copy(dx[0, 2][:, C2:C1], accs0[2][:, C2:C1])
        for kb in (1, 3):
            put(on_scalar, 0, kb, C2, C1)
        put(on_vector, 0, 2, 0, C1)
        for kb in (0, 2):
            nc.vector.tensor_copy(dx[1, kb], accs1[kb][:])
        nc.scalar.copy(dx[1, 1], accs1[1][:])
        nc.scalar.copy(dx[1, 3][:, 0:C2], accs1[3][:, 0:C2])
        for kb in (1, 3):
            put(on_scalar, 1, kb, 0, C2)
        put(on_vector, 1, 0, 0, C1)
        store(0, tokens[0])
        put(on_vector, 1, 2, 0, C1)
        store(2, tokens[2])
        put(on_scalar, 1, 1, C2, C1)
        nc.scalar.copy(dx[1, 3][:, C2:C1], accs1[3][:, C2:C1])
        store(1, tokens[1])
        put(on_scalar, 1, 3, C2, C1)
        store(3, tokens[3])
